import numpy as np, ml_dtypes
CORES = [6,15,38,47]
N = 4
BF = ml_dtypes.bfloat16
def gentries(a):
    return np.ascontiguousarray(a.reshape(8, 16, -1).transpose(0, 2, 1)).reshape(8, -1)
def gtable(e):
    e = np.asarray(e); return np.ascontiguousarray(e.reshape(8, -1, 16).transpose(0, 2, 1)).reshape(128, -1).astype(np.int32)
V, G, CAP, Q, C, CL, RO = 2560, 512, 64, (32, 32, 64, 128), 4, 3, 3
W = V + (N - 1) * G
def ghosted(xs):
    return np.stack([np.concatenate([xs[a]] + [xs[(a - d) % N][:, :, :G] for d in range(1, N)], axis=2) for a in range(N)])
def drawn(n, t, sd):
    r = []
    for c in range(C):
        if n[c] >= Q[c]:
            st = 4096 // Q[c]; b = (41 * t + 13 * n[0] + sd[c]) & (st - 1)
            r.append(V * c + (((np.arange(Q[c]) * st + b) * n[c]) >> 12))
    return np.concatenate(r)
def move(w, nb, s):
    m = np.add.reduce(w[:, nb[:, s]], axis=1) >> 4
    w[:, s] = w[:, s] + np.minimum(np.maximum(m - w[:, s], -CL), CL)
def hand(w, s):
    for a in range(N):
        for g in range(8):
            lo = np.sort(s[a][g]); lo = lo[lo < G][:CAP]
            for d in range(1, N): w[(a + d) % N, g][:, V + (d - 1) * G + lo] = w[a, g][:, lo]
def touched(nb, s):
    return np.unique(np.concatenate([s, nb[0, s]]))
def energy(w, nb, s):
    return np.sum(np.abs(w[:, nb[:, s]] - w[:, None, s]), axis=(0, 1))
def lay(n):
    return np.concatenate([V * c + np.arange(n[c]) for c in range(C)])
def force(rng, c, k):
    cuts = np.sort(rng.integers(0, V - k + 1, C - 2)); p = np.diff(np.concatenate([np.array([0]), cuts, np.array([V - k])]))
    return np.insert(p, c, k)
def parts(rng):
    amp = rng.choice(np.array([3, 12, 40, 127]), (N, 8, 1, V)); xs = 128 + rng.integers(-127, 128, (N, 8, 16, V)) * amp // 127
    nbr = rng.integers(0, W, (N, 8, 16, V)); nbr[:, :, 0] = np.argsort(rng.random((N, 8, V)), axis=2)
    z = np.zeros((N, 8, 1), np.int64); n = np.diff(np.concatenate([z, np.sort(rng.integers(0, V + 1, (N, 8, C - 1)), axis=2), z + V], axis=2), axis=2)
    o = np.argsort(rng.random((N, 8, V)), axis=2); sd = rng.integers(0, 4096, (N, 8, C))
    return xs, nbr, n, o, sd
def quant(rng, xs, nbr):
    w = ghosted(xs); th = np.zeros((N, 8, C - 1), np.int64)
    for a in range(N):
        for g in range(8): th[a, g] = np.sort(energy(w[a, g], nbr[a, g], rng.integers(0, V, 256)))[np.sort(rng.integers(16, 240, C - 1))]
    return th
def watched(rng, g, t, xs, nbr, n, o, th, sd):
    one = V * np.eye(C, dtype=np.int64)[C - 1]
    for a in range(0, N, 2):
        n[a, g] = V // C; n[a, g, C - 1] += V - C * (V // C)
        if t > 0: n[a, g] = one; th[a, g] = 0
        at = [np.searchsorted(lay(n[a, g]), drawn(n[a, g], u, sd[a, g])) for u in range(t + 1)]
        p = at[t]; early = np.concatenate([np.zeros(0, np.int64)] + at[:t]); m = np.ones(V, bool); m[p] = False; m[early] = False
        lo = rng.permutation(G); hi = G + rng.permutation(V - G); q = o[a, g]
        q[p] = lo[:len(p)]; q[early] = hi[:len(early)]; q[m] = rng.permutation(np.concatenate([lo[len(p):], hi[len(early):]]))
        xs[a, g] = 200; xs[a, g][:, :G] = 100; nbr[a, g, 0] = np.arange(V); nbr[a, g, 1:] = rng.integers(G, V, (15, V))
        z = np.sort(q[p]); still = rng.random(len(z)) < 0.5; still[CAP - 1:CAP + 1] = False
        nbr[a, g, 1:][:, z[still]] = z[still]
        b = a + 1; n[b, g] = one; xs[b, g] = 200; th[b, g] = 240 * (100 - CL)
        come = o[b, g][np.searchsorted(lay(one), drawn(one, t, sd[b, g]))]
        nbr[b, g, 0] = np.arange(V); nbr[b, g, 1:] = V + rng.choice(z, V)
        nbr[b, g, 1:][:, come] = V + rng.permutation(z[:len(come)])
def pack(xs, nbr, n, o, th, sd):
    pl = np.zeros((N, 8, V), np.int64)
    for a in range(N):
        for g in range(8): pl[a, g, o[a, g]] = lay(n[a, g])
    return {"x": np.ascontiguousarray(xs.reshape(N, 128, V)).astype(np.float32).astype(BF), "nb": np.ascontiguousarray(nbr.reshape(N, 128, V)).astype(np.int32),
            "plc": np.stack([gtable(p) for p in pl]), "th": th.astype(np.int32), "sd": sd.astype(np.int32)}
def setup_inputs(rng):
    xs, nbr, n, o, sd = parts(rng)
    for a in range(N): n[a, (3 * a + 2) % 8] = force(rng, a % C, int(rng.integers(0, Q[a % C])))
    return pack(xs, nbr, n, o, quant(rng, xs, nbr), sd)
def setup_inputs_room(rng):
    xs, nbr, n, o, sd = parts(rng)
    for a in range(N):
        for g in range(8):
            if a == 0:
                n[a, g] = V // C; n[a, g, C - 1] += V - C * (V // C); k = (CAP, CAP + 1, 2 * CAP, CAP - 1, 1, 0, CAP, CAP + 1)[g]
            else:
                c = (g + a) % C; n[a, g] = force(rng, c, (Q[c] - 1, Q[c], Q[c] + 1, 0)[(g + g // 4) % 4]); k = int(rng.choice(np.array([0, 1, CAP - 1, CAP, CAP + 1, 2 * CAP])))
            p = np.searchsorted(lay(n[a, g]), drawn(n[a, g], 0, sd[a, g])); k = min(k, len(p)); h = len(p) - k
            lo = rng.permutation(G); hi = G + rng.permutation(V - G); m = np.ones(V, bool); m[p] = False; q = o[a, g]
            q[p] = rng.permutation(np.concatenate([lo[:k], hi[:h]])); q[m] = rng.permutation(np.concatenate([lo[k:], hi[h:]]))
    return pack(xs, nbr, n, o, quant(rng, xs, nbr), sd)
def setup_inputs_ties(rng):
    xs, nbr, n, o, sd = parts(rng); xs[:, ::2] = 100 + rng.integers(0, 4, (N, 4, 16, V)); xs[:, 4] = 77
    for a in range(N):
        q = rng.permutation(V); lo = q[:V // 2]; hi = q[V // 2:]; xs[a, 6] = 0; xs[a, 6][:, hi] = 255
        nbr[a, 6, 0][lo] = hi; nbr[a, 6, 0][hi] = np.roll(lo, -1)
        nbr[a, 6, 1:][:, lo] = rng.choice(hi, (15, V // 2)); nbr[a, 6, 1:][:, hi] = rng.choice(lo, (15, V // 2))
    w = ghosted(xs); s = [[o[a, g][np.searchsorted(lay(n[a, g]), drawn(n[a, g], 0, sd[a, g]))] for g in range(8)] for a in range(N)]; th = np.zeros((N, 8, C - 1), np.int64)
    for a in range(N):
        for g in range(8): move(w[a, g], nbr[a, g], s[a][g])
    hand(w, s)
    for a in range(N):
        for g in range(8):
            e = energy(w[a, g], nbr[a, g], touched(nbr[a, g], s[a][g])); th[a, g] = e[rng.integers(0, len(e), C - 1)] + rng.integers(0, 2, C - 1)
    th[:, 1] = th[:, 1, :1]; th[::2, 6, 0] = 65280
    return pack(xs, nbr, n, o, th, sd)
def setup_inputs_flood(rng):
    xs, nbr, n, o, sd = parts(rng); th = quant(rng, xs, nbr); one = V * np.eye(C, dtype=np.int64)
    n[:, 0] = one[0]; th[:, 0] = 0; n[:, 1] = one[C - 1]; th[:, 1] = 65536; nbr[:, 2, 0] = np.arange(V); n[:, 5] = one[C - 1]; th[:, 5] = 0
    th[:, 4] = 0; th[:, 6] = 65536; th[:, 7] = 65536 * rng.integers(0, 2, (N, C - 1))
    for a in range(N):
        nbr[a, 3, 0][o[a, 3]] = np.roll(o[a, 3], -1); n[a, 4] = force(rng, 0, Q[0]); n[a, 6] = force(rng, C - 1, Q[C - 1])
    for a in range(0, N, 2):
        k = V // C; n[a, 5] = k; n[a, 5, C - 1] = V - (C - 1) * k; th[a, 5] = 32768; q = o[a, 5]
        for c in range(C):
            m = q[c * k:c * k + n[a, 5, c]]; nbr[a, 5, 0][m] = np.roll(m, -1)
        nbr[a, 5, 1:] = rng.choice(q[k:], (15, V)); xs[a, 5] = 0; xs[a, 5][:, q[:k]] = 255
    for a in range(1, N, 2):
        n[a, 1] = max(Q); k = (C - 1) * max(Q); n[a, 1, C - 1] = V - k; q = o[a, 1]
        p = np.searchsorted(lay(n[a, 1]), drawn(n[a, 1], 0, sd[a, 1])); m = np.ones(V, bool); m[p] = False
        early = k + np.flatnonzero(m[k:V - len(p) - Q[C - 1]]); early = rng.permutation(early)[:len(p)]; r = np.ones(V, bool); r[early] = False
        nbr[a, 1, 0][q[p]] = q[early]; nbr[a, 1, 0][q[m]] = rng.permutation(q[r])
    return pack(xs, nbr, n, o, th, sd)
def setup_inputs_alike(rng):
    xs, nbr, n, o, sd = parts(rng); xs[:, ::2] = 255 * rng.integers(0, 2, (N, 4, 16, V))
    nbr[:, 1, 1:] = rng.choice(np.array([0, V - 1, V, W - 1]), (N, 15, V)); nbr[:, 2, 1:] = nbr[:, 2, 1:2]
    nbr[:, 3, 1:] = rng.integers(V, W, (N, 15, V)); nbr[:, 5, 1:] = rng.integers(0, V, (N, 15, V)); nbr[:, 7] = np.arange(V)
    th = quant(rng, xs, nbr)
    watched(rng, 0, 0, xs, nbr, n, o, th, sd); watched(rng, 4, RO - 1, xs, nbr, n, o, th, sd)
    return pack(xs, nbr, n, o, th, sd)
def setup_inputs_spread(rng):
    xs, nbr, n, o, sd = parts(rng)
    xs = np.minimum((np.exp2(8 * rng.random((N, 8, 1, V))) * rng.random((N, 8, 16, V))).astype(np.int64), 255)
    nbr[:, :, 1:] = W - 1 - np.minimum((W * rng.random((N, 8, 15, V)) ** 3).astype(np.int64), W - 1)
    th = quant(rng, xs, nbr); th[:, 1::2] = np.minimum(np.exp2(16 * rng.random((N, 4, C - 1))).astype(np.int64), 65536)
    sd[:, ::3] = rng.choice(np.array([0, 1, 31, 4095]), sd[:, ::3].shape)
    return pack(xs, nbr, n, o, th, sd)
def check_inputs(d):
    bad = []
    v = np.asarray(d["x"]).astype(np.float32)
    if not np.all((v >= 0) & (v <= 255) & (v == np.floor(v))): bad.append("x: whole numbers from 0 to 255")
    for k, hi in (("nb", W - 1), ("plc", C * V - 1), ("th", 65536), ("sd", 4095)):
        if np.min(d[k]) < 0 or np.max(d[k]) > hi: bad.append("range of " + k)
    if np.any(np.sort(np.asarray(d["nb"]).reshape(N, 8, 16, V)[:, :, 0], axis=2) != np.arange(V)): bad.append("first neighbours: every own site once")
    k = np.sort(np.stack([gentries(a) for a in d["plc"]]).astype(np.int64), axis=2); c = k // V; p = np.arange(V)[None, None, :]
    for j in range(C): p = p - np.where(c > j, np.count_nonzero(c == j, axis=2)[:, :, None], 0)
    if np.any(k - V * c != p): bad.append("bags filled from position 0 on, each position once")
    return bad
def reference(x, nb, plc, th, sd):
    w = ghosted(x.astype(np.float32).astype(np.int64).reshape(N, 8, 16, V)); nbr = nb.astype(np.int64).reshape(N, 8, 16, V)
    pl = np.stack([gentries(a) for a in plc]).astype(np.int64)
    bag = np.zeros((N, 8, C * V), np.int64); np.put_along_axis(bag, pl, np.broadcast_to(np.arange(V), pl.shape), 2)
    n = np.stack([np.count_nonzero(pl // V == c, axis=2) for c in range(C)], axis=2).astype(np.int64)
    tv = th.astype(np.int64); sv = sd.astype(np.int64)
    for t in range(RO):
        s = [[bag[a, g][drawn(n[a, g], t, sv[a, g])] for g in range(8)] for a in range(N)]
        for a in range(N):
            for g in range(8): move(w[a, g], nbr[a, g], s[a][g])
        hand(w, s)
        for a in range(N):
            for g in range(8):
                k, h, z = bag[a, g], pl[a, g], n[a, g]
                u = touched(nbr[a, g], s[a][g]); e = energy(w[a, g], nbr[a, g], u)
                new = np.sum(e[None, :] >= tv[a, g][:, None], axis=0); old = h[u] // V
                go = new != old; u, new, old = u[go], new[go], old[go]
                for c in range(C):
                    out = u[old == c]; left = z[c] - len(out); p = h[out]; hole = p[p < V * c + left]
                    tail = k[V * c + left:V * c + z[c]]; stay = tail[~np.isin(tail, out)]
                    k[hole] = stay; h[stay] = hole; z[c] = left
                for c in range(C):
                    come = u[new == c]; p = V * c + z[c] + np.arange(len(come))
                    k[p] = come; h[come] = p; z[c] += len(come)
    return {"yx": np.ascontiguousarray(w[:, :, :, :V]).reshape(N, 128, V).astype(np.float32).astype(BF), "yp": pl.astype(np.float32)}

@@ -1,0 +1,676 @@
+from concourse.bass import DstId, RemoteDMATransfer
+from concourse.mybir import AluOpType, AxisListType, ActivationFunctionType
+
+AL, AF = AluOpType, ActivationFunctionType
+V_, SH, RO = 2560, 512, 3
+QS = (32, 32, 64, 128)
+DZ, BAGW, TW_ = 10240, 11792, 2064
+CHUNKS = ((80, "v"), (144, "s"), (128, "s"), (96, "s"), (64, "s"))
+
+F32 = dict(blk=256, rcol=16, E=16, BK=16, G9=16, col=48, JW=32, JH=16, C25=16, DZJ=16, SDE=16, Q4=16, C4=16,
+           TS=16, G4=16, N4=16, N4p=16, N4c=16, s13=16, jb=16, pc=16, inv=16, iv=16, mx=16, JT=256, c65=16, cD=32, c513=32,
+           TRJ=32, TRB=32, J544=32, J512=32, t16=16, t32=32, t32b=32, DD=128, DDn=128, pos=32, dl=128, q=128,
+           Z9=288, Z9o=288, R9=288, Z5=160, Z5o=160, R5=160, Z4=128, Z4o=128, R4=128, K4=16, KJ=16, KJa=16, n25=32, tp=32,
+           ta=32, tb=32, tc=32, td=32, te=32, m4=32, tf=32, tg=32, th=32, nA=16, plf=160, c1=160, c2=160, SLf=512, JVf=512, PUf=512,
+           one=128, msg=3 * 80, land=9 * 80)
+BF = dict(Z=16 * 144, Ys=144, Yj=144, Yr=144, Yk=144, Yc=144, Yp=144, Yb=144, Ym=144, Yt=144, BO=128, BO2=128, BOm=128, BOm16=128,
+          NUP=128, ID=128, ID16=128, IDm=128, IDb=128, IDmb=128, TR1=128, TR1b=128, TR2=128, TR3=128, C75=64, C512=128, ONE=512,
+          VD=256, VN=256, UF=512, XM=256, DL=256, ND=256, RS=256, RK=512, XU=512, PU=512, B=512, PEN=32, OH=128, NE=128, LV=128,
+          JN=128, HF=128, SLV=144, SHF=128, SJ=144, CU=512, TG=512, TSb=512, JV=512, ge=480, fl=5 * 160, nh=160, nl=160, th=16, tl=16,
+          blk=256, SEL=3 * 336, SL=3 * 1024, CS=1040)
+U16 = dict(plu=160, DP=16, U0=32, DWc=16, NBD=256, SW=16, JWu=16, RW=32, UW=32, NBU=512, GO=16, SLOT=32, TP=32, IDX=32, BOW=32,
+           PLO=32, BJ=32, PN=32)
+I32 = dict(plc=160, pi=16, ts=16, tsh=16, tsl=16, xi=16, bi=16, pr=16, sh=16, a=160, b=160, c=160, d=160, e=160, n0=160)
+
+
+def _arena(d):
+    o, at = 0, {}
+    for k, n in d.items():
+        at[k] = o
+        o += (n + 15) // 16 * 16
+    return at, o
+
+
+AT = {}
+SCRATCH = {}
+for _n, _d, _t in (("af", F32, "float32"), ("ab", BF, "bfloat16"), ("au", U16, "uint16"), ("ai", I32, "int32")):
+    AT[_n], _w = _arena(_d)
+    SCRATCH[_n] = ("sbuf", [128, _w], _t)
+SCRATCH.update({
+    "bag": ("sbuf", [128, BAGW], "float32"), "pl": ("sbuf", [128, 3072], "float32"), "ypb": ("sbuf", [128, V_], "float32"),
+    "nbt": ("sbuf", [128, 3072], "int32"), "xw": ("sbuf", [128, 5696], "bfloat16"), "sf": ("sbuf", [128, 3072], "bfloat16"),
+    "nf": ("sbuf", [128, 3072], "bfloat16"), "ff": ("sbuf", [128, 3072], "bfloat16"), "ct": ("sbuf", [128, 3072], "bfloat16"),
+    "d0": ("sbuf", [128, 1280], "bfloat16"), "gg": ("sbuf", [128, 8192], "bfloat16"), "mm": ("sbuf", [128, 4608], "bfloat16"),
+    "tt": ("sbuf", [128, TW_], "float32"),
+})
+for _k in range(8):
+    SCRATCH["p%d" % _k] = ("psum", [128, 512], "float32")
+NDMA = 22
+SEMAPHORES = ["qv", "qs", "qp", "qg", "gin", "sent", "sent0"] + ["arr%d" % k for k in range(3)] + ["dm%d" % k for k in range(NDMA)]
+
+
+def rank_program(g, core, T, topo):
+    rank = T.rank_of(core)
+    if rank is None:
+        return
+    N = len(T.cores)
+    ops = []
+
+    def R(buf, a, b, st=1, p0=0, ps=1):
+        return (buf, a, b, st, p0, ps)
+
+    def arena(name, tab):
+        def get(k, a=0, b=None, st=1):
+            o = AT[name][k]
+            return (name, o + a, o + (tab[k] if b is None else b), st, 0, 1)
+        return get
+    f, b_, u, i_ = arena("af", F32), arena("ab", BF), arena("au", U16), arena("ai", I32)
+
+    def P(k, a, b, st=1):
+        return ("p%d" % k, a, b, st, 0, 1)
+
+    def ind(win, off):
+        return ("ind", win, off)
+
+    def ap(x):
+        if not isinstance(x, tuple):
+            return x
+        if x[0] == "ind":
+            return ap(x[1]).indirect(ap(x[2]))
+        t = T[x[0]]
+        cs = slice(x[1], x[2]) if x[3] == 1 else slice(x[1], x[2], x[3])
+        return t[:, cs] if x[5] == 1 else t[x[4]:128:x[5], cs]
+
+    def add(eng, fn, out, ins, dma=False):
+        rd, wr = [], []
+        for x in ins:
+            if isinstance(x, tuple):
+                rd += [x[1], x[2]] if x[0] == "ind" else [x]
+        if isinstance(out, tuple):
+            if out[0] == "ind":
+                wr.append(out[1]); rd.append(out[2])
+            else:
+                wr.append(out)
+        ops.append(dict(e=eng, fn=fn, rd=rd, wr=wr, dma=dma, ext=None, scat=isinstance(out, tuple) and out[0] == "ind"))
+
+    def ext(sem, val, region):
+        ops.append(dict(e="x", fn=None, rd=[], wr=[region], dma=False, ext=(sem, val), scat=True))
+
+    def cp(o, x):
+        add("v", lambda: g.vector.tensor_copy(ap(o), ap(x)), o, [x])
+
+    def tt(o, x, y, op):
+        add("v", lambda: g.vector.tensor_tensor(ap(o), ap(x), ap(y), op), o, [x, y])
+
+    def ts(o, x, s1, op0, s2=None, op1=None):
+        if op1 is None:
+            add("v", lambda: g.vector.tensor_scalar(ap(o), ap(x), ap(s1), None, op0), o, [x, s1])
+        else:
+            add("v", lambda: g.vector.tensor_scalar(ap(o), ap(x), ap(s1), ap(s2), op0, op1), o, [x, s1, s2])
+
+    def scan(o, d0, d1, init, op0, op1):
+        add("v", lambda: g.vector.tensor_tensor_scan(ap(o), ap(d0), ap(d1), ap(init), op0, op1), o, [d0, d1, init])
+
+    def mset(o, c):
+        add("v", lambda: g.vector.memset(ap(o), c), o, [])
+
+    def red(o, x):
+        add("v", lambda: g.vector.tensor_reduce(ap(o), ap(x), AxisListType.X, AL.add), o, [x])
+
+    def act(o, x, fn=AF.Identity, bias=None, scale=None):
+        kw = {}
+        if bias is not None:
+            kw["bias"] = bias
+        if scale is not None:
+            kw["scale"] = scale
+        add("s", lambda: g.scalar.activation(ap(o), ap(x), fn, **{k: ap(v) for k, v in kw.items()}), o, [x, bias, scale])
+
+    def mm(o, l, r, st, sp):
+        add("p", lambda: g.tensor.matmul(ap(o), ap(l), ap(r), st, sp), o, [l, r])
+
+    def iota(o, pat, base=0, cm=0):
+        if o[0] in ("ai", "nbt"):
+            add("g", lambda: g.iota(ap(o), pat, base, cm), o, [])
+        else:
+            add("g", lambda: g.iota(ap(o), pat, base, cm, allow_small_or_imprecise_dtypes=True), o, [])
+
+    def asel(o, x, pat, op, base, cm):
+        add("g", lambda: g.affine_select(ap(o), ap(x), pat, op, 0.0, base, cm), o, [x])
+
+    def dma(o, x):
+        add("y", lambda: g.sync.dma_start(ap(o), ap(x)), o, [x], dma=True)
+
+    def sub(x, a, b, st=1):
+        return (x[0], x[1] + a, x[1] + b, st, x[4], x[5])
+
+    def conv(o, src, Y, n, extra=None):
+        if extra is not None:
+            mm(o, extra[0], extra[1], True, False)
+        for r in range(16):
+            mm(o, b_(Y, 16 - r, 144 - r), sub(src, r, n, 16), r == 0 and extra is None, r == 15)
+
+    def send(src, dst_of, sem, loc):
+        peers = [T.cores[(rank + d) % N] for d in range(1, N)]
+        m = topo.mask(core, peers[0])
+        for c in peers[1:]:
+            m &= topo.mask(core, c)
+        ids = [DstId(rid=topo.addr(c)[0], pnc=topo.addr(c)[1]) for c in peers]
+        add("g", lambda: g.remote_dma_fused([RemoteDMATransfer(dst_ids=ids, dma_engine_mask=m, remote_sem=T.sem[sem], srcs=[ap(src)],
+                                                               dsts=[ap(dst_of(d)) for d in range(1, N)])], local_sem=T.sem[loc]), None, [src])
+        ops[-1]["remote"] = True
+        return bin(m).count("1")
+
+    ncol = [0]
+
+    def column(terms, const=0.0):
+        if len(terms) == 1 and terms[0][1] == 1 and const == 0.0:
+            return f("E", terms[0][0], terms[0][0] + 1)
+        o = f("col", ncol[0], ncol[0] + 1); ncol[0] += 1
+        prev = const
+        for r, w in terms:
+            ts(o, f("E", r, r + 1), float(w), AL.mult, prev, AL.add)
+            prev = o
+        return o
+
+    def ymat(name, terms):
+        ts(b_(name, 0, 144, 16), f("G9", 0, 9), column(terms), AL.mult)
+
+    def trmat(name, outs):
+        for p, terms in outs.items():
+            ts(b_(name, p, 128, 16), f("G9", 1, 9), column(terms), AL.mult)
+
+    XO = R("xw", SH, SH + V_)
+    XS, XN = R("xw", 0, 3072), R("xw", SH, SH + 4096)
+    NBT, SF, NF, PL = R("nbt", 0, 3072), R("sf", 0, 3072), R("nf", 0, 3072), R("pl", 0, 3072)
+    BG, BS = R("bag", 0, DZ + 512), R("bag", 0, BAGW)
+    F, TT = R("ff", 0, 3072), R("tt", 0, TW_)
+    HI, LO = f("JVf", 0, 256), f("JVf", 256, 512)
+    cr = ((0, 2), (2, 4), (4, 8), (8, 16))
+    K = {}
+
+    mset(f("one"), 1.0)
+    mset(i_("ts"), 0)
+    dma(i_("plc"), T.plc[:])
+    dma(R("xw", SH, SH + 512), T.x[:, 0:512])
+    dma(R("ai", AT["ai"]["ts"], AT["ai"]["ts"] + 3, 1, 0, 16), T.th[:])
+    dma(R("ai", AT["ai"]["ts"] + 4, AT["ai"]["ts"] + 8, 1, 0, 16), T.sd[:])
+    dma(i_("n0"), T.nb[0:128:16, :])
+    dma(R("nbt", SH, SH + V_), T.nb[:])
+    dma(R("xw", SH + 512, SH + V_), T.x[:, 512:V_])
+    act(b_("C512"), f("one"), AF.Silu, scale=512.0)
+    iota(i_("pi", 0, 1), [[0, 1]], 0, 1)
+    iota(LO, [[0, 16], [1, 16]])
+    iota(HI, [[1, 16], [0, 16]])
+    mset(R("ab", AT["ab"]["Ys"], AT["ab"]["Yc"]), 0.0)
+    ts(i_("pi", 1, 2), i_("pi", 0, 1), 15, AL.bitwise_and)
+    cp(f("rcol", 0, 1), i_("pi", 1, 2))
+    ts(f("E"), sub(LO, 0, 16), f("rcol", 0, 1), AL.is_equal)
+    ts(f("BK", 0, 12), sub(LO, 0, 12), f("E", 0, 1), AL.mult, 16.0, AL.mult)
+    ts(f("blk"), LO, 32.0, AL.add, f("E", 1, 2), AL.mult)
+    ts(HI, HI, 32.0, AL.add, f("E", 0, 1), AL.mult)
+    tt(f("blk"), f("blk"), HI, AL.add)
+    for k in range(2, 7):
+        act(R("ypb", (k - 2) * 256, (k - 1) * 256), f("blk"), bias=f("BK", k, k + 1))
+    for k in range(7, 12):
+        ts(R("ypb", (k - 2) * 256, (k - 1) * 256), f("blk"), f("BK", k, k + 1), AL.add)
+    cp(u("plu"), i_("plc"))
+    act(ind(R("bag", 0, DZ), u("plu")), R("ypb", 0, V_), AF.Silu)
+    asel(f("G9", 0, 9), f("one", 0, 9), [[-16, 9]], AL.is_ge, 16, 1)
+    asel(f("G9", 0, 9), f("G9", 0, 9), [[16, 9]], AL.is_ge, -1, -1)
+    asel(b_("BO"), f("one"), [[-16, 8], [0, 16]], AL.is_ge, 0, 1)
+    asel(b_("BO"), b_("BO"), [[16, 8], [0, 16]], AL.is_ge, 15, -1)
+    iota(f("JW"), [[16, 32]])
+    ne = send(R("xw", SH, SH + 512), lambda d: R("xw", 3072 + (d - 1) * 512, 3072 + d * 512), "gin", "sent0")
+    ext("gin", ne * (N - 1), R("xw", 3072, 4608))
+    iota(f("C4", 0, 4), [[V_, 4]])
+    for c, (a, e) in enumerate(cr):
+        iota(f("C25", a, e), [[0, e - a]], V_ * c)
+    iota(f("JT"), [[1, 256]])
+    asel(b_("ID"), f("one"), [[-1, 128]], AL.is_equal, 0, 1)
+    iota(b_("ONE"), [[0, 512]], 1)
+    iota(R("nbt", 0, SH), [[0, SH]])
+    iota(R("xw", 0, SH), [[0, SH]])
+    iota(R("ff", SH, 3072), [[0, V_]])
+    iota(b_("CS"), [[0, 1040]], 65)
+    iota(R("ab", AT["ab"]["Yc"], AT["ab"]["BO"]), [[0, 720]])
+    iota(R("ab", AT["ab"]["TR1"], AT["ab"]["C75"]), [[0, 512]])
+    iota(R("pl", 0, SH), [[0, SH]])
+    iota(f("R9"), [[0, 32], [1, 9]]); iota(f("R5"), [[0, 32], [1, 5]]); iota(f("R4"), [[0, 32], [1, 4]])
+    iota(b_("SLV", 0, 16), [[0, 16]]); iota(b_("SJ", 0, 16), [[0, 16]])
+    cp(b_("blk"), f("blk"))
+    for k in range(12):
+        ts(R("sf", k * 256, (k + 1) * 256), b_("blk"), f("BK", k, k + 1), AL.add)
+    dma(NF, SF)
+    ts(i_("tsh"), i_("ts"), 0x1FF00, AL.bitwise_and)
+    ts(i_("tsl"), i_("ts"), 255, AL.bitwise_and)
+    cp(f("plf"), i_("plc"))
+    cp(b_("th"), i_("tsh")); cp(b_("tl"), i_("tsl"))
+    mm(P(4, 0, 16), b_("BO"), b_("th"), True, False); mm(P(4, 0, 16), b_("BO"), b_("tl"), False, True)
+    for c in range(1, 4):
+        ts(b_("ge", (c - 1) * 160, c * 160), f("plf"), float(V_ * c), AL.is_ge)
+    mm(P(5, 0, 480), b_("BO"), b_("ge"), True, True)
+    ts(i_("a"), i_("n0"), float(SH), AL.add)
+    mset(b_("Z"), 0.0)
+    ts(i_("b"), i_("a"), 4, AL.arith_shift_right)
+    ts(i_("c"), i_("a"), 15, AL.bitwise_and)
+    ts(b_("nh"), i_("b"), 32.0, AL.add); ts(b_("nl"), i_("c"), 32.0, AL.add)
+    dma(R("nf", SH, 3072, 1, 0, 16), b_("nh")); dma(R("nf", SH, 3072, 1, 1, 16), b_("nl"))
+    for t in range(RO):
+        dma(b_("SEL", t * 336, t * 336 + 64), R("sf", 2048, 2112))
+        dma(b_("SL", t * 1024, t * 1024 + 512), R("sf", 0, 512))
+    tt(f("c1"), b_("ge", 0, 160), b_("ge", 160, 320), AL.add)
+    ts(i_("d"), i_("plc"), 0x3FC0, AL.bitwise_and); ts(i_("e"), i_("plc"), 63, AL.bitwise_and)
+    tt(f("c1"), f("c1"), b_("ge", 320, 480), AL.add)
+    cp(b_("fl", 480, 640), i_("d")); cp(b_("fl", 640, 800), i_("e"))
+    ts(f("c2"), f("c1"), float(-V_), AL.mult)
+    ts(b_("fl", 0, 160), f("c1"), 32.0, AL.mult)
+    tt(i_("a"), f("c2"), f("plf"), AL.add)
+    for r in range(16):
+        ts(b_("Z", r * 144, (r + 1) * 144, 16), f("G9", 0, 9), f("E", r, r + 1), AL.mult)
+    ts(i_("b"), i_("a"), 4, AL.arith_shift_right); ts(i_("c"), i_("a"), 15, AL.bitwise_and)
+    cp(b_("fl", 160, 320), i_("b")); cp(b_("fl", 320, 480), i_("c"))
+    c32 = column([(0, 32), (2, 32), (3, 32)])
+
+    def piece(r):
+        return P((0, 2, 3, 6, 7)[r // 3], (r % 3) * 160, (r % 3 + 1) * 160) if r < 15 else P(1, 256, 416)
+
+    def spread(r0, r1):
+        for r in range(r0, r1):
+            for k, row in enumerate((1, 2, 3, 0, 0)):
+                mm(piece(r), b_("Z", r * 144 + 16 - row, r * 144 + 144 - row), b_("fl", k * 160, (k + 1) * 160), k == 0, k == 4)
+
+    def fetch(r0, r1):
+        for r in range(r0, r1):
+            act(R("pl", SH + r, 3072, 16), piece(r), bias=c32)
+    spread(0, 9)
+    fetch(0, 9)
+    ts(f("JW"), f("JW"), f("rcol", 0, 1), AL.add)
+    cp(f("TS"), P(4, 0, 16))
+    mset(f("G4", 0, 1), float(V_)); mset(f("G4", 4, 5), 0.0)
+    for c in range(1, 4):
+        red(f("G4", c, c + 1), P(5, (c - 1) * 160, c * 160))
+    mset(f("Q4", 0, 2), float(QS[0])); mset(f("Q4", 2, 3), float(QS[2])); mset(f("Q4", 3, 4), float(QS[3]))
+    tt(f("N4", 0, 4), f("G4", 0, 4), f("G4", 1, 5), AL.subtract)
+    for c, (a, e) in enumerate(cr):
+        ts(f("JH", a, e), f("JW", a, e), float(16 * a), AL.subtract, float(4096 // QS[c]), AL.mult)
+        ts(f("SDE", a, e), f("one", a, e), f("TS", 4 + c, 5 + c), AL.mult)
+    ts(f("DZJ"), f("JW", 0, 16), float(DZ), AL.add)
+
+    def draw_places(t):
+        ts(f("s13", 0, 1), f("N4", 0, 1), 13.0, AL.mult, float(41 * t), AL.add)
+        tt(f("inv", 0, 4), f("N4", 0, 4), f("Q4", 0, 4), AL.is_lt)
+        ts(i_("xi"), f("SDE"), f("s13", 0, 1), AL.add)
+        for c, (a, e) in enumerate(cr):
+            ts(f("iv", a, e), f("DZJ", a, e), f("inv", c, c + 1), AL.mult)
+        for a, e, m in ((0, 4, 127), (4, 8, 63), (8, 16, 31)):
+            ts(i_("bi", a, e), i_("xi", a, e), m, AL.bitwise_and)
+        tt(f("jb"), i_("bi"), f("JH"), AL.add)
+        for c, (a, e) in enumerate(cr):
+            ts(i_("pr", a, e), f("jb", a, e), f("N4", c, c + 1), AL.mult)
+        ts(i_("sh"), i_("pr"), 12, AL.arith_shift_right)
+        tt(f("pc"), i_("sh"), f("C25"), AL.add)
+        tt(f("mx"), f("pc"), f("iv"), AL.max)
+        cp(u("DP"), f("mx"))
+
+    draw_places(0)
+    cp(R("bag", DZ, DZ + 512), R("sf", 0, 512))
+    ts(f("JT"), f("JT"), f("E", 4, 5), AL.mult)
+    ymat("Ys", [(0, 16), (1, 1)])
+
+    def tables_move():
+        ts(b_("ID16"), b_("ID"), 0.0625, AL.mult); ts(b_("IDm"), b_("ID"), -1.0, AL.mult)
+        mset(b_("C75"), -7.5)
+        ts(b_("VN"), b_("ONE", 0, 256), f("E", 2, 3), AL.mult)
+        ts(b_("VD"), b_("ONE", 0, 256), column([(0, 1), (1, 1), (3, 1)]), AL.mult)
+
+    def tables_sort():
+        ymat("Yj", [(4, 1)]); ymat("Yr", [(0, 1), (1, 1000)])
+        K["k64"] = column([(1, 64)])
+        ts(f("c65"), f("JW", 0, 16), 65.0, AL.add)
+        keep = column([(3, -1), (8, -1)], 1.0)
+        for k in range(5):
+            act(R("d0", k * 256, (k + 1) * 256), b_("ONE", 0, 256), scale=keep)
+
+    def tables_sort2():
+        ts(R("ct", 0, SH), b_("ONE"), f("E", 3, 4), AL.mult, 2.0, AL.mult)
+        ymat("Yk", [(0, 1), (2, 1), (3, 2048)])
+        mset(f("cD", 0, 16), -2048.0); mset(f("cD", 16, 32), 0.0)
+        ts(f("c513"), f("JW"), 513.0, AL.add)
+
+    def tables_bags():
+        for nme, w in (("BOm", -1.0), ("BO2", 2.0), ("BOm16", -16.0)):
+            act(b_(nme), b_("BO"), scale=w)
+        asel(b_("NUP"), b_("BOm"), [[-1, 128]], AL.is_gt, 0, 1)
+        act(b_("IDb"), b_("ID"), scale=16384.0); act(b_("IDmb"), b_("ID"), scale=-16384.0)
+        act(f("TRJ"), f("JW"), bias=1552.0); act(f("TRB"), f("JW"), bias=float(DZ + 513))
+        act(f("J544"), f("JW"), bias=544.0); act(f("J512"), f("JW"), bias=512.0)
+        K["pus"] = column([(1, 1), (2, 1), (3, 1)]); K["m32"] = column([(8, 32)])
+        ymat("Yc", [(1, 1.0 / 32)]); ymat("Yp", [(2, 16), (3, 1)])
+        K["thc"] = column([(4, -1e9), (5, -1e9), (6, -1e9)], 1e9)
+        for k in range(3):
+            ts(K["thc"], f("E", 4 + k, 5 + k), f("TS", k, k + 1), AL.mult, K["thc"], AL.add)
+
+    def tables_bags2():
+        trmat("TR3", {2: [(0, 1)], 3: [(1, 1)]})
+        K["c128"] = column([(1, 128)]); K["m512"] = column([(0, -512)]); K["s01"] = column([(0, 1), (1, 1)])
+        ymat("Yb", [(4, 1), (5, 1), (6, 1)]); ymat("Ym", [(6, 1), (7, 1), (8, 64)]); ymat("Yt", [(1, 80), (2, 16), (3, 1)])
+        trmat("TR1", {0: [(0, 16), (1, 1)], 2: [(0, 1)], 3: [(1, 1)]})
+        trmat("TR1b", {0: [(4, V_), (5, V_), (6, V_)], 1: [(4, 32), (5, 32), (6, 32)]})
+        trmat("TR2", {0: [(1, 80), (2, 16), (3, 1)], 1: [(1, 1)], 2: [(2, 1)], 3: [(3, 1)]})
+        for nme in ("R9", "R5", "R4"):
+            ts(f(nme), f(nme), 1.0, AL.min)
+
+    def holes_table():
+        act(R("tt", 0, 256), b_("ONE", 0, 256), scale=f("E", 6, 7)); act(R("tt", 256, 512), b_("ONE", 0, 256), scale=f("E", 7, 8))
+        for k, a in ((3, 512), (7, 1024)):
+            mm(P(k, 0, 512), b_("TR3"), R("sf", a, a + 512), True, True)
+            act(R("tt", a, a + 512), P(k, 0, 512), bias=K["c128"])
+
+    def touched_update():
+        mm(P(1, 0, 512), b_("TR1b"), b_("B"), True, False)
+        mm(P(1, 0, 512), b_("TR1"), b_("JV"), False, True)
+        act(f("JVf"), P(1, 0, 512), bias=K["m512"])
+        act(ind(PL, u("UW")), f("JVf"), AF.Silu)
+
+    tables_sort()
+    for t in range(RO):
+        last = t == RO - 1
+        SEL, SL = b_("SEL", t * 336, (t + 1) * 336), b_("SL", t * 1024, (t + 1) * 1024)
+        DW, N0W, DF, N0F = u("U0", 0, 16), u("U0", 16, 32), b_("UF", 0, 256), b_("UF", 256, 512)
+        msg = f("msg", t * 80, t * 80 + 68)
+        tt(DF, ind(BG, u("DP")), f("JT"), AL.add)
+        conv(P(4, 0, 16), DF, "Ys", 256)
+        if t == 0:
+            tables_move()
+        ts(DW, P(4, 0, 16), -544.0, AL.add)
+        cp(u("NBD"), ind(NBT, DW))
+        cp(N0F, ind(NF, DW))
+        conv(P(5, 0, 16), N0F, "Ys", 256)
+        if t == 0:
+            spread(9, 16)
+        ts(u("DWc"), P(4, 0, 16), -544.0, AL.add, 1024.0, AL.min)
+        ts(b_("XM"), ind(XS, DW), -192.0, AL.add)
+        for k in range(4):
+            act(R("gg", k * 1024, (k + 1) * 1024), ind(XN, u("NBD", k * 64, (k + 1) * 64)))
+
+        def move_sum(k):
+            o = P(1, k * 64, (k + 1) * 64)
+            mm(o, b_("IDm"), b_("XM", k * 64, (k + 1) * 64), True, False)
+            mm(o, b_("ID16"), b_("C75"), False, False)
+            for j in range(16):
+                mm(o, b_("ID16"), R("gg", k * 1024 + j, (k + 1) * 1024, 16), False, j == 15)
+        ts(N0W, P(5, 0, 16), -544.0, AL.add)
+        cp(ind(F, N0W), b_("VN"))
+        cp(ind(F, DW), b_("VD"))
+        move_sum(0)
+        scan(b_("CS", 512, 1024), sub(F, 512, 1024), b_("CS", 0, 512), 0.0, AL.add, AL.min)
+        ts(b_("RS"), ind(b_("CS"), u("DWc")), K["k64"], AL.subtract, 0.0, AL.max)
+        move_sum(1)
+        conv(P(4, 0, 16), b_("RS"), "Yr", 256)
+        scan(R("ct", SH, SH + 1280), R("d0", 0, 1280), sub(F, SH, SH + 1280), 0.0, AL.mult, AL.add)
+        tt(f("t16"), P(4, 0, 16), f("c65"), AL.min)
+        ts(u("SW"), f("t16"), -1.0, AL.add)
+        cp(ind(SEL, u("SW")), DF)
+        move_sum(2)
+        conv(P(5, 0, 4), sub(SEL, 0, 64), "Yj", 64)
+        conv(P(5, 4, 8), sub(SEL, 0, 64), "Ys", 64)
+        move_sum(3)
+        scan(R("ct", SH + 1280, 3072), R("d0", 0, 1280), sub(F, SH + 1280, 3072), R("ct", SH + 1279, SH + 1280), AL.mult, AL.add)
+        if t == 0:
+            tables_sort2()
+        cp(u("JWu", 0, 4), P(5, 0, 4))
+        ts(sub(msg, 64, 68), P(5, 4, 8), -544.0 - SH, AL.add)
+        act(b_("RK"), ind(R("ct", 0, 3072), u("U0")))
+        ts(b_("DL"), P(1, 0, 256), 189.0, AL.max, 195.0, AL.min)
+        tt(b_("ND"), b_("DL"), b_("XM"), AL.add)
+        cp(sub(msg, 0, 64), ind(b_("ND"), u("JWu", 0, 4)))
+        ne = send(msg, lambda d, t=t: f("land", (3 * t + d - 1) * 80, (3 * t + d - 1) * 80 + 68), "arr%d" % t, "sent")
+        conv(P(4, 0, 32), b_("RK"), "Yk", 512)
+        if t > 0:
+            mm(P(2, 0, 512), b_("TR2"), b_("TG"), True, True)
+            act(f("JVf"), P(2, 0, 512), bias=K["m512"])
+            act(ind(PL, u("PLO")), f("JVf"), AF.Silu)
+        else:
+            fetch(9, 16)
+            ext("sent0", ne, R("xw", SH, SH + 512))
+        tt(f("t32"), P(4, 0, 32), f("cD"), AL.add)
+        tt(f("t32b"), f("t32"), f("c513"), AL.min)
+        ts(u("RW"), f("t32b"), -1.0, AL.add)
+        cp(ind(SL, u("RW")), b_("UF"))
+        conv(P(5, 0, 32), sub(SL, 0, 512), "Ys", 512)
+        cp(ind(XS, DW), b_("ND"))
+        if last:
+            dma(T.yx[:], XO)
+        if t == 0:
+            tables_bags()
+        if not last:
+            iota(R("ff", SH, 3072), [[0, V_]])
+        ts(u("UW"), P(5, 0, 32), -544.0, AL.add)
+        ts(b_("PEN"), P(5, 0, 32), 544.0 + SH, AL.is_lt, 8.0, AL.mult)
+        cp(u("NBU"), ind(NBT, u("UW")))
+        act(b_("XU"), ind(XS, u("UW")))
+        mm(P(0, 0, 512), b_("ID"), b_("XU"), True, True)
+        act(f("PUf"), ind(PL, u("UW")), bias=K["m32"], scale=K["pus"])
+        act(b_("PU"), f("PUf"))
+        conv(P(6, 0, 32), b_("PU"), "Yc", 512, (b_("ID"), b_("PEN")))
+        conv(P(6, 32, 64), b_("PU"), "Yp", 512)
+        if t == 0:
+            tables_bags2()
+        ext("arr%d" % t, ne * (N - 1), f("land", 3 * t * 80, 3 * (t + 1) * 80))
+        for d in range(1, N):
+            o = (3 * t + d - 1) * 80
+            cp(u("GO", 4 * (d - 1), 4 * d), f("land", o + 64, o + 68))
+        for d in range(1, N):
+            o = (3 * t + d - 1) * 80
+            cp(ind(R("xw", 3072 + (d - 1) * 512, 3072 + (d - 1) * 512 + 1600), u("GO", 4 * (d - 1), 4 * d)), f("land", o, o + 64))
+        at = 0
+        for n, e in CHUNKS:
+            o, w = R("gg", at * 16, (at + n) * 16), ind(XN, u("NBU", at, at + n))
+            if e == "v":
+                cp(o, w)
+            else:
+                act(o, w)
+            at += n
+        at = 0
+        for ci, (n, e) in enumerate(CHUNKS):
+            o = P(1 + ci % 2, 0, n)
+            mo = ci % 2 * 2304
+            mm(o, b_("BOm16"), b_("XU", at, at + n), True, False)
+            for k in range(16):
+                mm(o, b_("BOm"), R("gg", at * 16 + k, (at + n) * 16, 16), False, False)
+            for k in range(16):
+                tt(R("mm", mo + k * n, mo + (k + 1) * n), R("gg", at * 16 + k, (at + n) * 16, 16), P(0, at, at + n), AL.max)
+                mm(o, b_("BO2"), R("mm", mo + k * n, mo + (k + 1) * n), False, k == 15)
+            if ci > 0:
+                ts(b_("B", at - pn, at), P(1 + (ci - 1) % 2, 0, pn), K["thc"], AL.is_ge)
+            if ci == 1:
+                ts(f("N4p", 0, 4), f("N4", 0, 4), 544.0, AL.add)
+                tt(f("N4c", 0, 4), f("N4", 0, 4), f("C4", 0, 4), AL.add)
+                for c in range(4):
+                    ts(b_("OH", 32 * c, 32 * c + 32), P(6, 0, 32), float(c), AL.is_equal)
+                for c in range(4):
+                    ts(f("DD", 32 * c, 32 * c + 32), P(6, 32, 64), -1.0, AL.mult, f("N4p", c, c + 1), AL.add)
+                ts(f("pos"), P(6, 32, 64), -544.0, AL.add)
+                ts(f("DDn"), f("DD"), -1.0, AL.mult, 4096.0, AL.add)
+            if ci == 2:
+                holes_table()
+            at += n; pn = n
+        if not last:
+            act(f("SLf"), sub(SL, 0, 512), scale=K["s01"])
+        ts(b_("B", at - pn, at), P(1 + (len(CHUNKS) - 1) % 2, 0, pn), K["thc"], AL.is_ge)
+        conv(P(4, 0, 32), b_("B"), "Yb", 512, (b_("ID"), b_("PEN")))
+        for c in range(4):
+            ts(b_("NE", 32 * c, 32 * c + 32), P(4, 0, 32), float(c), AL.is_equal)
+        tt(b_("LV"), b_("OH"), b_("NE"), AL.is_gt)
+        scan(b_("SLV", 1, 129), b_("ONE", 0, 128), b_("LV"), 0.0, AL.mult, AL.add)
+        mm(P(5, 4, 8), b_("BO"), b_("SLV", 32, 129, 32), True, False)
+        mm(P(5, 4, 8), b_("BOm"), b_("SLV", 0, 128, 32), False, True)
+        mm(P(5, 0, 4), b_("BO"), b_("SLV", 32, 129, 32), True, True)
+        for c in range(4):
+            mm(P(5, 32, 64), b_("IDmb"), b_("LV", 32 * c, 32 * c + 32), c == 0, c == 3)
+        tt(f("dl"), b_("LV"), f("DD"), AL.mult)
+        tt(f("q"), b_("LV"), f("DDn"), AL.mult)
+        for c in range(4):
+            ts(b_("HF", 32 * c, 32 * c + 32), f("dl", 32 * c, 32 * c + 32), P(5, 4 + c, 5 + c), AL.is_gt)
+        scan(b_("SHF"), b_("ONE", 0, 128), b_("HF"), 0.0, AL.mult, AL.add)
+        mm(P(7, 0, 128), b_("ID"), b_("C512"), True, False)
+        mm(P(7, 0, 128), b_("NUP"), b_("HF"), False, False)
+        mm(P(7, 0, 128), b_("BO"), b_("SHF"), False, True)
+        for c in range(4):
+            ts(f("Z9", c, 288, 9), f("q", 32 * c, 32 * c + 32), P(5, c, c + 1), AL.add, -4096.0, AL.add)
+        tt(f("Z9", 8, 288, 9), P(5, 32, 64), f("TRJ"), AL.add)
+        for c in range(4):
+            tt(f("Z9", 4 + c, 288, 9), P(7, 32 * c, 32 * c + 32), b_("HF", 32 * c, 32 * c + 32), AL.mult)
+        scan(f("Z9o"), f("R9"), f("Z9"), 0.0, AL.mult, AL.max)
+        cp(u("SLOT"), f("Z9o", 8, 288, 9))
+        act(ind(TT, u("SLOT")), f("PUf"), AF.Silu)
+        tt(b_("JN"), b_("NE"), b_("OH"), AL.is_gt)
+        tt(f("K4", 0, 4), f("N4c", 0, 4), P(5, 0, 4), AL.subtract)
+        scan(b_("SJ", 1, 129), b_("ONE", 0, 128), b_("JN"), 0.0, AL.mult, AL.add)
+        mm(P(3, 0, 128), b_("IDb"), b_("JN"), True, False)
+        mm(P(3, 0, 128), b_("NUP"), b_("JN"), False, False)
+        mm(P(3, 0, 128), b_("BO"), b_("SJ", 1, 129), False, True)
+        mm(P(3, 128, 132), b_("BO"), b_("SJ", 0, 128, 32), True, True)
+        mm(P(3, 132, 136), b_("BO"), b_("SJ", 32, 129, 32), True, False)
+        mm(P(3, 132, 136), b_("BOm"), b_("SJ", 0, 128, 32), False, True)
+        for c in range(5):
+            ts(f("Z5", c, 160, 5), f("JW"), -1.0 if c == 0 else P(5, c - 1, c), AL.is_ge, float(DZ) if c == 4 else f("K4", c, c + 1), AL.mult)
+        scan(f("Z5o"), f("R5"), f("Z5"), 0.0, AL.mult, AL.max)
+        tt(f("KJa", 0, 4), f("N4c", 0, 4), P(5, 4, 8), AL.subtract)
+        tt(f("tp"), f("Z5o", 4, 160, 5), f("JW"), AL.add)
+        tt(f("KJ", 0, 4), f("KJa", 0, 4), P(3, 128, 132), AL.subtract)
+        cp(u("TP"), f("tp"))
+        act(b_("TSb"), ind(BG, u("TP")))
+        for c in range(4):
+            ts(f("Z4", c, 128, 4), P(3, 32 * c, 32 * c + 32), f("KJ", c, c + 1), AL.add, -16385.0, AL.add)
+        ts(f("n25"), P(4, 0, 32), float(V_), AL.mult)
+        tt(f("tb"), P(5, 32, 64), f("pos"), AL.add)
+        scan(f("Z4o"), f("R4"), f("Z4"), 0.0, AL.mult, AL.max)
+        if not last:
+            tt(f("ta"), P(5, 32, 64), f("TRB"), AL.add)
+            tt(f("nA", 0, 4), f("N4", 0, 4), P(5, 4, 8), AL.subtract)
+            tt(f("tc"), f("Z4o", 3, 128, 4), f("ta"), AL.max)
+            tt(f("N4", 0, 4), f("nA", 0, 4), P(3, 132, 136), AL.add)
+            cp(u("BJ"), f("tc"))
+            act(ind(BS, u("BJ")), f("SLf"), AF.Silu)
+        tt(f("td"), f("Z4o", 3, 128, 4), f("n25"), AL.subtract)
+        tt(f("te"), f("td"), f("tb"), AL.max)
+        cp(u("PN"), f("te"))
+        if last:
+            cp(b_("JV"), ind(SF, u("PN")))
+        else:
+            act(b_("JV"), ind(SF, u("PN")))
+        scan(b_("CU"), R("d0", 0, 512), sub(TT, 0, 512), 0.0, AL.mult, AL.add)
+        conv(P(6, 0, 32), b_("CU"), "Ym", 512)
+        if last:
+            touched_update()
+        conv(P(7, 0, 32), b_("TSb"), "Ys", 512)
+        if not last:
+            draw_places(t + 1)
+        tt(f("tf"), P(6, 0, 32), f("J512"), AL.min)
+        ts(u("IDX"), f("tf"), 512.0, AL.add)
+        cp(b_("TG"), ind(sub(TT, 0, 1536), u("IDX")))
+        if not last:
+            conv(P(0, 0, 32), b_("TG"), "Yt", 512)
+            touched_update()
+        else:
+            mm(P(2, 0, 512), b_("TR2"), b_("TG"), True, True)
+        ts(f("m4"), P(6, 0, 32), 2040.0, AL.is_ge, -4096.0, AL.mult)
+        tt(f("tg"), P(7, 0, 32), f("m4"), AL.add)
+        tt(f("th"), f("tg"), f("J544"), AL.max)
+        ts(u("PLO"), f("th"), -544.0, AL.add)
+        if not last:
+            ts(u("BOW"), P(0, 0, 32), -544.0, AL.add)
+            cp(ind(BS, u("BOW")), b_("TSb"))
+        else:
+            ts(f("SLf"), P(2, 0, 512), K["m512"], AL.add)
+            cp(ind(PL, u("PLO")), f("SLf"))
+            big = 12582912.0
+            act(R("bag", 0, 768), R("pl", SH + 1792, SH + V_), bias=big)
+            act(R("ypb", 1792, V_), R("bag", 0, 768), bias=-big - 32.0)
+            for a, e in ((0, 896), (896, 1792)):
+                ts(R("ypb", a, e), R("pl", SH + a, SH + e), big, AL.add, big + 32.0, AL.subtract)
+            for a, e in ((0, 896), (1792, V_), (896, 1792)):
+                dma(T.yp[:, a:e], R("ypb", a, e, 1, 0, 16))
+
+    def psum(x):
+        return x[0][0] == "p" and x[0][1:].isdigit()
+
+    def cols(x, y):
+        if x[3] == y[3] and x[3] > 1 and (x[1] - y[1]) % x[3]:
+            return False
+        return x[1] < y[2] and y[1] < x[2]
+
+    def meet(x, y):
+        if psum(x):
+            return True
+        if x[5] == y[5] and x[5] > 1 and x[4] != y[4]:
+            return False
+        return cols(x, y)
+
+    def covers(x, y):
+        return x[3] == 1 and x[5] == 1 and x[1] <= y[1] and y[2] <= x[2]
+
+    live = {}
+    deps = []
+    for n, o in enumerate(ops):
+        dp = set()
+        for x, w in [(x, False) for x in o["rd"]] + [(x, True) for x in o["wr"]]:
+            for y, m, wy in live.get(x[0], []):
+                if m == n or not meet(x, y):
+                    continue
+                q = ops[m]
+                if q["e"] == o["e"] and not q["dma"]:
+                    if o["e"] != "p" and cols(x, y) and (wy or w):
+                        dp.add(m)
+                elif (wy or w or psum(x)) and o["e"] != "x":
+                    dp.add(m)
+        deps.append(dp)
+        for x in o["wr"]:
+            if not o["scat"]:
+                live[x[0]] = [z for z in live.get(x[0], []) if not (covers(x, z[0]) and z[1] in dp)]
+            live.setdefault(x[0], []).append((x, n, True))
+        if not o.get("remote"):
+            for x in o["rd"]:
+                lst = live.setdefault(x[0], [])
+                if not o["dma"]:
+                    lst[:] = [z for z in lst if not (z[0] == x and not z[2] and ops[z[1]]["e"] == o["e"])]
+                lst.append((x, n, False))
+    seen = {e: {} for e in "vspgy"}
+    need = set()
+    for n, o in enumerate(ops):
+        if o["e"] == "x":
+            continue
+        best, s, kept = {}, seen[o["e"]], set()
+        for m in deps[n]:
+            q = ops[m]
+            key = m if (q["dma"] or q["ext"]) else q["e"]
+            best[key] = max(best.get(key, -1), m)
+        for key, m in best.items():
+            if s.get(key, -1) < m:
+                s[key] = m
+                kept.add(m)
+        deps[n] = kept
+        need |= kept
+    queue = {"v": g.vector, "s": g.scalar, "p": g.tensor, "g": g, "y": g.sync}
+    cnt = {e: 0 for e in "vspg"}
+    tok = {}
+    nd = 0
+    for n, o in enumerate(ops):
+        if o["ext"]:
+            tok[n] = o["ext"]
+            continue
+        for m in sorted(deps[n]):
+            queue[o["e"]].wait_ge(T.sem[tok[m][0]], tok[m][1])
+        ins = o["fn"]()
+        if o["dma"]:
+            tok[n] = ("dm%d" % nd, 16); nd += 1
+            ins.then_inc(T.sem[tok[n][0]], 16)
+        elif n in need:
+            cnt[o["e"]] += 1
+            tok[n] = ("q" + o["e"], cnt[o["e"]])
+            ins.then_inc(T.sem["q" + o["e"]], 1)
+    for n, o in enumerate(ops):
+        if o["dma"] and n not in need:
+            g.sync.wait_ge(T.sem[tok[n][0]], 16)
+    g.wait_ge(T.sem.sent, RO * ne)

@@ -6,18 +6,19 @@ V_, SH, RO = 2560, 512, 3
 QS = (32, 32, 64, 128)
 DZ, BAGW, TW_ = 10240, 11792, 2064
 CHUNKS = ((80, "v"), (144, "s"), (128, "s"), (96, "s"), (64, "s"))
+MV = 16
 
 F32 = dict(blk=256, rcol=16, E=16, BK=16, G9=16, col=48, JW=32, JH=16, C25=16, DZJ=16, SDE=16, Q4=16, C4=16,
            TS=16, G4=16, N4=16, N4p=16, N4c=16, s13=16, jb=16, pc=16, inv=16, iv=16, mx=16, JT=256, c65=16, cD=32, c513=32,
-           TRJ=32, TRB=32, J544=32, J512=32, t16=16, t32=32, t32b=32, DD=128, DDn=128, pos=32, dl=128, q=128,
+           TRJ=32, TRB=32, J544=32, J512=32, t16=16, t32=32, t32b=32, DD=128, DDn=128, pos=32, ocv=32, dl=128, q=128,
            Z9=288, Z9o=288, R9=288, Z5=160, Z5o=160, R5=160, Z4=128, Z4o=128, R4=128, K4=16, KJ=16, KJa=16, n25=32, tp=32,
            ta=32, tb=32, tc=32, td=32, te=32, m4=32, tf=32, tg=32, th=32, nA=16, plf=160, c1=160, c2=160, SLf=512, JVf=512, PUf=512,
            one=128, msg=3 * 80, land=9 * 80)
 BF = dict(Z=16 * 144, Ys=144, Yj=144, Yr=144, Yk=144, Yc=144, Yp=144, Yb=144, Ym=144, Yt=144, BO=128, BO2=128, BOm=128, BOm16=128,
           NUP=128, ID=128, ID16=128, IDm=128, IDb=128, IDmb=128, TR1=128, TR1b=128, TR2=128, TR3=128, C75=64, C512=128, ONE=512,
-          VD=256, VN=256, UF=512, XM=256, DL=256, ND=256, RS=256, RK=512, XU=512, PU=512, B=512, PEN=32, OH=128, NE=128, LV=128,
+          VD=256, VN=256, UF=512, XM=256, DL=256, XL=64, RS=256, RK=512, XU=512, PU=512, B=512, PEN=32, OH=128, NE=128, LV=128,
           JN=128, HF=128, SLV=144, SHF=128, SJ=144, CU=512, TG=512, TSb=512, JV=512, ge=480, fl=5 * 160, nh=160, nl=160, th=16, tl=16,
-          blk=256, SEL=3 * 336, SL=3 * 1024, CS=1040)
+          blk=256, lv=32, SEL=3 * 336, SL=3 * 1024, CS=1040)
 U16 = dict(plu=160, DP=16, U0=32, DWc=16, NBD=256, SW=16, JWu=16, RW=32, UW=32, NBU=512, GO=16, SLOT=32, TP=32, IDX=32, BOW=32,
            PLO=32, BJ=32, PN=32)
 I32 = dict(plc=160, pi=16, ts=16, tsh=16, tsl=16, xi=16, bi=16, pr=16, sh=16, a=160, b=160, c=160, d=160, e=160, n0=160)
@@ -45,7 +46,7 @@ SCRATCH.update({
 })
 for _k in range(8):
     SCRATCH["p%d" % _k] = ("psum", [128, 512], "float32")
-NDMA = 22
+NDMA = 30
 SEMAPHORES = ["qv", "qs", "qp", "qg", "gin", "sent", "sent0"] + ["arr%d" % k for k in range(3)] + ["dm%d" % k for k in range(NDMA)]
 
 
@@ -160,6 +161,18 @@ def rank_program(g, core, T, topo):
         ops[-1]["remote"] = True
         return bin(m).count("1")
 
+    def weave(*parts):
+        lists = []
+        for p in parts:
+            k = len(ops)
+            p()
+            lists.append(ops[k:])
+            del ops[k:]
+        while any(lists):
+            for l in lists:
+                if l:
+                    ops.append(l.pop(0))
+
     ncol = [0]
 
     def column(terms, const=0.0):
@@ -202,6 +215,7 @@ def rank_program(g, core, T, topo):
     iota(LO, [[0, 16], [1, 16]])
     iota(HI, [[1, 16], [0, 16]])
     mset(R("ab", AT["ab"]["Ys"], AT["ab"]["Yc"]), 0.0)
+    mset(R("xw", 0, SH), 0.0)
     ts(i_("pi", 1, 2), i_("pi", 0, 1), 15, AL.bitwise_and)
     cp(f("rcol", 0, 1), i_("pi", 1, 2))
     ts(f("E"), sub(LO, 0, 16), f("rcol", 0, 1), AL.is_equal)
@@ -219,18 +233,20 @@ def rank_program(g, core, T, topo):
     asel(f("G9", 0, 9), f("G9", 0, 9), [[16, 9]], AL.is_ge, -1, -1)
     asel(b_("BO"), f("one"), [[-16, 8], [0, 16]], AL.is_ge, 0, 1)
     asel(b_("BO"), b_("BO"), [[16, 8], [0, 16]], AL.is_ge, 15, -1)
-    iota(f("JW"), [[16, 32]])
     ne = send(R("xw", SH, SH + 512), lambda d: R("xw", 3072 + (d - 1) * 512, 3072 + d * 512), "gin", "sent0")
     ext("gin", ne * (N - 1), R("xw", 3072, 4608))
+    iota(f("JW"), [[16, 32]])
+    iota(b_("ONE"), [[0, 512]], 1)
     iota(f("C4", 0, 4), [[V_, 4]])
     for c, (a, e) in enumerate(cr):
         iota(f("C25", a, e), [[0, e - a]], V_ * c)
-    iota(f("JT"), [[1, 256]])
-    asel(b_("ID"), f("one"), [[-1, 128]], AL.is_equal, 0, 1)
-    iota(b_("ONE"), [[0, 512]], 1)
-    iota(R("nbt", 0, SH), [[0, SH]])
-    iota(R("xw", 0, SH), [[0, SH]])
-    iota(R("ff", SH, 3072), [[0, V_]])
+    for r in range(0, 15, 3):
+        asel(b_("Z", r * 144, (r + 3) * 144), b_("ONE", 0, 432), [[-1, 3], [-16, 9], [-1000, 16]], AL.is_equal, 16 - r, 1)
+        if r == 3:
+            iota(f("JT"), [[1, 256]])
+            iota(R("nbt", 0, SH), [[0, SH]])
+            asel(b_("ID"), f("one"), [[-1, 128]], AL.is_equal, 0, 1)
+    asel(b_("Z", 15 * 144, 16 * 144), b_("ONE", 0, 144), [[-16, 9], [-1000, 16]], AL.is_equal, 1, 1)
     iota(b_("CS"), [[0, 1040]], 65)
     iota(R("ab", AT["ab"]["Yc"], AT["ab"]["BO"]), [[0, 720]])
     iota(R("ab", AT["ab"]["TR1"], AT["ab"]["C75"]), [[0, 512]])
@@ -241,35 +257,50 @@ def rank_program(g, core, T, topo):
     for k in range(12):
         ts(R("sf", k * 256, (k + 1) * 256), b_("blk"), f("BK", k, k + 1), AL.add)
     dma(NF, SF)
+    for k in range(1, 6):
+        dma(R("ff", k * 512, (k + 1) * 512), R("xw", 0, SH))
     ts(i_("tsh"), i_("ts"), 0x1FF00, AL.bitwise_and)
     ts(i_("tsl"), i_("ts"), 255, AL.bitwise_and)
     cp(f("plf"), i_("plc"))
     cp(b_("th"), i_("tsh")); cp(b_("tl"), i_("tsl"))
     mm(P(4, 0, 16), b_("BO"), b_("th"), True, False); mm(P(4, 0, 16), b_("BO"), b_("tl"), False, True)
+    ts(i_("a"), i_("n0"), float(SH), AL.add)
     for c in range(1, 4):
         ts(b_("ge", (c - 1) * 160, c * 160), f("plf"), float(V_ * c), AL.is_ge)
     mm(P(5, 0, 480), b_("BO"), b_("ge"), True, True)
-    ts(i_("a"), i_("n0"), float(SH), AL.add)
-    mset(b_("Z"), 0.0)
     ts(i_("b"), i_("a"), 4, AL.arith_shift_right)
     ts(i_("c"), i_("a"), 15, AL.bitwise_and)
     ts(b_("nh"), i_("b"), 32.0, AL.add); ts(b_("nl"), i_("c"), 32.0, AL.add)
     dma(R("nf", SH, 3072, 1, 0, 16), b_("nh")); dma(R("nf", SH, 3072, 1, 1, 16), b_("nl"))
+    ts(R("d0", 0, 320), b_("ONE", 0, 320), column([(3, -1), (8, -1)], 1.0), AL.mult)
+    for k in range(1, 4):
+        dma(R("d0", k * 320, (k + 1) * 320), R("d0", 0, 320))
     for t in range(RO):
         dma(b_("SEL", t * 336, t * 336 + 64), R("sf", 2048, 2112))
         dma(b_("SL", t * 1024, t * 1024 + 512), R("sf", 0, 512))
-    tt(f("c1"), b_("ge", 0, 160), b_("ge", 160, 320), AL.add)
-    ts(i_("d"), i_("plc"), 0x3FC0, AL.bitwise_and); ts(i_("e"), i_("plc"), 63, AL.bitwise_and)
-    tt(f("c1"), f("c1"), b_("ge", 320, 480), AL.add)
-    cp(b_("fl", 480, 640), i_("d")); cp(b_("fl", 640, 800), i_("e"))
-    ts(f("c2"), f("c1"), float(-V_), AL.mult)
-    ts(b_("fl", 0, 160), f("c1"), 32.0, AL.mult)
-    tt(i_("a"), f("c2"), f("plf"), AL.add)
-    for r in range(16):
-        ts(b_("Z", r * 144, (r + 1) * 144, 16), f("G9", 0, 9), f("E", r, r + 1), AL.mult)
-    ts(i_("b"), i_("a"), 4, AL.arith_shift_right); ts(i_("c"), i_("a"), 15, AL.bitwise_and)
-    cp(b_("fl", 160, 320), i_("b")); cp(b_("fl", 320, 480), i_("c"))
-    c32 = column([(0, 32), (2, 32), (3, 32)])
+
+    def place_fields():
+        tt(f("c1"), b_("ge", 0, 160), b_("ge", 160, 320), AL.add)
+        ts(i_("d"), i_("plc"), 0x3FC0, AL.bitwise_and)
+        tt(f("c1"), f("c1"), b_("ge", 320, 480), AL.add)
+        ts(i_("e"), i_("plc"), 63, AL.bitwise_and)
+        ts(f("c2"), f("c1"), float(-V_), AL.mult)
+        cp(b_("fl", 480, 640), i_("d"))
+        tt(i_("a"), f("c2"), f("plf"), AL.add)
+        cp(b_("fl", 640, 800), i_("e"))
+        ts(b_("fl", 0, 160), f("c1"), 32.0, AL.mult)
+        ts(i_("b"), i_("a"), 4, AL.arith_shift_right); ts(i_("c"), i_("a"), 15, AL.bitwise_and)
+        cp(b_("fl", 160, 320), i_("b")); cp(b_("fl", 320, 480), i_("c"))
+
+    def sizes():
+        K["c32"] = column([(0, 32), (2, 32), (3, 32)])
+        ts(f("JW"), f("JW"), f("rcol", 0, 1), AL.add)
+        cp(f("TS"), P(4, 0, 16))
+        mset(f("G4", 0, 1), float(V_)); mset(f("G4", 4, 5), 0.0)
+        for c in range(1, 4):
+            red(f("G4", c, c + 1), P(5, (c - 1) * 160, c * 160))
+        mset(f("Q4", 0, 2), float(QS[0])); mset(f("Q4", 2, 3), float(QS[2])); mset(f("Q4", 3, 4), float(QS[3]))
+    weave(place_fields, sizes)
 
     def piece(r):
         return P((0, 2, 3, 6, 7)[r // 3], (r % 3) * 160, (r % 3 + 1) * 160) if r < 15 else P(1, 256, 416)
@@ -281,22 +312,16 @@ def rank_program(g, core, T, topo):
 
     def fetch(r0, r1):
         for r in range(r0, r1):
-            act(R("pl", SH + r, 3072, 16), piece(r), bias=c32)
-    spread(0, 9)
-    fetch(0, 9)
-    ts(f("JW"), f("JW"), f("rcol", 0, 1), AL.add)
-    cp(f("TS"), P(4, 0, 16))
-    mset(f("G4", 0, 1), float(V_)); mset(f("G4", 4, 5), 0.0)
-    for c in range(1, 4):
-        red(f("G4", c, c + 1), P(5, (c - 1) * 160, c * 160))
-    mset(f("Q4", 0, 2), float(QS[0])); mset(f("Q4", 2, 3), float(QS[2])); mset(f("Q4", 3, 4), float(QS[3]))
+            act(R("pl", SH + r, 3072, 16), piece(r), bias=K["c32"])
+    spread(0, 6)
+    fetch(0, 6)
     tt(f("N4", 0, 4), f("G4", 0, 4), f("G4", 1, 5), AL.subtract)
     for c, (a, e) in enumerate(cr):
         ts(f("JH", a, e), f("JW", a, e), float(16 * a), AL.subtract, float(4096 // QS[c]), AL.mult)
         ts(f("SDE", a, e), f("one", a, e), f("TS", 4 + c, 5 + c), AL.mult)
     ts(f("DZJ"), f("JW", 0, 16), float(DZ), AL.add)
 
-    def draw_places(t):
+    def draw_first(t):
         ts(f("s13", 0, 1), f("N4", 0, 1), 13.0, AL.mult, float(41 * t), AL.add)
         tt(f("inv", 0, 4), f("N4", 0, 4), f("Q4", 0, 4), AL.is_lt)
         ts(i_("xi"), f("SDE"), f("s13", 0, 1), AL.add)
@@ -304,6 +329,8 @@ def rank_program(g, core, T, topo):
             ts(f("iv", a, e), f("DZJ", a, e), f("inv", c, c + 1), AL.mult)
         for a, e, m in ((0, 4, 127), (4, 8, 63), (8, 16, 31)):
             ts(i_("bi", a, e), i_("xi", a, e), m, AL.bitwise_and)
+
+    def draw_second():
         tt(f("jb"), i_("bi"), f("JH"), AL.add)
         for c, (a, e) in enumerate(cr):
             ts(i_("pr", a, e), f("jb", a, e), f("N4", c, c + 1), AL.mult)
@@ -312,10 +339,13 @@ def rank_program(g, core, T, topo):
         tt(f("mx"), f("pc"), f("iv"), AL.max)
         cp(u("DP"), f("mx"))
 
-    draw_places(0)
-    cp(R("bag", DZ, DZ + 512), R("sf", 0, 512))
-    ts(f("JT"), f("JT"), f("E", 4, 5), AL.mult)
-    ymat("Ys", [(0, 16), (1, 1)])
+    def tables_draw():
+        ymat("Ys", [(0, 16), (1, 1)])
+        ymat("Yj", [(4, 1)]); ymat("Yr", [(0, 1), (1, 1000)])
+        K["k64"] = column([(1, 64)])
+        ts(f("c65"), f("JW", 0, 16), 65.0, AL.add)
+        ts(f("JT"), f("JT"), f("E", 4, 5), AL.mult)
+        cp(R("bag", DZ, DZ + 512), R("sf", 0, 512))
 
     def tables_move():
         ts(b_("ID16"), b_("ID"), 0.0625, AL.mult); ts(b_("IDm"), b_("ID"), -1.0, AL.mult)
@@ -323,42 +353,39 @@ def rank_program(g, core, T, topo):
         ts(b_("VN"), b_("ONE", 0, 256), f("E", 2, 3), AL.mult)
         ts(b_("VD"), b_("ONE", 0, 256), column([(0, 1), (1, 1), (3, 1)]), AL.mult)
 
-    def tables_sort():
-        ymat("Yj", [(4, 1)]); ymat("Yr", [(0, 1), (1, 1000)])
-        K["k64"] = column([(1, 64)])
-        ts(f("c65"), f("JW", 0, 16), 65.0, AL.add)
-        keep = column([(3, -1), (8, -1)], 1.0)
-        for k in range(5):
-            act(R("d0", k * 256, (k + 1) * 256), b_("ONE", 0, 256), scale=keep)
-
     def tables_sort2():
         ts(R("ct", 0, SH), b_("ONE"), f("E", 3, 4), AL.mult, 2.0, AL.mult)
         ymat("Yk", [(0, 1), (2, 1), (3, 2048)])
         mset(f("cD", 0, 16), -2048.0); mset(f("cD", 16, 32), 0.0)
         ts(f("c513"), f("JW"), 513.0, AL.add)
 
-    def tables_bags():
-        for nme, w in (("BOm", -1.0), ("BO2", 2.0), ("BOm16", -16.0)):
-            act(b_(nme), b_("BO"), scale=w)
-        asel(b_("NUP"), b_("BOm"), [[-1, 128]], AL.is_gt, 0, 1)
-        act(b_("IDb"), b_("ID"), scale=16384.0); act(b_("IDmb"), b_("ID"), scale=-16384.0)
-        act(f("TRJ"), f("JW"), bias=1552.0); act(f("TRB"), f("JW"), bias=float(DZ + 513))
-        act(f("J544"), f("JW"), bias=544.0); act(f("J512"), f("JW"), bias=512.0)
+    def tables_a():
         K["pus"] = column([(1, 1), (2, 1), (3, 1)]); K["m32"] = column([(8, 32)])
         ymat("Yc", [(1, 1.0 / 32)]); ymat("Yp", [(2, 16), (3, 1)])
+
+    def tables_b():
         K["thc"] = column([(4, -1e9), (5, -1e9), (6, -1e9)], 1e9)
         for k in range(3):
             ts(K["thc"], f("E", 4 + k, 5 + k), f("TS", k, k + 1), AL.mult, K["thc"], AL.add)
 
-    def tables_bags2():
+    def tables_c():
         trmat("TR3", {2: [(0, 1)], 3: [(1, 1)]})
         K["c128"] = column([(1, 128)]); K["m512"] = column([(0, -512)]); K["s01"] = column([(0, 1), (1, 1)])
-        ymat("Yb", [(4, 1), (5, 1), (6, 1)]); ymat("Ym", [(6, 1), (7, 1), (8, 64)]); ymat("Yt", [(1, 80), (2, 16), (3, 1)])
-        trmat("TR1", {0: [(0, 16), (1, 1)], 2: [(0, 1)], 3: [(1, 1)]})
-        trmat("TR1b", {0: [(4, V_), (5, V_), (6, V_)], 1: [(4, 32), (5, 32), (6, 32)]})
-        trmat("TR2", {0: [(1, 80), (2, 16), (3, 1)], 1: [(1, 1)], 2: [(2, 1)], 3: [(3, 1)]})
         for nme in ("R9", "R5", "R4"):
             ts(f(nme), f(nme), 1.0, AL.min)
+
+    def tables_d():
+        ymat("Yb", [(4, 1), (5, 1), (6, 1)]); ymat("Ym", [(6, 1), (7, 1), (8, 64)])
+
+    def tables_e():
+        ymat("Yt", [(1, 80), (2, 16), (3, 1)])
+        trmat("TR1", {0: [(0, 16), (1, 1)], 2: [(0, 1)], 3: [(1, 1)]})
+
+    def tables_f():
+        trmat("TR1b", {0: [(4, V_), (5, V_), (6, V_)], 1: [(4, 32), (5, 32), (6, 32)]})
+
+    def tables_g():
+        trmat("TR2", {0: [(1, 80), (2, 16), (3, 1)], 1: [(1, 1)], 2: [(2, 1)], 3: [(3, 1)]})
 
     def holes_table():
         act(R("tt", 0, 256), b_("ONE", 0, 256), scale=f("E", 6, 7)); act(R("tt", 256, 512), b_("ONE", 0, 256), scale=f("E", 7, 8))
@@ -366,13 +393,26 @@ def rank_program(g, core, T, topo):
             mm(P(k, 0, 512), b_("TR3"), R("sf", a, a + 512), True, True)
             act(R("tt", a, a + 512), P(k, 0, 512), bias=K["c128"])
 
+    def joins_positions():
+        ts(f("n25"), P(4, 0, 32), float(V_), AL.mult)
+        tt(f("tb"), P(5, 32, 64), f("pos"), AL.add)
+        tt(f("td"), f("Z4o", 3, 128, 4), f("n25"), AL.subtract)
+        tt(f("te"), f("td"), f("tb"), AL.max)
+        cp(u("PN"), f("te"))
+
+    def stayers_sites():
+        ts(f("m4"), P(6, 0, 32), 2040.0, AL.is_ge, -4096.0, AL.mult)
+        tt(f("tg"), P(7, 0, 32), f("m4"), AL.add)
+        tt(f("th"), f("tg"), f("J544"), AL.max)
+        ts(u("PLO"), f("th"), -544.0, AL.add)
+
     def touched_update():
         mm(P(1, 0, 512), b_("TR1b"), b_("B"), True, False)
         mm(P(1, 0, 512), b_("TR1"), b_("JV"), False, True)
         act(f("JVf"), P(1, 0, 512), bias=K["m512"])
         act(ind(PL, u("UW")), f("JVf"), AF.Silu)
 
-    tables_sort()
+    weave(lambda: (draw_first(0), draw_second()), tables_draw)
     for t in range(RO):
         last = t == RO - 1
         SEL, SL = b_("SEL", t * 336, (t + 1) * 336), b_("SL", t * 1024, (t + 1) * 1024)
@@ -382,16 +422,21 @@ def rank_program(g, core, T, topo):
         conv(P(4, 0, 16), DF, "Ys", 256)
         if t == 0:
             tables_move()
+        elif t == 1:
+            weave(stayers_sites, tables_g)
+        else:
+            stayers_sites()
         ts(DW, P(4, 0, 16), -544.0, AL.add)
         cp(u("NBD"), ind(NBT, DW))
         cp(N0F, ind(NF, DW))
         conv(P(5, 0, 16), N0F, "Ys", 256)
         if t == 0:
-            spread(9, 16)
+            spread(6, 11)
         ts(u("DWc"), P(4, 0, 16), -544.0, AL.add, 1024.0, AL.min)
         ts(b_("XM"), ind(XS, DW), -192.0, AL.add)
         for k in range(4):
-            act(R("gg", k * 1024, (k + 1) * 1024), ind(XN, u("NBD", k * 64, (k + 1) * 64)))
+            e = (k + 1) * 64 - (MV if k == 3 else 0)
+            act(R("gg", k * 1024, e * 16), ind(XN, u("NBD", k * 64, e)))
 
         def move_sum(k):
             o = P(1, k * 64, (k + 1) * 64)
@@ -411,19 +456,20 @@ def rank_program(g, core, T, topo):
         tt(f("t16"), P(4, 0, 16), f("c65"), AL.min)
         ts(u("SW"), f("t16"), -1.0, AL.add)
         cp(ind(SEL, u("SW")), DF)
+        cp(R("gg", (256 - MV) * 16, 4096), ind(XN, u("NBD", 256 - MV, 256)))
         move_sum(2)
         conv(P(5, 0, 4), sub(SEL, 0, 64), "Yj", 64)
-        conv(P(5, 4, 8), sub(SEL, 0, 64), "Ys", 64)
         move_sum(3)
+        conv(P(5, 4, 8), sub(SEL, 0, 64), "Ys", 64)
         scan(R("ct", SH + 1280, 3072), R("d0", 0, 1280), sub(F, SH + 1280, 3072), R("ct", SH + 1279, SH + 1280), AL.mult, AL.add)
         if t == 0:
             tables_sort2()
+        act(b_("RK"), ind(R("ct", 0, 3072), u("U0")))
         cp(u("JWu", 0, 4), P(5, 0, 4))
         ts(sub(msg, 64, 68), P(5, 4, 8), -544.0 - SH, AL.add)
-        act(b_("RK"), ind(R("ct", 0, 3072), u("U0")))
         ts(b_("DL"), P(1, 0, 256), 189.0, AL.max, 195.0, AL.min)
-        tt(b_("ND"), b_("DL"), b_("XM"), AL.add)
-        cp(sub(msg, 0, 64), ind(b_("ND"), u("JWu", 0, 4)))
+        cp(b_("XL"), ind(b_("XM"), u("JWu", 0, 4)))
+        tt(sub(msg, 0, 64), ind(b_("DL"), u("JWu", 0, 4)), b_("XL"), AL.add)
         ne = send(msg, lambda d, t=t: f("land", (3 * t + d - 1) * 80, (3 * t + d - 1) * 80 + 68), "arr%d" % t, "sent")
         conv(P(4, 0, 32), b_("RK"), "Yk", 512)
         if t > 0:
@@ -431,31 +477,32 @@ def rank_program(g, core, T, topo):
             act(f("JVf"), P(2, 0, 512), bias=K["m512"])
             act(ind(PL, u("PLO")), f("JVf"), AF.Silu)
         else:
-            fetch(9, 16)
+            spread(11, 16)
+            fetch(6, 16)
             ext("sent0", ne, R("xw", SH, SH + 512))
+            weave(tables_a, tables_b)
         tt(f("t32"), P(4, 0, 32), f("cD"), AL.add)
         tt(f("t32b"), f("t32"), f("c513"), AL.min)
         ts(u("RW"), f("t32b"), -1.0, AL.add)
         cp(ind(SL, u("RW")), b_("UF"))
         conv(P(5, 0, 32), sub(SL, 0, 512), "Ys", 512)
-        cp(ind(XS, DW), b_("ND"))
+        tt(ind(XS, DW), b_("DL"), b_("XM"), AL.add)
         if last:
             dma(T.yx[:], XO)
+        ts(u("UW"), P(5, 0, 32), -544.0, AL.add)
+        act(b_("XU"), ind(XS, u("UW")))
+        ts(b_("PEN"), P(5, 0, 32), 544.0 + SH, AL.is_lt, 8.0, AL.mult)
+        cp(u("NBU", 0, 256), ind(NBT, u("UW", 0, 16)))
         if t == 0:
-            tables_bags()
+            for nme, w in (("BOm", -1.0), ("BO2", 2.0), ("BOm16", -16.0)):
+                act(b_(nme), b_("BO"), scale=w)
+            asel(b_("NUP"), b_("BOm"), [[-1, 128]], AL.is_gt, 0, 1)
         if not last:
             iota(R("ff", SH, 3072), [[0, V_]])
-        ts(u("UW"), P(5, 0, 32), -544.0, AL.add)
-        ts(b_("PEN"), P(5, 0, 32), 544.0 + SH, AL.is_lt, 8.0, AL.mult)
-        cp(u("NBU"), ind(NBT, u("UW")))
-        act(b_("XU"), ind(XS, u("UW")))
         mm(P(0, 0, 512), b_("ID"), b_("XU"), True, True)
-        act(f("PUf"), ind(PL, u("UW")), bias=K["m32"], scale=K["pus"])
-        act(b_("PU"), f("PUf"))
+        act(b_("PU"), ind(PL, u("UW")), bias=K["m32"], scale=K["pus"])
         conv(P(6, 0, 32), b_("PU"), "Yc", 512, (b_("ID"), b_("PEN")))
         conv(P(6, 32, 64), b_("PU"), "Yp", 512)
-        if t == 0:
-            tables_bags2()
         ext("arr%d" % t, ne * (N - 1), f("land", 3 * t * 80, 3 * (t + 1) * 80))
         for d in range(1, N):
             o = (3 * t + d - 1) * 80
@@ -463,6 +510,7 @@ def rank_program(g, core, T, topo):
         for d in range(1, N):
             o = (3 * t + d - 1) * 80
             cp(ind(R("xw", 3072 + (d - 1) * 512, 3072 + (d - 1) * 512 + 1600), u("GO", 4 * (d - 1), 4 * d)), f("land", o, o + 64))
+        cp(u("NBU", 256, 512), ind(NBT, u("UW", 16, 32)))
         at = 0
         for n, e in CHUNKS:
             o, w = R("gg", at * 16, (at + n) * 16), ind(XN, u("NBU", at, at + n))
@@ -488,20 +536,30 @@ def rank_program(g, core, T, topo):
                 tt(f("N4c", 0, 4), f("N4", 0, 4), f("C4", 0, 4), AL.add)
                 for c in range(4):
                     ts(b_("OH", 32 * c, 32 * c + 32), P(6, 0, 32), float(c), AL.is_equal)
+                act(f("ocv"), P(6, 0, 32))
                 for c in range(4):
-                    ts(f("DD", 32 * c, 32 * c + 32), P(6, 32, 64), -1.0, AL.mult, f("N4p", c, c + 1), AL.add)
-                ts(f("pos"), P(6, 32, 64), -544.0, AL.add)
-                ts(f("DDn"), f("DD"), -1.0, AL.mult, 4096.0, AL.add)
+                    act(f("DD", 32 * c, 32 * c + 32), P(6, 32, 64), scale=-1.0, bias=f("N4p", c, c + 1))
+                if t == 0:
+                    act(b_("IDmb"), b_("ID"), scale=-16384.0); act(f("TRJ"), f("JW"), bias=1552.0)
+                    weave(tables_c, tables_d)
+                act(f("DDn"), f("DD"), scale=-1.0, bias=4096.0)
+                act(f("PUf"), ind(PL, u("UW")), bias=K["m32"], scale=K["pus"])
             if ci == 2:
                 holes_table()
+                act(f("pos"), P(6, 32, 64), bias=-544.0)
+                if t == 0:
+                    act(b_("IDb"), b_("ID"), scale=16384.0); act(f("TRB"), f("JW"), bias=float(DZ + 513))
+                    act(f("J544"), f("JW"), bias=544.0); act(f("J512"), f("JW"), bias=512.0)
             at += n; pn = n
         if not last:
             act(f("SLf"), sub(SL, 0, 512), scale=K["s01"])
         ts(b_("B", at - pn, at), P(1 + (len(CHUNKS) - 1) % 2, 0, pn), K["thc"], AL.is_ge)
         conv(P(4, 0, 32), b_("B"), "Yb", 512, (b_("ID"), b_("PEN")))
+        if t == 0:
+            weave(tables_e, tables_f)
+        tt(b_("lv"), P(4, 0, 32), f("ocv"), AL.not_equal)
         for c in range(4):
-            ts(b_("NE", 32 * c, 32 * c + 32), P(4, 0, 32), float(c), AL.is_equal)
-        tt(b_("LV"), b_("OH"), b_("NE"), AL.is_gt)
+            tt(b_("LV", 32 * c, 32 * c + 32), b_("OH", 32 * c, 32 * c + 32), b_("lv"), AL.mult)
         scan(b_("SLV", 1, 129), b_("ONE", 0, 128), b_("LV"), 0.0, AL.mult, AL.add)
         mm(P(5, 4, 8), b_("BO"), b_("SLV", 32, 129, 32), True, False)
         mm(P(5, 4, 8), b_("BOm"), b_("SLV", 0, 128, 32), False, True)
@@ -509,23 +567,27 @@ def rank_program(g, core, T, topo):
         for c in range(4):
             mm(P(5, 32, 64), b_("IDmb"), b_("LV", 32 * c, 32 * c + 32), c == 0, c == 3)
         tt(f("dl"), b_("LV"), f("DD"), AL.mult)
-        tt(f("q"), b_("LV"), f("DDn"), AL.mult)
         for c in range(4):
             ts(b_("HF", 32 * c, 32 * c + 32), f("dl", 32 * c, 32 * c + 32), P(5, 4 + c, 5 + c), AL.is_gt)
         scan(b_("SHF"), b_("ONE", 0, 128), b_("HF"), 0.0, AL.mult, AL.add)
         mm(P(7, 0, 128), b_("ID"), b_("C512"), True, False)
         mm(P(7, 0, 128), b_("NUP"), b_("HF"), False, False)
         mm(P(7, 0, 128), b_("BO"), b_("SHF"), False, True)
+        tt(f("q"), b_("LV"), f("DDn"), AL.mult)
+        tt(f("Z9", 8, 288, 9), P(5, 32, 64), f("TRJ"), AL.add)
         for c in range(4):
             ts(f("Z9", c, 288, 9), f("q", 32 * c, 32 * c + 32), P(5, c, c + 1), AL.add, -4096.0, AL.add)
-        tt(f("Z9", 8, 288, 9), P(5, 32, 64), f("TRJ"), AL.add)
         for c in range(4):
             tt(f("Z9", 4 + c, 288, 9), P(7, 32 * c, 32 * c + 32), b_("HF", 32 * c, 32 * c + 32), AL.mult)
         scan(f("Z9o"), f("R9"), f("Z9"), 0.0, AL.mult, AL.max)
         cp(u("SLOT"), f("Z9o", 8, 288, 9))
         act(ind(TT, u("SLOT")), f("PUf"), AF.Silu)
-        tt(b_("JN"), b_("NE"), b_("OH"), AL.is_gt)
+        for c in range(4):
+            ts(b_("NE", 32 * c, 32 * c + 32), P(4, 0, 32), float(c), AL.is_equal)
         tt(f("K4", 0, 4), f("N4c", 0, 4), P(5, 0, 4), AL.subtract)
+        tt(b_("JN"), b_("NE"), b_("OH"), AL.is_gt)
+        for c in range(5):
+            ts(f("Z5", c, 160, 5), f("JW"), -1.0 if c == 0 else P(5, c - 1, c), AL.is_ge, float(DZ) if c == 4 else f("K4", c, c + 1), AL.mult)
         scan(b_("SJ", 1, 129), b_("ONE", 0, 128), b_("JN"), 0.0, AL.mult, AL.add)
         mm(P(3, 0, 128), b_("IDb"), b_("JN"), True, False)
         mm(P(3, 0, 128), b_("NUP"), b_("JN"), False, False)
@@ -533,56 +595,49 @@ def rank_program(g, core, T, topo):
         mm(P(3, 128, 132), b_("BO"), b_("SJ", 0, 128, 32), True, True)
         mm(P(3, 132, 136), b_("BO"), b_("SJ", 32, 129, 32), True, False)
         mm(P(3, 132, 136), b_("BOm"), b_("SJ", 0, 128, 32), False, True)
-        for c in range(5):
-            ts(f("Z5", c, 160, 5), f("JW"), -1.0 if c == 0 else P(5, c - 1, c), AL.is_ge, float(DZ) if c == 4 else f("K4", c, c + 1), AL.mult)
         scan(f("Z5o"), f("R5"), f("Z5"), 0.0, AL.mult, AL.max)
         tt(f("KJa", 0, 4), f("N4c", 0, 4), P(5, 4, 8), AL.subtract)
         tt(f("tp"), f("Z5o", 4, 160, 5), f("JW"), AL.add)
-        tt(f("KJ", 0, 4), f("KJa", 0, 4), P(3, 128, 132), AL.subtract)
+        if not last:
+            tt(f("nA", 0, 4), f("N4", 0, 4), P(5, 4, 8), AL.subtract)
         cp(u("TP"), f("tp"))
         act(b_("TSb"), ind(BG, u("TP")))
+        tt(f("KJ", 0, 4), f("KJa", 0, 4), P(3, 128, 132), AL.subtract)
+        if not last:
+            tt(f("N4", 0, 4), f("nA", 0, 4), P(3, 132, 136), AL.add)
         for c in range(4):
             ts(f("Z4", c, 128, 4), P(3, 32 * c, 32 * c + 32), f("KJ", c, c + 1), AL.add, -16385.0, AL.add)
-        ts(f("n25"), P(4, 0, 32), float(V_), AL.mult)
-        tt(f("tb"), P(5, 32, 64), f("pos"), AL.add)
-        scan(f("Z4o"), f("R4"), f("Z4"), 0.0, AL.mult, AL.max)
         if not last:
             tt(f("ta"), P(5, 32, 64), f("TRB"), AL.add)
-            tt(f("nA", 0, 4), f("N4", 0, 4), P(5, 4, 8), AL.subtract)
-            tt(f("tc"), f("Z4o", 3, 128, 4), f("ta"), AL.max)
-            tt(f("N4", 0, 4), f("nA", 0, 4), P(3, 132, 136), AL.add)
-            cp(u("BJ"), f("tc"))
-            act(ind(BS, u("BJ")), f("SLf"), AF.Silu)
-        tt(f("td"), f("Z4o", 3, 128, 4), f("n25"), AL.subtract)
-        tt(f("te"), f("td"), f("tb"), AL.max)
-        cp(u("PN"), f("te"))
+        scan(f("Z4o"), f("R4"), f("Z4"), 0.0, AL.mult, AL.max)
         if last:
+            joins_positions()
             cp(b_("JV"), ind(SF, u("PN")))
-        else:
-            act(b_("JV"), ind(SF, u("PN")))
         scan(b_("CU"), R("d0", 0, 512), sub(TT, 0, 512), 0.0, AL.mult, AL.add)
         conv(P(6, 0, 32), b_("CU"), "Ym", 512)
         if last:
             touched_update()
         conv(P(7, 0, 32), b_("TSb"), "Ys", 512)
         if not last:
-            draw_places(t + 1)
+            tt(f("tc"), f("Z4o", 3, 128, 4), f("ta"), AL.max)
+            k = len(ops)
+            draw_first(t + 1)
+            cp(u("BJ"), f("tc"))
+            ops.insert(k + 1, ops.pop())
+            act(ind(BS, u("BJ")), f("SLf"), AF.Silu)
         tt(f("tf"), P(6, 0, 32), f("J512"), AL.min)
         ts(u("IDX"), f("tf"), 512.0, AL.add)
         cp(b_("TG"), ind(sub(TT, 0, 1536), u("IDX")))
         if not last:
             conv(P(0, 0, 32), b_("TG"), "Yt", 512)
+            weave(joins_positions, draw_second)
+            act(b_("JV"), ind(SF, u("PN")))
             touched_update()
-        else:
-            mm(P(2, 0, 512), b_("TR2"), b_("TG"), True, True)
-        ts(f("m4"), P(6, 0, 32), 2040.0, AL.is_ge, -4096.0, AL.mult)
-        tt(f("tg"), P(7, 0, 32), f("m4"), AL.add)
-        tt(f("th"), f("tg"), f("J544"), AL.max)
-        ts(u("PLO"), f("th"), -544.0, AL.add)
-        if not last:
             ts(u("BOW"), P(0, 0, 32), -544.0, AL.add)
             cp(ind(BS, u("BOW")), b_("TSb"))
         else:
+            mm(P(2, 0, 512), b_("TR2"), b_("TG"), True, True)
+            stayers_sites()
             ts(f("SLf"), P(2, 0, 512), K["m512"], AL.add)
             cp(ind(PL, u("PLO")), f("SLf"))
             big = 12582912.0

@@ -3,25 +3,28 @@ from concourse.mybir import AluOpType, AxisListType, ActivationFunctionType
 
 AL, AF = AluOpType, ActivationFunctionType
 V_, SH, RO = 2560, 512, 3
-QS = (32, 32, 64, 128)
-DZ, BAGW, TW_ = 10240, 11792, 2064
-CHUNKS = ((80, "v"), (144, "s"), (128, "s"), (96, "s"), (64, "s"))
-MV = 16
+DZ, BAGW, PLW, BIG = 10240, 11328, 3584, 131072
+CHUNKS = ((0, 64), (128, 0), (112, 16), (96, 16), (80, 0))
+MOVE_S = ((0, 64), (64, 144), (144, 192), (192, 208))
+MOVE_V = ((224, 256), (208, 224))
+SUMS = ((144, 192), (192, 256))
+SPR = (4, 10)
+ZG = 10
 
-F32 = dict(blk=256, rcol=16, E=16, BK=16, G9=16, col=48, JW=32, JH=16, C25=16, DZJ=16, SDE=16, Q4=16, C4=16,
-           TS=16, G4=16, N4=16, N4p=16, N4c=16, s13=16, jb=16, pc=16, inv=16, iv=16, mx=16, JT=256, c65=16, cD=32, c513=32,
-           TRJ=32, TRB=32, J544=32, J512=32, t16=16, t32=32, t32b=32, DD=128, DDn=128, pos=32, ocv=32, dl=128, q=128,
-           Z9=288, Z9o=288, R9=288, Z5=160, Z5o=160, R5=160, Z4=128, Z4o=128, R4=128, K4=16, KJ=16, KJa=16, n25=32, tp=32,
-           ta=32, tb=32, tc=32, td=32, te=32, m4=32, tf=32, tg=32, th=32, nA=16, plf=160, c1=160, c2=160, SLf=512, JVf=512, PUf=512,
-           one=128, msg=3 * 80, land=9 * 80)
-BF = dict(Z=16 * 144, Ys=144, Yj=144, Yr=144, Yk=144, Yc=144, Yp=144, Yb=144, Ym=144, Yt=144, BO=128, BO2=128, BOm=128, BOm16=128,
-          NUP=128, ID=128, ID16=128, IDm=128, IDb=128, IDmb=128, TR1=128, TR1b=128, TR2=128, TR3=128, C75=64, C512=128, ONE=512,
-          VD=256, VN=256, UF=512, XM=256, DL=256, XL=64, RS=256, RK=512, XU=512, PU=512, B=512, PEN=32, OH=128, NE=128, LV=128,
-          JN=128, HF=128, SLV=144, SHF=128, SJ=144, CU=512, TG=512, TSb=512, JV=512, ge=480, fl=5 * 160, nh=160, nl=160, th=16, tl=16,
-          blk=256, lv=32, SEL=3 * 336, SL=3 * 1024, CS=1040)
+CL = {k: n for n, k in enumerate("c cD km p0 k c25 pp iv0 ivc t n sd sd0 sd1 sd2 npp inv bk thc c33 sb NP nNP fn L s01 s03 s23 y".split())}
+F32 = dict(blk=256, rcol=16, E=16, E32=16, BK=16, G9=16, col=48, cl=32, JW=32, JH=16, TS=16, G4=16, G3=16, EQ=16, Aa=16, t4=16, T3=16,
+           TR=16, TR2=16, JT=256, c65=16, cD=32, c513=32, t16=16, t32=32, t32b=32, dB=32, dP=32, tc=32, tg=32, AD=128, A0=128,
+           S32=144, IQ=128, dq=128, qq=128, dl=128, q=128, mk=128, s1=128, ss=128, X=128, nh=160, nl=160, SLf=512, PUf=512, JVf=512,
+           TGf=512, one=128, msg=3 * 80, land=9 * 80)
+BF = dict(Z=16 * 144, G2=144, Ys=144, Yj=144, Yr=144, Yk=144, Yt=144, YP=144, YL=144, YJ=144, PEN=128, TR1=128, TR1b=128, TR3=128,
+          BO=128, BO2=128, BOm=128, BOm16=128, ID=128, ID16=128, IDm=128, TR2=128, Aeq=128, Ale=128, Alt=128, MB=128, SB=144, SG=144,
+          cB=128, C75=128, ONE=528, VD=256, VN=256, UF=512, RS=256, XM=256, DL=256, XL=64, RK=512, XU=512, PU=512, B=512,
+          JN=128, HF=128, SLV=128, SHF=128, SJ=128, TG=512, TSb=512, JV=512, d0u=512, SFb=512, fl=5 * 160, th=16,
+          tl=16, cnt=16, SEL=3 * 336, SL=3 * 1024, CS=1040)
+F16 = dict(ID=128, nd=128, dW=32, JW=32, nJ=32, Yu=144, S=144, fin=128, CU=512)
 U16 = dict(plu=160, DP=16, U0=32, DWc=16, NBD=256, SW=16, JWu=16, RW=32, UW=32, NBU=512, GO=16, SLOT=32, TP=32, IDX=32, BOW=32,
-           PLO=32, BJ=32, PN=32)
-I32 = dict(plc=160, pi=16, ts=16, tsh=16, tsl=16, xi=16, bi=16, pr=16, sh=16, a=160, b=160, c=160, d=160, e=160, n0=160)
+           PLO=32, BJ=32, PN=32, POF=32)
+I32 = dict(plc=160, pi=16, ts=16, tsh=16, tsl=16, xi=16, bi=16, pr=16, sh=16, b=160, c=160, d=160, e=160, n0=160)
 
 
 def _arena(d):
@@ -34,19 +37,19 @@ def _arena(d):
 
 AT = {}
 SCRATCH = {}
-for _n, _d, _t in (("af", F32, "float32"), ("ab", BF, "bfloat16"), ("au", U16, "uint16"), ("ai", I32, "int32")):
+for _n, _d, _t in (("af", F32, "float32"), ("ab", BF, "bfloat16"), ("ah", F16, "float16"), ("au", U16, "uint16"), ("ai", I32, "int32")):
     AT[_n], _w = _arena(_d)
     SCRATCH[_n] = ("sbuf", [128, _w], _t)
 SCRATCH.update({
-    "bag": ("sbuf", [128, BAGW], "float32"), "pl": ("sbuf", [128, 3072], "float32"), "ypb": ("sbuf", [128, V_], "float32"),
-    "nbt": ("sbuf", [128, 3072], "int32"), "xw": ("sbuf", [128, 5696], "bfloat16"), "sf": ("sbuf", [128, 3072], "bfloat16"),
-    "nf": ("sbuf", [128, 3072], "bfloat16"), "ff": ("sbuf", [128, 3072], "bfloat16"), "ct": ("sbuf", [128, 3072], "bfloat16"),
+    "bag": ("sbuf", [128, BAGW], "float32"), "pl": ("sbuf", [128, PLW], "float32"), "ypb": ("sbuf", [128, PLW], "float32"),
+    "nbt": ("sbuf", [128, 3072], "int32"), "xw": ("sbuf", [128, 5728], "bfloat16"), "sf": ("sbuf", [128, 3072], "float32"),
+    "ff": ("sbuf", [128, 3072], "bfloat16"), "ct": ("sbuf", [128, 3072], "bfloat16"),
     "d0": ("sbuf", [128, 1280], "bfloat16"), "gg": ("sbuf", [128, 8192], "bfloat16"), "mm": ("sbuf", [128, 4608], "bfloat16"),
-    "tt": ("sbuf", [128, TW_], "float32"),
+    "tt": ("sbuf", [128, 3 * 1536], "float32"),
 })
 for _k in range(8):
     SCRATCH["p%d" % _k] = ("psum", [128, 512], "float32")
-NDMA = 30
+NDMA = 40
 SEMAPHORES = ["qv", "qs", "qp", "qg", "gin", "sent", "sent0"] + ["arr%d" % k for k in range(3)] + ["dm%d" % k for k in range(NDMA)]
 
 
@@ -65,7 +68,7 @@ def rank_program(g, core, T, topo):
             o = AT[name][k]
             return (name, o + a, o + (tab[k] if b is None else b), st, 0, 1)
         return get
-    f, b_, u, i_ = arena("af", F32), arena("ab", BF), arena("au", U16), arena("ai", I32)
+    f, b_, h_, u, i_ = arena("af", F32), arena("ab", BF), arena("ah", F16), arena("au", U16), arena("ai", I32)
 
     def P(k, a, b, st=1):
         return ("p%d" % k, a, b, st, 0, 1)
@@ -115,8 +118,8 @@ def rank_program(g, core, T, topo):
     def mset(o, c):
         add("v", lambda: g.vector.memset(ap(o), c), o, [])
 
-    def red(o, x):
-        add("v", lambda: g.vector.tensor_reduce(ap(o), ap(x), AxisListType.X, AL.add), o, [x])
+    def red(o, x, op=AL.add):
+        add("v", lambda: g.vector.tensor_reduce(ap(o), ap(x), AxisListType.X, op), o, [x])
 
     def act(o, x, fn=AF.Identity, bias=None, scale=None):
         kw = {}
@@ -138,17 +141,28 @@ def rank_program(g, core, T, topo):
     def asel(o, x, pat, op, base, cm):
         add("g", lambda: g.affine_select(ap(o), ap(x), pat, op, 0.0, base, cm), o, [x])
 
+    def put(o, pat, base, fill):
+        add("g", lambda: g.affine_select(ap(o), ap(o), pat, AL.not_equal, float(fill), base, 1), o, [o])
+
     def dma(o, x):
         add("y", lambda: g.sync.dma_start(ap(o), ap(x)), o, [x], dma=True)
 
     def sub(x, a, b, st=1):
         return (x[0], x[1] + a, x[1] + b, st, x[4], x[5])
 
-    def conv(o, src, Y, n, extra=None):
-        if extra is not None:
-            mm(o, extra[0], extra[1], True, False)
+    def conv(o, src, Y, n, stop=True):
         for r in range(16):
-            mm(o, b_(Y, 16 - r, 144 - r), sub(src, r, n, 16), r == 0 and extra is None, r == 15)
+            mm(o, b_(Y, 16 - r, 144 - r), sub(src, r, n, 16), r == 0, stop and r == 15)
+
+    def quad(o, src, Y, a, n, first=None):
+        if first is not None:
+            mm(o, first[0], first[1], True, False)
+        for r in range(4):
+            mm(o, b_(Y, 16 - r, 144 - r), sub(src, a + r, a + n, 4), r == 0 and first is None, r == 3)
+
+    def fold(o, tab, Y, src, st, sp):
+        for a in range(4):
+            mm(o, tab(Y, 16 - 4 * a, 144 - 4 * a), sub(src, a, 128, 4), st and a == 0, sp and a == 3)
 
     def send(src, dst_of, sem, loc):
         peers = [T.cores[(rank + d) % N] for d in range(1, N)]
@@ -176,31 +190,32 @@ def rank_program(g, core, T, topo):
     ncol = [0]
 
     def column(terms, const=0.0):
-        if len(terms) == 1 and terms[0][1] == 1 and const == 0.0:
-            return f("E", terms[0][0], terms[0][0] + 1)
         o = f("col", ncol[0], ncol[0] + 1); ncol[0] += 1
         prev = const
         for r, w in terms:
-            ts(o, f("E", r, r + 1), float(w), AL.mult, prev, AL.add)
+            act(o, f("E", r, r + 1), scale=float(w), bias=prev)
             prev = o
         return o
 
-    def ymat(name, terms):
-        ts(b_(name, 0, 144, 16), f("G9", 0, 9), column(terms), AL.mult)
+    def ymat(name, w):
+        act(b_(name, 0, 144, 16), f("G9", 0, 9), scale=w)
 
-    def trmat(name, outs):
-        for p, terms in outs.items():
-            ts(b_(name, p, 128, 16), f("G9", 1, 9), column(terms), AL.mult)
+    def trmat(name, p, w):
+        act(b_(name, p, 128, 16), f("G9", 1, 9), scale=w)
+
+    def c_(k):
+        return f("cl", CL[k], CL[k] + 1)
 
     XO = R("xw", SH, SH + V_)
     XS, XN = R("xw", 0, 3072), R("xw", SH, SH + 4096)
-    NBT, SF, NF, PL = R("nbt", 0, 3072), R("sf", 0, 3072), R("nf", 0, 3072), R("pl", 0, 3072)
-    BG, BS = R("bag", 0, DZ + 512), R("bag", 0, BAGW)
-    F, TT = R("ff", 0, 3072), R("tt", 0, TW_)
+    NBT, SF, PL = R("nbt", 0, 3072), R("sf", 0, 3072), R("pl", 0, PLW)
+    BD, BG, BS = R("bag", 0, DZ + 256), R("bag", 0, DZ + 512), R("bag", 0, BAGW)
+    F, YP = R("ff", 0, 3072), R("ypb", 0, PLW)
     HI, LO = f("JVf", 0, 256), f("JVf", 256, 512)
-    cr = ((0, 2), (2, 4), (4, 8), (8, 16))
+    ZERO = R("xw", 0, SH)
     K = {}
 
+    mset(b_("ONE"), 1.0)
     mset(f("one"), 1.0)
     mset(i_("ts"), 0)
     dma(i_("plc"), T.plc[:])
@@ -208,319 +223,431 @@ def rank_program(g, core, T, topo):
     dma(R("ai", AT["ai"]["ts"], AT["ai"]["ts"] + 3, 1, 0, 16), T.th[:])
     dma(R("ai", AT["ai"]["ts"] + 4, AT["ai"]["ts"] + 8, 1, 0, 16), T.sd[:])
     dma(i_("n0"), T.nb[0:128:16, :])
-    dma(R("nbt", SH, SH + V_), T.nb[:])
-    dma(R("xw", SH + 512, SH + V_), T.x[:, 512:V_])
-    act(b_("C512"), f("one"), AF.Silu, scale=512.0)
+    act(b_("CS", 0, 528), b_("ONE"), AF.Silu, scale=65.0)
+    act(b_("CS", 1024, 1040), b_("ONE", 0, 16), scale=65.0)
     iota(i_("pi", 0, 1), [[0, 1]], 0, 1)
-    iota(LO, [[0, 16], [1, 16]])
-    iota(HI, [[1, 16], [0, 16]])
-    mset(R("ab", AT["ab"]["Ys"], AT["ab"]["Yc"]), 0.0)
-    mset(R("xw", 0, SH), 0.0)
+    iota(LO, [[0, 4], [1, 64]])
+    iota(HI, [[64, 4], [0, 64]])
+    mset(ZERO, 0.0)
+    dma(R("nbt", SH, SH + V_), T.nb[:])
+    for k in range(1, 6):
+        dma(R("ff", k * 512, (k + 1) * 512), ZERO)
+    dma(R("xw", SH + 512, SH + V_), T.x[:, 512:V_])
+    mset(R("ab", AT["ab"]["G2"], AT["ab"]["Yt"]), 0.0)
+    for k, nme in enumerate(("Yt", "YJ")):
+        dma(R("ab", AT["ab"][nme], AT["ab"][nme] + 432 - 32 * k), sub(ZERO, 0, 432 - 32 * k))
+    dma(R("ab", AT["ab"]["TR1b"], AT["ab"]["BO"]), sub(ZERO, 0, 256))
     ts(i_("pi", 1, 2), i_("pi", 0, 1), 15, AL.bitwise_and)
-    cp(f("rcol", 0, 1), i_("pi", 1, 2))
+    ts(i_("pi", 2, 3), i_("pi", 0, 1), 3, AL.bitwise_and)
+    cp(f("rcol", 0, 2), i_("pi", 1, 3))
     ts(f("E"), sub(LO, 0, 16), f("rcol", 0, 1), AL.is_equal)
-    ts(f("BK", 0, 12), sub(LO, 0, 12), f("E", 0, 1), AL.mult, 16.0, AL.mult)
+    ts(f("BK", 0, 12), sub(LO, 0, 12), f("E", 0, 1), AL.mult, 256.0, AL.mult)
     ts(f("blk"), LO, 32.0, AL.add, f("E", 1, 2), AL.mult)
-    ts(HI, HI, 32.0, AL.add, f("E", 0, 1), AL.mult)
-    tt(f("blk"), f("blk"), HI, AL.add)
-    for k in range(2, 7):
-        act(R("ypb", (k - 2) * 256, (k - 1) * 256), f("blk"), bias=f("BK", k, k + 1))
-    for k in range(7, 12):
-        ts(R("ypb", (k - 2) * 256, (k - 1) * 256), f("blk"), f("BK", k, k + 1), AL.add)
+    ts(HI, HI, f("E", 0, 1), AL.mult)
     cp(u("plu"), i_("plc"))
-    act(ind(R("bag", 0, DZ), u("plu")), R("ypb", 0, V_), AF.Silu)
+    tt(R("sf", 0, 256), f("blk"), HI, AL.add)
+
+    def sfk(k):
+        ts(R("sf", k * 256, (k + 1) * 256), R("sf", 0, 256), f("BK", k, k + 1), AL.add)
+    for a, e in ((2, 3), (3, 6), (6, 12)):
+        for k in range(a, e):
+            sfk(k)
+        act(ind(R("bag", 0, DZ), u("plu", (a - 2) * 16, (e - 2) * 16)), R("sf", a * 256, e * 256), AF.Silu)
+        if a == 3:
+            mset(R("af", AT["af"]["AD"], AT["af"]["S32"] + 144), 0.0)
+    sfk(1)
     asel(f("G9", 0, 9), f("one", 0, 9), [[-16, 9]], AL.is_ge, 16, 1)
     asel(f("G9", 0, 9), f("G9", 0, 9), [[16, 9]], AL.is_ge, -1, -1)
     asel(b_("BO"), f("one"), [[-16, 8], [0, 16]], AL.is_ge, 0, 1)
     asel(b_("BO"), b_("BO"), [[16, 8], [0, 16]], AL.is_ge, 15, -1)
     ne = send(R("xw", SH, SH + 512), lambda d: R("xw", 3072 + (d - 1) * 512, 3072 + d * 512), "gin", "sent0")
     ext("gin", ne * (N - 1), R("xw", 3072, 4608))
+    put(f("AD"), [[-16, 8], [1000, 8], [0, 2]], 0, 1.0)
+    put(f("A0"), [[-16, 8], [1000, 2], [0, 8]], -1000, 52.0)
+    put(f("AD"), [[-16, 8], [1000, 8], [0, 2]], -1004, 1.0)
+    put(f("A0"), [[-16, 8], [1000, 4], [0, 4]], -1000, 26.0)
+    put(f("AD"), [[-16, 8], [1000, 4], [0, 4]], -1008, 0.5)
+    put(f("A0"), [[-16, 8], [1000, 4], [0, 4]], 0, 13.0)
+    put(f("AD"), [[-16, 8], [1000, 2], [0, 8]], -1012, 0.25)
+    iota(f("JT"), [[1, 256]])
     iota(f("JW"), [[16, 32]])
-    iota(b_("ONE"), [[0, 512]], 1)
-    iota(f("C4", 0, 4), [[V_, 4]])
-    for c, (a, e) in enumerate(cr):
-        iota(f("C25", a, e), [[0, e - a]], V_ * c)
-    for r in range(0, 15, 3):
-        asel(b_("Z", r * 144, (r + 3) * 144), b_("ONE", 0, 432), [[-1, 3], [-16, 9], [-1000, 16]], AL.is_equal, 16 - r, 1)
-        if r == 3:
-            iota(f("JT"), [[1, 256]])
-            iota(R("nbt", 0, SH), [[0, SH]])
-            asel(b_("ID"), f("one"), [[-1, 128]], AL.is_equal, 0, 1)
-    asel(b_("Z", 15 * 144, 16 * 144), b_("ONE", 0, 144), [[-16, 9], [-1000, 16]], AL.is_equal, 1, 1)
-    iota(b_("CS"), [[0, 1040]], 65)
-    iota(R("ab", AT["ab"]["Yc"], AT["ab"]["BO"]), [[0, 720]])
-    iota(R("ab", AT["ab"]["TR1"], AT["ab"]["C75"]), [[0, 512]])
-    iota(R("pl", 0, SH), [[0, SH]])
-    iota(f("R9"), [[0, 32], [1, 9]]); iota(f("R5"), [[0, 32], [1, 5]]); iota(f("R4"), [[0, 32], [1, 4]])
-    iota(b_("SLV", 0, 16), [[0, 16]]); iota(b_("SJ", 0, 16), [[0, 16]])
-    cp(b_("blk"), f("blk"))
-    for k in range(12):
-        ts(R("sf", k * 256, (k + 1) * 256), b_("blk"), f("BK", k, k + 1), AL.add)
-    dma(NF, SF)
-    for k in range(1, 6):
-        dma(R("ff", k * 512, (k + 1) * 512), R("xw", 0, SH))
-    ts(i_("tsh"), i_("ts"), 0x1FF00, AL.bitwise_and)
-    ts(i_("tsl"), i_("ts"), 255, AL.bitwise_and)
-    cp(f("plf"), i_("plc"))
-    cp(b_("th"), i_("tsh")); cp(b_("tl"), i_("tsl"))
-    mm(P(4, 0, 16), b_("BO"), b_("th"), True, False); mm(P(4, 0, 16), b_("BO"), b_("tl"), False, True)
-    ts(i_("a"), i_("n0"), float(SH), AL.add)
-    for c in range(1, 4):
-        ts(b_("ge", (c - 1) * 160, c * 160), f("plf"), float(V_ * c), AL.is_ge)
-    mm(P(5, 0, 480), b_("BO"), b_("ge"), True, True)
-    ts(i_("b"), i_("a"), 4, AL.arith_shift_right)
-    ts(i_("c"), i_("a"), 15, AL.bitwise_and)
-    ts(b_("nh"), i_("b"), 32.0, AL.add); ts(b_("nl"), i_("c"), 32.0, AL.add)
-    dma(R("nf", SH, 3072, 1, 0, 16), b_("nh")); dma(R("nf", SH, 3072, 1, 1, 16), b_("nl"))
-    ts(R("d0", 0, 320), b_("ONE", 0, 320), column([(3, -1), (8, -1)], 1.0), AL.mult)
-    for k in range(1, 4):
-        dma(R("d0", k * 320, (k + 1) * 320), R("d0", 0, 320))
-    for t in range(RO):
-        dma(b_("SEL", t * 336, t * 336 + 64), R("sf", 2048, 2112))
-        dma(b_("SL", t * 1024, t * 1024 + 512), R("sf", 0, 512))
-
-    def place_fields():
-        tt(f("c1"), b_("ge", 0, 160), b_("ge", 160, 320), AL.add)
-        ts(i_("d"), i_("plc"), 0x3FC0, AL.bitwise_and)
-        tt(f("c1"), f("c1"), b_("ge", 320, 480), AL.add)
-        ts(i_("e"), i_("plc"), 63, AL.bitwise_and)
-        ts(f("c2"), f("c1"), float(-V_), AL.mult)
-        cp(b_("fl", 480, 640), i_("d"))
-        tt(i_("a"), f("c2"), f("plf"), AL.add)
-        cp(b_("fl", 640, 800), i_("e"))
-        ts(b_("fl", 0, 160), f("c1"), 32.0, AL.mult)
-        ts(i_("b"), i_("a"), 4, AL.arith_shift_right); ts(i_("c"), i_("a"), 15, AL.bitwise_and)
-        cp(b_("fl", 160, 320), i_("b")); cp(b_("fl", 320, 480), i_("c"))
+    asel(b_("ID"), f("one"), [[-1, 128]], AL.is_equal, 0, 1)
+    iota(R("nbt", 0, SH), [[0, SH]])
 
     def sizes():
-        K["c32"] = column([(0, 32), (2, 32), (3, 32)])
-        ts(f("JW"), f("JW"), f("rcol", 0, 1), AL.add)
-        cp(f("TS"), P(4, 0, 16))
-        mset(f("G4", 0, 1), float(V_)); mset(f("G4", 4, 5), 0.0)
         for c in range(1, 4):
-            red(f("G4", c, c + 1), P(5, (c - 1) * 160, c * 160))
-        mset(f("Q4", 0, 2), float(QS[0])); mset(f("Q4", 2, 3), float(QS[2])); mset(f("Q4", 3, 4), float(QS[3]))
-    weave(place_fields, sizes)
+            ts(b_("fl", (c + 1) * 160, (c + 2) * 160), i_("plc"), float(V_ * c), AL.is_ge, 32.0, AL.mult)
+        for c in range(1, 4):
+            red(f("G4", c - 1, c), b_("fl", (c + 1) * 160, (c + 2) * 160))
+        cp(b_("cnt", 0, 3), f("G4", 0, 3))
+        mm(P(6, 496, 499), b_("BO"), b_("cnt", 0, 3), True, True)
+
+    def seeds():
+        ts(i_("tsh"), i_("ts"), 0x1FF00, AL.bitwise_and)
+        ts(i_("tsl"), i_("ts"), 255, AL.bitwise_and)
+        cp(b_("th"), i_("tsh")); cp(b_("tl"), i_("tsl"))
+        mm(P(6, 480, 496), b_("BO"), b_("th"), True, False); mm(P(6, 480, 496), b_("BO"), b_("tl"), False, True)
+
+    def columns():
+        for k, v in enumerate((2.0, 4.0, 8.0)):
+            ts(f("G3", k, k + 1), f("rcol", 0, 1), v, AL.is_ge)
+        ts(c_("c"), f("rcol", 0, 1), f("rcol", 1, 2), AL.subtract, 0.25, AL.mult)
+        ts(c_("cD"), f("G3", 0, 1), f("G3", 1, 2), AL.add, f("G3", 2, 3), AL.add)
+        ts(c_("km"), f("G3", 2, 3), 2.0, AL.mult, f("G3", 1, 2), AL.add)
+        ts(f("EQ", 0, 4), sub(LO, 0, 4), c_("c"), AL.is_equal)
+        ts(f("EQ", 4, 8), sub(LO, 0, 4), c_("cD"), AL.is_equal)
+        ts(c_("p0"), c_("km"), f("G3", 0, 1), AL.add, 2.0, AL.mult)
+        ts(c_("k"), c_("km"), 1.0, AL.add)
+        tt(f("Aa", 0, 3), f("EQ", 1, 4), f("EQ", 0, 3), AL.subtract)
+        ts(c_("c25"), c_("cD"), float(V_), AL.mult)
+        ts(c_("pp"), c_("p0"), -1.0, AL.mult, f("rcol", 0, 1), AL.add)
+        ts(c_("iv0"), c_("p0"), 16.0, AL.mult, float(DZ), AL.add)
+        ts(c_("pp"), c_("pp"), 16.0, AL.mult)
+        ts(c_("ivc"), c_("iv0"), c_("c25"), AL.subtract)
+        ts(f("JH"), sub(LO, 0, 16), c_("pp"), AL.add, 128.0, AL.mult)
+    weave(sizes, seeds, columns)
+
+    def first_sizes():
+        tt(f("t4", 0, 3), P(6, 496, 499), f("Aa", 0, 3), AL.mult)
+        red(c_("t"), f("t4", 0, 3))
+        ts(c_("t"), c_("t"), 1.0 / 32, AL.mult)
+        ts(c_("n"), f("EQ", 0, 1), float(V_), AL.mult, c_("t"), AL.add)
+
+    def first_seeds():
+        cp(f("TS"), P(6, 480, 496))
+        tt(f("t4", 4, 8), f("TS", 4, 8), f("EQ", 4, 8), AL.mult)
+        red(c_("sd"), f("t4", 4, 8))
+        ts(c_("sd0"), c_("sd"), c_("k"), AL.mult)
+
+    def first_fields():
+        ts(i_("b"), i_("n0"), 0xFC0, AL.bitwise_and)
+        ts(i_("c"), i_("n0"), 63, AL.bitwise_and)
+        ts(f("nh"), i_("b"), float(SH), AL.add); ts(f("nl"), i_("c"), 32.0, AL.add)
+    weave(first_sizes, first_seeds, first_fields)
+
+    def draw_sizes():
+        mm(P(5, 496, 497), f("AD"), c_("n"), True, True)
+        mm(P(5, 497, 498), f("A0"), c_("n"), True, True)
+
+    def draw_a(t):
+        ts(i_("xi", 0, 1), P(5, 497, 498), c_("sd%d" % t), AL.add)
+        ts(c_("npp"), P(5, 496, 497), 32.0, AL.max)
+        ts(i_("bi", 0, 1), i_("xi", 0, 1), 127, AL.bitwise_and)
+        ts(c_("inv"), P(5, 496, 497), 32.0, AL.is_lt, c_("ivc"), AL.mult)
+        cp(c_("bk"), i_("bi", 0, 1))
+
+    def draw_b():
+        ts(i_("pr"), f("JH"), c_("bk"), AL.add, c_("npp"), AL.mult)
+        ts(i_("sh"), i_("pr"), 12, AL.arith_shift_right)
+        ts(u("DP"), i_("sh"), c_("inv"), AL.add, c_("c25"), AL.add)
+
+    def final(a, e):
+        act(sub(YP, a, e), sub(PL, a, e), bias=12582912.0)
+        act(sub(YP, a, e), sub(YP, a, e), bias=-12582912.0 - 33.0)
+
+    def leavers():
+        tt(f("tg"), P(0, 288, 320), f("dP"), AL.min)
+        ts(u("POF"), f("tg"), 16384.0 - 32.0, AL.add)
 
     def piece(r):
-        return P((0, 2, 3, 6, 7)[r // 3], (r % 3) * 160, (r % 3 + 1) * 160) if r < 15 else P(1, 256, 416)
+        return P((0, 2, 7, 5, 6)[r // 3], (r % 3) * 160, (r % 3 + 1) * 160) if r < 15 else P(1, 256, 416)
 
     def spread(r0, r1):
         for r in range(r0, r1):
-            for k, row in enumerate((1, 2, 3, 0, 0)):
+            for k, row in enumerate((2, 3, 7, 9, 11)):
                 mm(piece(r), b_("Z", r * 144 + 16 - row, r * 144 + 144 - row), b_("fl", k * 160, (k + 1) * 160), k == 0, k == 4)
 
     def fetch(r0, r1):
         for r in range(r0, r1):
-            act(R("pl", SH + r, 3072, 16), piece(r), bias=K["c32"])
-    spread(0, 6)
-    fetch(0, 6)
-    tt(f("N4", 0, 4), f("G4", 0, 4), f("G4", 1, 5), AL.subtract)
-    for c, (a, e) in enumerate(cr):
-        ts(f("JH", a, e), f("JW", a, e), float(16 * a), AL.subtract, float(4096 // QS[c]), AL.mult)
-        ts(f("SDE", a, e), f("one", a, e), f("TS", 4 + c, 5 + c), AL.mult)
-    ts(f("DZJ"), f("JW", 0, 16), float(DZ), AL.add)
+            act(R("pl", SH + r, 3072, 16), piece(r), bias=K["c33"])
 
-    def draw_first(t):
-        ts(f("s13", 0, 1), f("N4", 0, 1), 13.0, AL.mult, float(41 * t), AL.add)
-        tt(f("inv", 0, 4), f("N4", 0, 4), f("Q4", 0, 4), AL.is_lt)
-        ts(i_("xi"), f("SDE"), f("s13", 0, 1), AL.add)
-        for c, (a, e) in enumerate(cr):
-            ts(f("iv", a, e), f("DZJ", a, e), f("inv", c, c + 1), AL.mult)
-        for a, e, m in ((0, 4, 127), (4, 8, 63), (8, 16, 31)):
-            ts(i_("bi", a, e), i_("xi", a, e), m, AL.bitwise_and)
+    def tables_z():
+        cp(b_("G2", 0, 144, 16), f("G9", 0, 9)); cp(b_("G2", 1, 144, 16), f("G9", 0, 9))
+        ts(i_("d"), i_("plc"), 0x3FC0, AL.bitwise_and)
+        ts(i_("e"), i_("plc"), 63, AL.bitwise_and)
+        for r in range(ZG):
+            asel(b_("Z", r * 144, (r + 1) * 144), b_("G2"), [[-16, 9], [0, 16]], AL.is_equal, 16 - r, 1)
+        cp(b_("fl", 0, 160), i_("d"))
+        cp(b_("fl", 160, 320), i_("e"))
 
-    def draw_second():
-        tt(f("jb"), i_("bi"), f("JH"), AL.add)
-        for c, (a, e) in enumerate(cr):
-            ts(i_("pr", a, e), f("jb", a, e), f("N4", c, c + 1), AL.mult)
-        ts(i_("sh"), i_("pr"), 12, AL.arith_shift_right)
-        tt(f("pc"), i_("sh"), f("C25"), AL.add)
-        tt(f("mx"), f("pc"), f("iv"), AL.max)
-        cp(u("DP"), f("mx"))
+    def tables_z2():
+        for r in range(ZG, 16):
+            act(b_("Z", r * 144, (r + 1) * 144), b_("G2"), scale=f("E", r, r + 1))
 
     def tables_draw():
-        ymat("Ys", [(0, 16), (1, 1)])
-        ymat("Yj", [(4, 1)]); ymat("Yr", [(0, 1), (1, 1000)])
-        K["k64"] = column([(1, 64)])
-        ts(f("c65"), f("JW", 0, 16), 65.0, AL.add)
+        ts(c_("s01"), f("rcol", 0, 1), 2.0, AL.is_lt)
+        ts(c_("s03"), f("rcol", 0, 1), 4.0, AL.is_lt)
+        cp(R("bag", DZ, DZ + 256), R("sf", 0, 256))
+        ts(b_("Ys", 0, 144, 16), f("G9", 0, 9), c_("s03"), AL.mult)
+        ts(c_("s23"), c_("s03"), c_("s01"), AL.subtract)
         ts(f("JT"), f("JT"), f("E", 4, 5), AL.mult)
-        cp(R("bag", DZ, DZ + 512), R("sf", 0, 512))
+        cp(b_("SEL", 0, 64), R("sf", 2048, 2112))
+        act(b_("SFb"), R("sf", 0, 512))
+        act(R("bag", DZ + 256, DZ + 512), R("sf", 256, 512))
+        dma(R("sf", SH, 3072, 1, 2, 16), f("nh")); dma(R("sf", SH, 3072, 1, 3, 16), f("nl"))
+        for r in range(2):
+            dma(R("sf", 0, SH, 1, 2 + r, 16), R("bag", DZ, DZ + SH, 1, r, 16))
+        for t in range(RO):
+            dma(b_("SL", t * 1024, t * 1024 + 512), b_("SFb"))
+            if t:
+                dma(b_("SEL", t * 336, t * 336 + 64), b_("SEL", 0, 64))
 
     def tables_move():
-        ts(b_("ID16"), b_("ID"), 0.0625, AL.mult); ts(b_("IDm"), b_("ID"), -1.0, AL.mult)
+        ts(f("JW"), f("JW"), f("rcol", 0, 1), AL.add)
+        K["k64"] = column([(1, 64)])
+        ts(c_("t"), f("E", 1, 2), 999.0, AL.mult, c_("s03"), AL.add)
+        ts(f("c65"), f("JW", 0, 16), 65.0, AL.add)
+        ts(b_("Yr", 0, 144, 16), f("G9", 0, 9), c_("t"), AL.mult)
+        act(b_("VD"), b_("ONE", 0, 256), scale=c_("s01"))
+        act(b_("ID16"), b_("ID"), scale=0.0625); act(b_("IDm"), b_("ID"), scale=-1.0)
         mset(b_("C75"), -7.5)
-        ts(b_("VN"), b_("ONE", 0, 256), f("E", 2, 3), AL.mult)
-        ts(b_("VD"), b_("ONE", 0, 256), column([(0, 1), (1, 1), (3, 1)]), AL.mult)
+        act(R("d0", 0, 320), b_("ONE", 0, 320), scale=column([(3, -1)], 1.0))
+        act(b_("VN"), b_("ONE", 0, 256), scale=c_("s23"))
+        for k in range(1, 4):
+            dma(R("d0", k * 320, (k + 1) * 320), R("d0", 0, 320))
 
-    def tables_sort2():
-        ts(R("ct", 0, SH), b_("ONE"), f("E", 3, 4), AL.mult, 2.0, AL.mult)
-        ymat("Yk", [(0, 1), (2, 1), (3, 2048)])
-        mset(f("cD", 0, 16), -2048.0); mset(f("cD", 16, 32), 0.0)
-        ts(f("c513"), f("JW"), 513.0, AL.add)
+    def tables_move2():
+        ts(c_("y"), c_("s03"), 1.0 / 8192, AL.mult, f("E", 4, 5), AL.add)
+        mset(f("msg"), 0.0)
+        ts(b_("Yj", 0, 144, 16), f("G9", 0, 9), c_("y"), AL.mult)
+        for d in range(N - 1):
+            ts(u("GO", 5 * d + 4, 5 * d + 5), f("rcol", 0, 1), 1600.0 + 512 * d, AL.add)
+
+    def tables_sort():
+        def one():
+            K["c33"] = column([(3, 33), (4, 33), (5, 32)])
+
+        def two():
+            ymat("Yk", column([(3, 2048), (0, 1), (2, 1)]))
+
+        def three():
+            act(R("ct", 0, SH), b_("ONE", 0, 512), scale=column([(3, 2)]))
+            act(c_("c33"), c_("c"), scale=float(V_), bias=33.0)
+            act(f("c513"), f("JW"), bias=513.0)
+        weave(one, two, three)
+        iota(f("cD"), [[-2048, 2], [0, 16]])
+
+    def thresholds():
+        red(f("T3", 0, 1), f("TS", 0, 3), AL.min)
+        red(f("T3", 2, 3), f("TS", 0, 3), AL.max)
+        red(c_("t"), f("TS", 0, 3))
+        mset(f("TR"), 0.0)
+        ts(f("T3", 1, 2), c_("t"), f("T3", 0, 1), AL.subtract, f("T3", 2, 3), AL.subtract)
+        mset(f("TR", 14, 15), 1e9)
+        for a in (2, 5, 7):
+            cp(f("TR", a, a + 9, 4), f("T3", 0, 3))
+
+    def thresholds2():
+        tt(f("TR2"), f("TR"), f("E"), AL.mult)
+        red(c_("t"), f("TR2"))
+        ts(c_("thc"), c_("t"), float(BIG), AL.add)
+        for t in range(1, RO):
+            ts(c_("sd%d" % t), c_("sd"), float(41 * t), AL.add, c_("k"), AL.mult)
+
+    def tables_q():
+        cp(h_("ID"), b_("ID"))
+        ts(h_("nd"), f("IQ"), -1.0, AL.mult, -1024.0, AL.add)
+        ts(h_("dW"), f("JW"), 1024.0, AL.add); cp(h_("JW"), f("JW")); ts(h_("nJ"), f("JW"), -1.0, AL.mult)
+
+    def tables_g1():
+        iota(f("IQ"), [[4, 128]])
+        iota(R("pl", 0, SH), [[0, SH]])
+        for row in (2, 4):
+            put(b_("YP"), [[-16, 9], [0, 4], [1000, 4]], 16 - row, 1.0)
+        put(b_("PEN"), [[-16, 8], [-2, 4], [0, 4]], -5, BIG / 32)
+        put(b_("PEN"), [[-16, 8], [-2, 4], [0, 4]], -7, -BIG / 32)
+        asel(b_("PEN"), b_("PEN"), [[0, 32], [1, 4]], AL.not_equal, -3, 0)
+        put(b_("PEN"), [[-16, 8], [0, 4], [1000, 4]], -3005, BIG / 32)
+
+    def tables_g2():
+        q = [[-16, 9], [-4, 4], [1000, 4]]
+        for row, w in ((0, 1.0), (1, -1.0), (2, 1.0)):
+            put(b_("YL"), q, 16 - row, w)
+        put(b_("YJ"), q, 16 - 7, -1.0)
+        asel(b_("YJ"), b_("YJ"), [[0, 9], [1, 4], [0, 4]], AL.not_equal, -3, 0)
+        for row, w in ((3, 1.0), (1, -1.0), (2, 1.0)):
+            put(b_("YJ"), q, 16 - row, w)
+        asel(b_("Ale"), b_("BO"), [[16, 8], [4, 4], [0, 4]], AL.is_ge, 3, -1)
+        asel(b_("Alt"), b_("BO"), [[16, 8], [4, 4], [0, 4]], AL.is_ge, -1, -1)
+        asel(b_("Aeq"), b_("Ale"), [[-16, 8], [-4, 4], [0, 4]], AL.is_ge, 0, 1)
+        asel(b_("MB"), b_("BOm"), [[-1, 128]], AL.is_gt, 0, 1)
+        asel(b_("MB"), b_("MB"), [[16, 8], [4, 4], [0, 4]], AL.is_ge, 3, -1)
+        put(b_("MB"), [[-1, 128]], 0, 16384.0)
+        for c in range(4):
+            put(f("S32"), [[-16, 9], [1000, 4], [-1, 4]], 16 - 4 * c, 1.0)
+
+    def tables_s1():
+        for nme, w in (("BOm", -1.0), ("BO2", 2.0), ("BOm16", -16.0)):
+            act(b_(nme), b_("BO"), scale=w)
 
     def tables_a():
-        K["pus"] = column([(1, 1), (2, 1), (3, 1)]); K["m32"] = column([(8, 32)])
-        ymat("Yc", [(1, 1.0 / 32)]); ymat("Yp", [(2, 16), (3, 1)])
+        f2 = column([(14, 1), (15, 1)])
+        trmat("TR3", 2, f("E", 0, 1)); trmat("TR3", 4, f("E", 1, 2))
+        hd = column([(2, DZ + 576)])
+        act(R("tt", 0, 512), b_("SFb"), bias=f2)
+        act(b_("d0u"), b_("ONE", 0, 512), scale=f("E", 14, 15))
+        mm(P(7, 0, 512), b_("TR3"), b_("SFb"), True, True)
+        act(R("tt", 512, 1024), P(7, 0, 512), bias=hd)
+        for t in range(1, RO):
+            dma(R("tt", t * 1536, t * 1536 + 1024), R("tt", 0, 1024))
 
     def tables_b():
-        K["thc"] = column([(4, -1e9), (5, -1e9), (6, -1e9)], 1e9)
-        for k in range(3):
-            ts(K["thc"], f("E", 4 + k, 5 + k), f("TS", k, k + 1), AL.mult, K["thc"], AL.add)
+        K["yu"] = column([(15, -544), (14, 1)], c_("s01"))
+        K["s24"] = column([(2, 1), (4, 1)])
+        ymat("Yt", K["s24"])
+        iota(b_("cB"), [[0, 128]], -16384)
+        act(c_("sb"), c_("c"), scale=float(V_), bias=-16384.0)
+        act(f("dB"), f("JW"), bias=float(DZ + 576 - 16383))
+        act(f("dP"), f("JW"), bias=float(3072 + 32 - 16384))
 
     def tables_c():
-        trmat("TR3", {2: [(0, 1)], 3: [(1, 1)]})
-        K["c128"] = column([(1, 128)]); K["m512"] = column([(0, -512)]); K["s01"] = column([(0, 1), (1, 1)])
-        for nme in ("R9", "R5", "R4"):
-            ts(f(nme), f(nme), 1.0, AL.min)
+        mset(h_("Yu"), 0.0)
+        cp(h_("S"), f("S32"))
+        ts(h_("Yu", 0, 144, 16), f("G9", 0, 9), K["yu"], AL.mult)
+        act(b_("SB"), f("S32"), scale=c_("sb"))
+        act(b_("SG"), f("S32"), scale=-16384.0)
 
     def tables_d():
-        ymat("Yb", [(4, 1), (5, 1), (6, 1)]); ymat("Ym", [(6, 1), (7, 1), (8, 64)])
+        act(f("E32"), f("E"), scale=32.0)
+        for k in range(4):
+            trmat("TR1b", 5 + 2 * k, f("E32", 4 * k + 3, 4 * k + 4))
+        w = column([(7, V_), (11, V_), (15, V_)])
+        for p in (2, 3):
+            trmat("TR1b", p, w)
 
     def tables_e():
-        ymat("Yt", [(1, 80), (2, 16), (3, 1)])
-        trmat("TR1", {0: [(0, 16), (1, 1)], 2: [(0, 1)], 3: [(1, 1)]})
+        act(b_("TR2"), b_("ID"))
+        trmat("TR1", 2, f("E", 0, 1)); trmat("TR1", 3, c_("s01")); trmat("TR1", 4, f("E", 1, 2))
+        trmat("TR2", 3, K["s24"])
 
-    def tables_f():
-        trmat("TR1b", {0: [(4, V_), (5, V_), (6, V_)], 1: [(4, 32), (5, 32), (6, 32)]})
-
-    def tables_g():
-        trmat("TR2", {0: [(1, 80), (2, 16), (3, 1)], 1: [(1, 1)], 2: [(2, 1)], 3: [(3, 1)]})
-
-    def holes_table():
-        act(R("tt", 0, 256), b_("ONE", 0, 256), scale=f("E", 6, 7)); act(R("tt", 256, 512), b_("ONE", 0, 256), scale=f("E", 7, 8))
-        for k, a in ((3, 512), (7, 1024)):
-            mm(P(k, 0, 512), b_("TR3"), R("sf", a, a + 512), True, True)
-            act(R("tt", a, a + 512), P(k, 0, 512), bias=K["c128"])
-
-    def joins_positions():
-        ts(f("n25"), P(4, 0, 32), float(V_), AL.mult)
-        tt(f("tb"), P(5, 32, 64), f("pos"), AL.add)
-        tt(f("td"), f("Z4o", 3, 128, 4), f("n25"), AL.subtract)
-        tt(f("te"), f("td"), f("tb"), AL.max)
-        cp(u("PN"), f("te"))
-
-    def stayers_sites():
-        ts(f("m4"), P(6, 0, 32), 2040.0, AL.is_ge, -4096.0, AL.mult)
-        tt(f("tg"), P(7, 0, 32), f("m4"), AL.add)
-        tt(f("th"), f("tg"), f("J544"), AL.max)
-        ts(u("PLO"), f("th"), -544.0, AL.add)
-
-    def touched_update():
-        mm(P(1, 0, 512), b_("TR1b"), b_("B"), True, False)
-        mm(P(1, 0, 512), b_("TR1"), b_("JV"), False, True)
-        act(f("JVf"), P(1, 0, 512), bias=K["m512"])
-        act(ind(PL, u("UW")), f("JVf"), AF.Silu)
-
-    weave(lambda: (draw_first(0), draw_second()), tables_draw)
+    draw_sizes()
+    weave(lambda: (draw_a(0), draw_b()), tables_draw, tables_z)
     for t in range(RO):
         last = t == RO - 1
         SEL, SL = b_("SEL", t * 336, (t + 1) * 336), b_("SL", t * 1024, (t + 1) * 1024)
+        TT = R("tt", t * 1536, (t + 1) * 1536)
         DW, N0W, DF, N0F = u("U0", 0, 16), u("U0", 16, 32), b_("UF", 0, 256), b_("UF", 256, 512)
-        msg = f("msg", t * 80, t * 80 + 68)
-        tt(DF, ind(BG, u("DP")), f("JT"), AL.add)
-        conv(P(4, 0, 16), DF, "Ys", 256)
+        msg = f("msg", t * 80, t * 80 + 80)
+        tt(DF, ind(BD, u("DP")), f("JT"), AL.add)
+        conv(P(3, 0, 16), DF, "Ys", 256)
         if t == 0:
+            spread(0, SPR[0])
             tables_move()
-        elif t == 1:
-            weave(stayers_sites, tables_g)
         else:
-            stayers_sites()
-        ts(DW, P(4, 0, 16), -544.0, AL.add)
-        cp(u("NBD"), ind(NBT, DW))
-        cp(N0F, ind(NF, DW))
-        conv(P(5, 0, 16), N0F, "Ys", 256)
-        if t == 0:
-            spread(6, 11)
-        ts(u("DWc"), P(4, 0, 16), -544.0, AL.add, 1024.0, AL.min)
-        ts(b_("XM"), ind(XS, DW), -192.0, AL.add)
-        for k in range(4):
-            e = (k + 1) * 64 - (MV if k == 3 else 0)
-            act(R("gg", k * 1024, e * 16), ind(XN, u("NBD", k * 64, e)))
+            leavers()
+        ts(DW, P(3, 0, 16), -32.0, AL.add)
+        ts(u("DWc"), P(3, 0, 16), -32.0, AL.add, 1024.0, AL.min)
+        cp(u("NBD", 0, 64), ind(NBT, sub(DW, 0, 4)))
+        cp(u("NBD", 64, 256), ind(NBT, sub(DW, 4, 16)))
+        act(b_("XM"), ind(XS, DW), bias=-192.0)
+        for a, e in MOVE_S:
+            act(R("gg", a * 16, e * 16), ind(XN, u("NBD", a, e)))
 
-        def move_sum(k):
-            o = P(1, k * 64, (k + 1) * 64)
-            mm(o, b_("IDm"), b_("XM", k * 64, (k + 1) * 64), True, False)
-            mm(o, b_("ID16"), b_("C75"), False, False)
+        def move_sum(a, e):
+            o = P(1, a, e)
+            mm(o, b_("IDm"), b_("XM", a, e), True, False)
+            mm(o, b_("ID16"), b_("C75", 0, e - a), False, False)
             for j in range(16):
-                mm(o, b_("ID16"), R("gg", k * 1024 + j, (k + 1) * 1024, 16), False, j == 15)
-        ts(N0W, P(5, 0, 16), -544.0, AL.add)
-        cp(ind(F, N0W), b_("VN"))
+                mm(o, b_("ID16"), R("gg", a * 16 + j, e * 16, 16), False, j == 15)
         cp(ind(F, DW), b_("VD"))
-        move_sum(0)
+        ts(N0F, ind(SF, DW), c_("s23"), AL.mult)
         scan(b_("CS", 512, 1024), sub(F, 512, 1024), b_("CS", 0, 512), 0.0, AL.add, AL.min)
+        move_sum(*MOVE_S[0])
+        if t == 0:
+            tables_move2()
         ts(b_("RS"), ind(b_("CS"), u("DWc")), K["k64"], AL.subtract, 0.0, AL.max)
-        move_sum(1)
-        conv(P(4, 0, 16), b_("RS"), "Yr", 256)
-        scan(R("ct", SH, SH + 1280), R("d0", 0, 1280), sub(F, SH, SH + 1280), 0.0, AL.mult, AL.add)
-        tt(f("t16"), P(4, 0, 16), f("c65"), AL.min)
+        conv(P(4, 0, 32), R("ab", AT["ab"]["UF"] + 256, AT["ab"]["UF"] + 768), "Yr", 512)
+        a, e = MOVE_V[0]
+        cp(R("gg", a * 16, e * 16), ind(XN, u("NBD", a, e)))
+        tt(f("t16"), P(4, 16, 32), f("c65"), AL.min)
+        ts(N0W, P(4, 0, 16), -32.0, AL.add)
         ts(u("SW"), f("t16"), -1.0, AL.add)
         cp(ind(SEL, u("SW")), DF)
-        cp(R("gg", (256 - MV) * 16, 4096), ind(XN, u("NBD", 256 - MV, 256)))
-        move_sum(2)
-        conv(P(5, 0, 4), sub(SEL, 0, 64), "Yj", 64)
-        move_sum(3)
-        conv(P(5, 4, 8), sub(SEL, 0, 64), "Ys", 64)
-        scan(R("ct", SH + 1280, 3072), R("d0", 0, 1280), sub(F, SH + 1280, 3072), R("ct", SH + 1279, SH + 1280), AL.mult, AL.add)
+        move_sum(*MOVE_S[1])
+        conv(P(3, 64, 68), sub(SEL, 0, 64), "Yj", 64)
+        for a, e in MOVE_V[1:]:
+            cp(R("gg", a * 16, e * 16), ind(XN, u("NBD", a, e)))
         if t == 0:
-            tables_sort2()
-        act(b_("RK"), ind(R("ct", 0, 3072), u("U0")))
-        cp(u("JWu", 0, 4), P(5, 0, 4))
-        ts(sub(msg, 64, 68), P(5, 4, 8), -544.0 - SH, AL.add)
-        ts(b_("DL"), P(1, 0, 256), 189.0, AL.max, 195.0, AL.min)
+            tables_sort()
+        for a, e in SUMS:
+            move_sum(a, e)
+        cp(u("JWu", 0, 4), P(3, 64, 68))
+        cp(ind(F, N0W), b_("VN"))
+        ts(f("t16", 0, 4), u("JWu", 0, 4), -1.0, AL.mult, (-32.0 - SH) / 8192, AL.add)
         cp(b_("XL"), ind(b_("XM"), u("JWu", 0, 4)))
+        tt(sub(msg, 64, 68), P(3, 64, 68), f("t16", 0, 4), AL.add)
+        ts(b_("DL"), P(1, 0, 256), 189.0, AL.max, 195.0, AL.min)
         tt(sub(msg, 0, 64), ind(b_("DL"), u("JWu", 0, 4)), b_("XL"), AL.add)
-        ne = send(msg, lambda d, t=t: f("land", (3 * t + d - 1) * 80, (3 * t + d - 1) * 80 + 68), "arr%d" % t, "sent")
-        conv(P(4, 0, 32), b_("RK"), "Yk", 512)
+        ne = send(msg, lambda d, t=t: f("land", (3 * t + d - 1) * 80, (3 * t + d) * 80), "arr%d" % t, "sent")
         if t > 0:
-            mm(P(2, 0, 512), b_("TR2"), b_("TG"), True, True)
-            act(f("JVf"), P(2, 0, 512), bias=K["m512"])
-            act(ind(PL, u("PLO")), f("JVf"), AF.Silu)
+            act(f("JVf"), P(6, 0, 512))
+            act(ind(PL, u("POF")), f("JVf"), AF.Silu)
         else:
-            spread(11, 16)
-            fetch(6, 16)
+            tables_g1()
+            spread(SPR[0], SPR[1])
+            fetch(0, SPR[0])
+            tables_z2()
+            fetch(SPR[0], SPR[1])
+        scan(R("ct", SH, SH + 1280), R("d0", 0, 1280), sub(F, SH, SH + 1280), 0.0, AL.mult, AL.add)
+        scan(R("ct", SH + 1280, 3072), R("d0", 0, 1280), sub(F, SH + 1280, 3072), R("ct", SH + 1279, SH + 1280), AL.mult, AL.add)
+        act(b_("RK", 0, 256), ind(R("ct", 0, 3072), DW))
+        cp(b_("RK", 256, 512), ind(R("ct", 0, 3072), N0W))
+        conv(P(3, 32, 64), b_("RK"), "Yk", 512)
+        if t == 0:
+            weave(tables_s1, tables_b)
+            act(f("IQ"), f("IQ"), bias=f("rcol", 1, 2))
+            tables_a()
+            spread(SPR[1], 16)
+            fetch(SPR[1], 16)
             ext("sent0", ne, R("xw", SH, SH + 512))
-            weave(tables_a, tables_b)
-        tt(f("t32"), P(4, 0, 32), f("cD"), AL.add)
-        tt(f("t32b"), f("t32"), f("c513"), AL.min)
-        ts(u("RW"), f("t32b"), -1.0, AL.add)
-        cp(ind(SL, u("RW")), b_("UF"))
-        conv(P(5, 0, 32), sub(SL, 0, 512), "Ys", 512)
         tt(ind(XS, DW), b_("DL"), b_("XM"), AL.add)
         if last:
             dma(T.yx[:], XO)
-        ts(u("UW"), P(5, 0, 32), -544.0, AL.add)
-        act(b_("XU"), ind(XS, u("UW")))
-        ts(b_("PEN"), P(5, 0, 32), 544.0 + SH, AL.is_lt, 8.0, AL.mult)
-        cp(u("NBU", 0, 256), ind(NBT, u("UW", 0, 16)))
         if t == 0:
-            for nme, w in (("BOm", -1.0), ("BO2", 2.0), ("BOm16", -16.0)):
-                act(b_(nme), b_("BO"), scale=w)
-            asel(b_("NUP"), b_("BOm"), [[-1, 128]], AL.is_gt, 0, 1)
+            thresholds()
+        tt(f("t32"), P(3, 32, 64), f("cD"), AL.add)
+        ts(c_("NP"), c_("n"), c_("c33"), AL.add)
+        tt(f("t32b"), f("t32"), f("c513"), AL.min)
+        ts(c_("nNP"), c_("n"), -1.0, AL.mult, c_("c33"), AL.subtract)
+        ts(u("RW"), f("t32b"), -1.0, AL.add)
+        ts(c_("fn"), c_("n"), -1.0, AL.mult, float(V_), AL.add)
+        if last:
+            final(SH, 2304)
+        cp(ind(SL, u("RW")), b_("UF"))
+        conv(P(4, 32, 64), sub(SL, 0, 512), "Ys", 512)
+        if t == 0:
+            weave(thresholds2, tables_q)
+            tables_g2()
         if not last:
             iota(R("ff", SH, 3072), [[0, V_]])
-        mm(P(0, 0, 512), b_("ID"), b_("XU"), True, True)
-        act(b_("PU"), ind(PL, u("UW")), bias=K["m32"], scale=K["pus"])
-        conv(P(6, 0, 32), b_("PU"), "Yc", 512, (b_("ID"), b_("PEN")))
-        conv(P(6, 32, 64), b_("PU"), "Yp", 512)
+        ts(u("UW"), P(4, 32, 64), -32.0, AL.add)
+        act(b_("XU"), ind(XS, u("UW")))
+        for a, e in ((0, 256), (256, 512)):
+            cp(u("NBU", a, e), ind(NBT, u("UW", a // 16, e // 16)))
+        act(b_("PU"), ind(PL, u("UW")))
         ext("arr%d" % t, ne * (N - 1), f("land", 3 * t * 80, 3 * (t + 1) * 80))
         for d in range(1, N):
             o = (3 * t + d - 1) * 80
-            cp(u("GO", 4 * (d - 1), 4 * d), f("land", o + 64, o + 68))
-        for d in range(1, N):
-            o = (3 * t + d - 1) * 80
-            cp(ind(R("xw", 3072 + (d - 1) * 512, 3072 + (d - 1) * 512 + 1600), u("GO", 4 * (d - 1), 4 * d)), f("land", o, o + 64))
-        cp(u("NBU", 256, 512), ind(NBT, u("UW", 16, 32)))
+            ts(u("GO", 5 * (d - 1), 5 * d - 1), f("land", o + 64, o + 68), 8192.0, AL.mult, 512.0 * (d - 1), AL.add)
+        cp(ind(R("xw", 3072, 5728), u("GO", 0, 15)), f("land", 3 * t * 80, 3 * (t + 1) * 80))
+        mm(P(0, 0, 512), b_("ID"), b_("XU"), True, True)
         at = 0
-        for n, e in CHUNKS:
-            o, w = R("gg", at * 16, (at + n) * 16), ind(XN, u("NBU", at, at + n))
-            if e == "v":
-                cp(o, w)
-            else:
-                act(o, w)
-            at += n
+        for ci, (ns, nv) in enumerate(CHUNKS):
+            if ci == 0:
+                cp(R("gg", 0, nv * 16), ind(XN, u("NBU", 0, nv)))
+            if ns:
+                act(R("gg", at * 16, (at + ns) * 16), ind(XN, u("NBU", at, at + ns)))
+            at += ns + nv
+
+        def classes(ci, a, n):
+            ts(b_("B", a, a + n), P(1 + ci % 2, 0, n), c_("thc"), AL.is_ge)
+            quad(P(3, 256 + a // 4, 256 + (a + n) // 4), b_("B"), "YL", a, n)
+            quad(P(4, 256 + a // 4, 256 + (a + n) // 4), b_("B"), "YJ", a, n)
         at = 0
-        for ci, (n, e) in enumerate(CHUNKS):
+        for ci, (ns, nv) in enumerate(CHUNKS):
+            n = ns + nv
+            if ci and nv:
+                cp(R("gg", (at + ns) * 16, (at + n) * 16), ind(XN, u("NBU", at + ns, at + n)))
             o = P(1 + ci % 2, 0, n)
             mo = ci % 2 * 2304
             mm(o, b_("BOm16"), b_("XU", at, at + n), True, False)
@@ -528,125 +655,105 @@ def rank_program(g, core, T, topo):
                 mm(o, b_("BOm"), R("gg", at * 16 + k, (at + n) * 16, 16), False, False)
             for k in range(16):
                 tt(R("mm", mo + k * n, mo + (k + 1) * n), R("gg", at * 16 + k, (at + n) * 16, 16), P(0, at, at + n), AL.max)
-                mm(o, b_("BO2"), R("mm", mo + k * n, mo + (k + 1) * n), False, k == 15)
-            if ci > 0:
-                ts(b_("B", at - pn, at), P(1 + (ci - 1) % 2, 0, pn), K["thc"], AL.is_ge)
+                mm(o, b_("BO2"), R("mm", mo + k * n, mo + (k + 1) * n), False, False)
+            mm(o, b_("PEN"), b_("PU", at, at + n), False, True)
             if ci == 1:
-                ts(f("N4p", 0, 4), f("N4", 0, 4), 544.0, AL.add)
-                tt(f("N4c", 0, 4), f("N4", 0, 4), f("C4", 0, 4), AL.add)
-                for c in range(4):
-                    ts(b_("OH", 32 * c, 32 * c + 32), P(6, 0, 32), float(c), AL.is_equal)
-                act(f("ocv"), P(6, 0, 32))
-                for c in range(4):
-                    act(f("DD", 32 * c, 32 * c + 32), P(6, 32, 64), scale=-1.0, bias=f("N4p", c, c + 1))
-                if t == 0:
-                    act(b_("IDmb"), b_("ID"), scale=-16384.0); act(f("TRJ"), f("JW"), bias=1552.0)
-                    weave(tables_c, tables_d)
-                act(f("DDn"), f("DD"), scale=-1.0, bias=4096.0)
-                act(f("PUf"), ind(PL, u("UW")), bias=K["m32"], scale=K["pus"])
-            if ci == 2:
-                holes_table()
-                act(f("pos"), P(6, 32, 64), bias=-544.0)
-                if t == 0:
-                    act(b_("IDb"), b_("ID"), scale=16384.0); act(f("TRB"), f("JW"), bias=float(DZ + 513))
-                    act(f("J544"), f("JW"), bias=544.0); act(f("J512"), f("JW"), bias=512.0)
+                quad(P(5, 0, 128), b_("PU"), "YP", 0, 512)
+                quad(P(5, 128, 256), b_("PU"), "YP", 0, 512, (h_("ID"), h_("nd")))
+            if ci > 0:
+                classes(ci - 1, at - pn, pn)
             at += n; pn = n
-        if not last:
-            act(f("SLf"), sub(SL, 0, 512), scale=K["s01"])
-        ts(b_("B", at - pn, at), P(1 + (len(CHUNKS) - 1) % 2, 0, pn), K["thc"], AL.is_ge)
-        conv(P(4, 0, 32), b_("B"), "Yb", 512, (b_("ID"), b_("PEN")))
+        act(f("dq"), P(5, 0, 128), scale=-1.0, bias=c_("NP"))
+        act(f("qq"), P(5, 128, 256), bias=c_("nNP"))
         if t == 0:
-            weave(tables_e, tables_f)
-        tt(b_("lv"), P(4, 0, 32), f("ocv"), AL.not_equal)
-        for c in range(4):
-            tt(b_("LV", 32 * c, 32 * c + 32), b_("OH", 32 * c, 32 * c + 32), b_("lv"), AL.mult)
-        scan(b_("SLV", 1, 129), b_("ONE", 0, 128), b_("LV"), 0.0, AL.mult, AL.add)
-        mm(P(5, 4, 8), b_("BO"), b_("SLV", 32, 129, 32), True, False)
-        mm(P(5, 4, 8), b_("BOm"), b_("SLV", 0, 128, 32), False, True)
-        mm(P(5, 0, 4), b_("BO"), b_("SLV", 32, 129, 32), True, True)
-        for c in range(4):
-            mm(P(5, 32, 64), b_("IDmb"), b_("LV", 32 * c, 32 * c + 32), c == 0, c == 3)
-        tt(f("dl"), b_("LV"), f("DD"), AL.mult)
-        for c in range(4):
-            ts(b_("HF", 32 * c, 32 * c + 32), f("dl", 32 * c, 32 * c + 32), P(5, 4 + c, 5 + c), AL.is_gt)
-        scan(b_("SHF"), b_("ONE", 0, 128), b_("HF"), 0.0, AL.mult, AL.add)
-        mm(P(7, 0, 128), b_("ID"), b_("C512"), True, False)
-        mm(P(7, 0, 128), b_("NUP"), b_("HF"), False, False)
-        mm(P(7, 0, 128), b_("BO"), b_("SHF"), False, True)
-        tt(f("q"), b_("LV"), f("DDn"), AL.mult)
-        tt(f("Z9", 8, 288, 9), P(5, 32, 64), f("TRJ"), AL.add)
-        for c in range(4):
-            ts(f("Z9", c, 288, 9), f("q", 32 * c, 32 * c + 32), P(5, c, c + 1), AL.add, -4096.0, AL.add)
-        for c in range(4):
-            tt(f("Z9", 4 + c, 288, 9), P(7, 32 * c, 32 * c + 32), b_("HF", 32 * c, 32 * c + 32), AL.mult)
-        scan(f("Z9o"), f("R9"), f("Z9"), 0.0, AL.mult, AL.max)
-        cp(u("SLOT"), f("Z9o", 8, 288, 9))
-        act(ind(TT, u("SLOT")), f("PUf"), AF.Silu)
-        for c in range(4):
-            ts(b_("NE", 32 * c, 32 * c + 32), P(4, 0, 32), float(c), AL.is_equal)
-        tt(f("K4", 0, 4), f("N4c", 0, 4), P(5, 0, 4), AL.subtract)
-        tt(b_("JN"), b_("NE"), b_("OH"), AL.is_gt)
-        for c in range(5):
-            ts(f("Z5", c, 160, 5), f("JW"), -1.0 if c == 0 else P(5, c - 1, c), AL.is_ge, float(DZ) if c == 4 else f("K4", c, c + 1), AL.mult)
-        scan(b_("SJ", 1, 129), b_("ONE", 0, 128), b_("JN"), 0.0, AL.mult, AL.add)
-        mm(P(3, 0, 128), b_("IDb"), b_("JN"), True, False)
-        mm(P(3, 0, 128), b_("NUP"), b_("JN"), False, False)
-        mm(P(3, 0, 128), b_("BO"), b_("SJ", 1, 129), False, True)
-        mm(P(3, 128, 132), b_("BO"), b_("SJ", 0, 128, 32), True, True)
-        mm(P(3, 132, 136), b_("BO"), b_("SJ", 32, 129, 32), True, False)
-        mm(P(3, 132, 136), b_("BOm"), b_("SJ", 0, 128, 32), False, True)
-        scan(f("Z5o"), f("R5"), f("Z5"), 0.0, AL.mult, AL.max)
-        tt(f("KJa", 0, 4), f("N4c", 0, 4), P(5, 4, 8), AL.subtract)
-        tt(f("tp"), f("Z5o", 4, 160, 5), f("JW"), AL.add)
-        if not last:
-            tt(f("nA", 0, 4), f("N4", 0, 4), P(5, 4, 8), AL.subtract)
-        cp(u("TP"), f("tp"))
-        act(b_("TSb"), ind(BG, u("TP")))
-        tt(f("KJ", 0, 4), f("KJa", 0, 4), P(3, 128, 132), AL.subtract)
-        if not last:
-            tt(f("N4", 0, 4), f("nA", 0, 4), P(3, 132, 136), AL.add)
-        for c in range(4):
-            ts(f("Z4", c, 128, 4), P(3, 32 * c, 32 * c + 32), f("KJ", c, c + 1), AL.add, -16385.0, AL.add)
-        if not last:
-            tt(f("ta"), P(5, 32, 64), f("TRB"), AL.add)
-        scan(f("Z4o"), f("R4"), f("Z4"), 0.0, AL.mult, AL.max)
+            weave(tables_d, tables_e)
+        act(f("PUf"), b_("PU"))
         if last:
-            joins_positions()
-            cp(b_("JV"), ind(SF, u("PN")))
-        scan(b_("CU"), R("d0", 0, 512), sub(TT, 0, 512), 0.0, AL.mult, AL.add)
-        conv(P(6, 0, 32), b_("CU"), "Ym", 512)
-        if last:
-            touched_update()
-        conv(P(7, 0, 32), b_("TSb"), "Ys", 512)
-        if not last:
-            tt(f("tc"), f("Z4o", 3, 128, 4), f("ta"), AL.max)
-            k = len(ops)
-            draw_first(t + 1)
-            cp(u("BJ"), f("tc"))
-            ops.insert(k + 1, ops.pop())
-            act(ind(BS, u("BJ")), f("SLf"), AF.Silu)
-        tt(f("tf"), P(6, 0, 32), f("J512"), AL.min)
-        ts(u("IDX"), f("tf"), 512.0, AL.add)
-        cp(b_("TG"), ind(sub(TT, 0, 1536), u("IDX")))
-        if not last:
-            conv(P(0, 0, 32), b_("TG"), "Yt", 512)
-            weave(joins_positions, draw_second)
-            act(b_("JV"), ind(SF, u("PN")))
-            touched_update()
-            ts(u("BOW"), P(0, 0, 32), -544.0, AL.add)
-            cp(ind(BS, u("BOW")), b_("TSb"))
+            final(2304, 3072)
         else:
-            mm(P(2, 0, 512), b_("TR2"), b_("TG"), True, True)
-            stayers_sites()
-            ts(f("SLf"), P(2, 0, 512), K["m512"], AL.add)
-            cp(ind(PL, u("PLO")), f("SLf"))
-            big = 12582912.0
-            act(R("bag", 0, 768), R("pl", SH + 1792, SH + V_), bias=big)
-            act(R("ypb", 1792, V_), R("bag", 0, 768), bias=-big - 32.0)
-            for a, e in ((0, 896), (896, 1792)):
-                ts(R("ypb", a, e), R("pl", SH + a, SH + e), big, AL.add, big + 32.0, AL.subtract)
-            for a, e in ((0, 896), (1792, V_), (896, 1792)):
-                dma(T.yp[:, a:e], R("ypb", a, e, 1, 0, 16))
+            act(f("SLf"), sub(SL, 0, 512), scale=c_("s03"))
+        if t == 0:
+            tables_c()
+        mm(P(6, 0, 128), h_("ID"), h_("nd"), True, False)
+        mm(P(7, 0, 32), h_("ID"), h_("dW"), True, False)
+        classes(len(CHUNKS) - 1, at - pn, pn)
+        LV, JN = P(3, 256, 384), P(4, 256, 384)
+        scan(b_("SLV"), b_("ONE", 0, 128), LV, 0.0, AL.mult, AL.add)
+        for k, A in enumerate(("Aeq", "Ale", "Alt")):
+            mm(P(5, 488 + k, 489 + k), b_(A), b_("SLV", 127, 128), True, True)
+        cm, cMn, cM = P(5, 488, 489), P(5, 489, 490), P(5, 490, 491)
+        tt(f("dl"), LV, f("dq"), AL.mult)
+        mm(P(2, 0, 1), b_("Aeq"), b_("SLV", 127, 128), True, True)
+        tt(f("q"), LV, f("qq"), AL.mult)
+        act(b_("JN"), JN)
+        act(c_("L"), P(2, 0, 1), scale=-1.0, bias=c_("n"))
+        ts(b_("HF"), f("dl"), cm, AL.is_gt)
+        mm(P(6, 0, 128), b_("MB"), b_("HF"), False, False)
+        scan(b_("SJ"), b_("ONE", 0, 128), b_("JN"), 0.0, AL.mult, AL.add)
+        scan(b_("SHF"), b_("ONE", 0, 128), b_("HF"), 0.0, AL.mult, AL.add)
+        mm(P(6, 0, 128), b_("Aeq"), b_("SHF"), False, True)
+        mm(P(6, 128, 129), b_("Alt"), b_("SHF", 127, 128), True, True)
+        mm(P(0, 0, 128), b_("ID"), b_("cB"), True, False)
+        mm(P(0, 0, 128), b_("MB"), b_("JN"), False, False)
+        mm(P(0, 0, 128), b_("Aeq"), b_("SJ"), False, True)
+        mm(P(0, 128, 129), b_("Aeq"), b_("SJ", 127, 128), True, True)
+        ts(f("mk"), f("q"), cMn, AL.add, 0.0, AL.min)
+        ts(P(1, 128, 256), f("IQ"), cMn, AL.is_ge, c_("fn"), AL.mult)
+        ts(P(6, 256, 384), P(6, 0, 128), P(6, 128, 129), AL.add, 511.0 - 16384.0, AL.add)
+        ts(f("s1"), f("IQ"), cM, AL.is_ge, c_("L"), AL.mult)
+        tt(h_("fin"), P(6, 256, 384), f("mk"), AL.max)
+        fold(P(7, 0, 32), h_, "S", h_("fin"), False, True)
+        tt(f("ss"), P(1, 128, 256), f("s1"), AL.add)
+        act(f("X"), P(0, 0, 128), AF.Relu, bias=c_("L"))
+        if not last:
+            act(c_("n"), P(0, 128, 129), bias=c_("L"))
+        ts(u("SLOT"), P(7, 0, 32), 0.0, AL.add)
+        act(ind(TT, u("SLOT")), f("PUf"), AF.Silu)
+        mm(P(1, 0, 32), h_("ID"), h_("JW"), True, False)
+        fold(P(1, 0, 32), f, "S32", f("ss"), False, True)
+        if not last:
+            fold(P(2, 32, 64), f, "S32", f("X"), True, False)
+            fold(P(2, 32, 64), b_, "SB", b_("JN"), False, True)
+            draw_sizes()
+        fold(P(0, 256, 288), f, "S32", f("X"), True, True)
+        ts(u("TP"), P(1, 0, 32), 0.0, AL.add)
+        cp(b_("TSb"), ind(BG, u("TP")))
+        if not last:
+            tt(f("tc"), P(2, 32, 64), f("dB"), AL.min)
+            ts(u("BJ"), f("tc"), 16383.0, AL.add)
+            act(ind(BS, u("BJ")), f("SLf"), AF.Silu)
+        scan(h_("CU"), b_("d0u"), sub(TT, 0, 512), 0.0, AL.mult, AL.add)
+        mm(P(3, 384, 416), h_("ID"), h_("nJ"), True, False)
+        for r in range(16):
+            mm(P(3, 384, 416), h_("Yu", 16 - r, 144 - r), h_("CU", r, 512, 16), False, r == 15)
+        ts(u("PN"), P(0, 256, 288), 0.0, AL.add)
+        if not last:
+            draw_a(t + 1)
+        ts(u("IDX"), P(3, 384, 416), 1023.0, AL.add)
+        cp(b_("TG"), ind(sub(TT, 0, 1024), u("IDX")))
+        act(b_("JV"), ind(SF, u("PN")))
+        conv(P(4, 384, 416), b_("TSb"), "Ys", 512)
+        if not last:
+            conv(P(5, 32, 64), b_("TG"), "Yt", 512)
+        mm(P(7, 0, 512), b_("TR2"), b_("TG"), True, True)
+        mm(P(6, 0, 512), b_("TR1b"), b_("B"), True, False)
+        mm(P(6, 0, 512), b_("TR1"), b_("JV"), False, True)
+        conv(P(0, 288, 320), sub(SL, 0, 512), "Ys", 512, False)
+        fold(P(0, 288, 320), b_, "SG", b_("JN"), False, True)
+        ts(u("PLO"), P(4, 384, 416), -32.0, AL.add)
+        if not last:
+            draw_b()
+            ts(u("BOW"), P(5, 32, 64), -33.0, AL.add)
+            cp(ind(BS, u("BOW")), b_("TSb"))
+            act(f("TGf"), P(7, 0, 512))
+            act(ind(PL, u("PLO")), f("TGf"), AF.Silu)
+        else:
+            ts(f("TGf"), P(7, 0, 512), -33.0, AL.add)
+            act(f("JVf"), P(6, 0, 512), bias=-33.0)
+            cp(ind(YP, u("PLO")), f("TGf"))
+            leavers()
+            cp(ind(YP, u("POF")), f("JVf"))
+            dma(T.yp[:], R("ypb", SH, 3072, 1, 3, 16))
 
     def psum(x):
         return x[0][0] == "p" and x[0][1:].isdigit()

@@ -4,24 +4,25 @@ from concourse.mybir import AluOpType, AxisListType, ActivationFunctionType
 AL, AF = AluOpType, ActivationFunctionType
 V_, SH, RO = 2560, 512, 3
 DZ, BAGW, PLW, BIG = 10240, 11328, 3584, 131072
-CHUNKS = ((0, 64), (128, 0), (112, 16), (96, 16), (80, 0))
-MOVE_S = ((0, 64), (64, 144), (144, 192), (192, 208))
-MOVE_V = ((224, 256), (208, 224))
-SUMS = ((144, 192), (192, 256))
-SPR = (4, 10)
-ZG = 10
+CHUNKS = ((0, 100), (128, 0), (112, 0), (108, 0), (64, 0))
+MOVE_S = ((0, 64), (64, 128), (172, 224))
+MOVE_V = ((128, 172), (224, 256))
+SPR = (4, 11, 15)
+ZG = 11
+BAT = 7
+NBU1 = 256
 
 CL = {k: n for n, k in enumerate("c cD km p0 k c25 pp iv0 ivc t n sd sd0 sd1 sd2 npp inv bk thc c33 sb NP nNP fn L s01 s03 s23 y".split())}
-F32 = dict(blk=256, rcol=16, E=16, E32=16, BK=16, G9=16, col=48, cl=32, JW=32, JH=16, TS=16, G4=16, G3=16, EQ=16, Aa=16, t4=16, T3=16,
-           TR=16, TR2=16, JT=256, c65=16, cD=32, c513=32, t16=16, t32=32, t32b=32, dB=32, dP=32, tc=32, tg=32, AD=128, A0=128,
-           S32=144, IQ=128, dq=128, qq=128, dl=128, q=128, mk=128, s1=128, ss=128, X=128, nh=160, nl=160, SLf=512, PUf=512, JVf=512,
+F32 = dict(blk=128, rcol=16, E=16, BK=32, G9=16, col=48, cl=32, JW=32, JH=16, TS=16, G4=16, G3=16, EQ=16, Aa=16, t4=16, T3=16,
+           JT=256, c65=16, c513=32, t16=16, t32b=32, dB=32, dP=32, tc=32, tg=32, AD=128, A0=128,
+           S32=144, IQ=128, dq=128, qq=128, s1=128, ss=128, X=128, SLf=512, PUf=512, JVf=512,
            TGf=512, one=128, msg=3 * 80, land=9 * 80)
 BF = dict(Z=16 * 144, G2=144, Ys=144, Yj=144, Yr=144, Yk=144, Yt=144, YP=144, YL=144, YJ=144, PEN=128, TR1=128, TR1b=128, TR3=128,
           BO=128, BO2=128, BOm=128, BOm16=128, ID=128, ID16=128, IDm=128, TR2=128, Aeq=128, Ale=128, Alt=128, MB=128, SB=144, SG=144,
-          cB=128, C75=128, ONE=528, VD=256, VN=256, UF=512, RS=256, XM=256, DL=256, XL=64, RK=512, XU=512, PU=512, B=512,
-          JN=128, HF=128, SLV=128, SHF=128, SJ=128, TG=512, TSb=512, JV=512, d0u=512, SFb=512, fl=5 * 160, th=16,
+          cB=128, cD=32, C75=128, ONE=528, VD=256, VN=256, UF=512, RS=256, XM=256, DL=256, XL=64, RK=512, XU=512, PU=512, B=512,
+          JN=128, HF=128, SLV=128, SHF=128, SJ=128, TG=512, TSb=512, JV=512, d0u=512, SFb=512, ZR=512, fl=5 * 160, th=16,
           tl=16, cnt=16, SEL=3 * 336, SL=3 * 1024, CS=1040)
-F16 = dict(ID=128, nd=128, dW=32, JW=32, nJ=32, Yu=144, S=144, fin=128, CU=512)
+F16 = dict(ID=128, nd=128, dW=32, JW=32, nJ=32, Yu=144, Yv=144, S=144, fin=128, dl=128, q=128, mk=128, B14=128, CU=512)
 U16 = dict(plu=160, DP=16, U0=32, DWc=16, NBD=256, SW=16, JWu=16, RW=32, UW=32, NBU=512, GO=16, SLOT=32, TP=32, IDX=32, BOW=32,
            PLO=32, BJ=32, PN=32, POF=32)
 I32 = dict(plc=160, pi=16, ts=16, tsh=16, tsl=16, xi=16, bi=16, pr=16, sh=16, b=160, c=160, d=160, e=160, n0=160)
@@ -44,12 +45,12 @@ SCRATCH.update({
     "bag": ("sbuf", [128, BAGW], "float32"), "pl": ("sbuf", [128, PLW], "float32"), "ypb": ("sbuf", [128, PLW], "float32"),
     "nbt": ("sbuf", [128, 3072], "int32"), "xw": ("sbuf", [128, 5728], "bfloat16"), "sf": ("sbuf", [128, 3072], "float32"),
     "ff": ("sbuf", [128, 3072], "bfloat16"), "ct": ("sbuf", [128, 3072], "bfloat16"),
-    "d0": ("sbuf", [128, 1280], "bfloat16"), "gg": ("sbuf", [128, 8192], "bfloat16"), "mm": ("sbuf", [128, 4608], "bfloat16"),
+    "d0": ("sbuf", [128, V_], "bfloat16"), "gg": ("sbuf", [128, 8192], "bfloat16"), "mm": ("sbuf", [128, 4096], "bfloat16"),
     "tt": ("sbuf", [128, 3 * 1536], "float32"),
 })
 for _k in range(8):
     SCRATCH["p%d" % _k] = ("psum", [128, 512], "float32")
-NDMA = 40
+NDMA = 48
 SEMAPHORES = ["qv", "qs", "qp", "qg", "gin", "sent", "sent0"] + ["arr%d" % k for k in range(3)] + ["dm%d" % k for k in range(NDMA)]
 
 
@@ -150,9 +151,9 @@ def rank_program(g, core, T, topo):
     def sub(x, a, b, st=1):
         return (x[0], x[1] + a, x[1] + b, st, x[4], x[5])
 
-    def conv(o, src, Y, n, stop=True):
+    def conv(o, src, Y, n, stop=True, start=True, tab=b_):
         for r in range(16):
-            mm(o, b_(Y, 16 - r, 144 - r), sub(src, r, n, 16), r == 0, stop and r == 15)
+            mm(o, tab(Y, 16 - r, 144 - r), sub(src, r, n, 16), start and r == 0, stop and r == 15)
 
     def quad(o, src, Y, a, n, first=None):
         if first is not None:
@@ -175,13 +176,15 @@ def rank_program(g, core, T, topo):
         ops[-1]["remote"] = True
         return bin(m).count("1")
 
+    def aside(part):
+        k = len(ops)
+        part()
+        l = ops[k:]
+        del ops[k:]
+        return l
+
     def weave(*parts):
-        lists = []
-        for p in parts:
-            k = len(ops)
-            p()
-            lists.append(ops[k:])
-            del ops[k:]
+        lists = [aside(p) for p in parts]
         while any(lists):
             for l in lists:
                 if l:
@@ -200,9 +203,6 @@ def rank_program(g, core, T, topo):
     def ymat(name, w):
         act(b_(name, 0, 144, 16), f("G9", 0, 9), scale=w)
 
-    def trmat(name, p, w):
-        act(b_(name, p, 128, 16), f("G9", 1, 9), scale=w)
-
     def c_(k):
         return f("cl", CL[k], CL[k] + 1)
 
@@ -211,7 +211,8 @@ def rank_program(g, core, T, topo):
     NBT, SF, PL = R("nbt", 0, 3072), R("sf", 0, 3072), R("pl", 0, PLW)
     BD, BG, BS = R("bag", 0, DZ + 256), R("bag", 0, DZ + 512), R("bag", 0, BAGW)
     F, YP = R("ff", 0, 3072), R("ypb", 0, PLW)
-    HI, LO = f("JVf", 0, 256), f("JVf", 256, 512)
+    HI, LO = f("JVf", 0, 128), f("JVf", 256, 384)
+    NH, NL = f("PUf", 0, 160), f("PUf", 160, 320)
     ZERO = R("xw", 0, SH)
     K = {}
 
@@ -226,14 +227,13 @@ def rank_program(g, core, T, topo):
     act(b_("CS", 0, 528), b_("ONE"), AF.Silu, scale=65.0)
     act(b_("CS", 1024, 1040), b_("ONE", 0, 16), scale=65.0)
     iota(i_("pi", 0, 1), [[0, 1]], 0, 1)
-    iota(LO, [[0, 4], [1, 64]])
-    iota(HI, [[64, 4], [0, 64]])
+    iota(LO, [[0, 2], [1, 64]])
+    iota(HI, [[64, 2], [0, 64]])
     mset(ZERO, 0.0)
     dma(R("nbt", SH, SH + V_), T.nb[:])
     for k in range(1, 6):
         dma(R("ff", k * 512, (k + 1) * 512), ZERO)
     dma(R("xw", SH + 512, SH + V_), T.x[:, 512:V_])
-    mset(R("ab", AT["ab"]["G2"], AT["ab"]["Yt"]), 0.0)
     for k, nme in enumerate(("Yt", "YJ")):
         dma(R("ab", AT["ab"][nme], AT["ab"][nme] + 432 - 32 * k), sub(ZERO, 0, 432 - 32 * k))
     dma(R("ab", AT["ab"]["TR1b"], AT["ab"]["BO"]), sub(ZERO, 0, 256))
@@ -241,21 +241,27 @@ def rank_program(g, core, T, topo):
     ts(i_("pi", 2, 3), i_("pi", 0, 1), 3, AL.bitwise_and)
     cp(f("rcol", 0, 2), i_("pi", 1, 3))
     ts(f("E"), sub(LO, 0, 16), f("rcol", 0, 1), AL.is_equal)
-    ts(f("BK", 0, 12), sub(LO, 0, 12), f("E", 0, 1), AL.mult, 256.0, AL.mult)
+    ts(f("BK", 0, 24), sub(LO, 0, 24), f("E", 0, 1), AL.mult, 128.0, AL.mult)
     ts(f("blk"), LO, 32.0, AL.add, f("E", 1, 2), AL.mult)
     ts(HI, HI, f("E", 0, 1), AL.mult)
-    cp(u("plu"), i_("plc"))
-    tt(R("sf", 0, 256), f("blk"), HI, AL.add)
+    tt(R("sf", 0, 128), f("blk"), HI, AL.add)
 
-    def sfk(k):
-        ts(R("sf", k * 256, (k + 1) * 256), R("sf", 0, 256), f("BK", k, k + 1), AL.add)
-    for a, e in ((2, 3), (3, 6), (6, 12)):
-        for k in range(a, e):
-            sfk(k)
-        act(ind(R("bag", 0, DZ), u("plu", (a - 2) * 16, (e - 2) * 16)), R("sf", a * 256, e * 256), AF.Silu)
-        if a == 3:
+    def sfk(k, n):
+        ts(R("sf", k * 128, (k + n) * 128), R("sf", 0, n * 128), f("BK", k, k + 1), AL.add)
+
+    def bags(a, e):
+        act(ind(R("bag", 0, DZ), u("plu", (a - 4) * 8, (e - 4) * 8)), R("sf", a * 128, e * 128), AF.Silu)
+    sfk(4, 1); sfk(1, 1); sfk(5, 1)
+    cp(u("plu"), i_("plc"))
+    bags(4, 6)
+    mset(R("ab", AT["ab"]["G2"], AT["ab"]["Yt"]), 0.0)
+    for a, e in ((6, 12), (12, 24)):
+        for k in range(a, e, 2):
+            sfk(k, 2)
+        bags(a, e)
+        if a == 6:
             mset(R("af", AT["af"]["AD"], AT["af"]["S32"] + 144), 0.0)
-    sfk(1)
+    sfk(2, 2)
     asel(f("G9", 0, 9), f("one", 0, 9), [[-16, 9]], AL.is_ge, 16, 1)
     asel(f("G9", 0, 9), f("G9", 0, 9), [[16, 9]], AL.is_ge, -1, -1)
     asel(b_("BO"), f("one"), [[-16, 8], [0, 16]], AL.is_ge, 0, 1)
@@ -322,7 +328,7 @@ def rank_program(g, core, T, topo):
     def first_fields():
         ts(i_("b"), i_("n0"), 0xFC0, AL.bitwise_and)
         ts(i_("c"), i_("n0"), 63, AL.bitwise_and)
-        ts(f("nh"), i_("b"), float(SH), AL.add); ts(f("nl"), i_("c"), 32.0, AL.add)
+        ts(NH, i_("b"), float(SH), AL.add); ts(NL, i_("c"), 32.0, AL.add)
     weave(first_sizes, first_seeds, first_fields)
 
     def draw_sizes():
@@ -341,16 +347,19 @@ def rank_program(g, core, T, topo):
         ts(i_("sh"), i_("pr"), 12, AL.arith_shift_right)
         ts(u("DP"), i_("sh"), c_("inv"), AL.add, c_("c25"), AL.add)
 
-    def final(a, e):
+    def final_s(a, e):
         act(sub(YP, a, e), sub(PL, a, e), bias=12582912.0)
         act(sub(YP, a, e), sub(YP, a, e), bias=-12582912.0 - 33.0)
+
+    def final_v(a, e):
+        ts(sub(YP, a, e), sub(PL, a, e), 12582912.0, AL.add, 12582912.0 + 33.0, AL.subtract)
 
     def leavers():
         tt(f("tg"), P(0, 288, 320), f("dP"), AL.min)
         ts(u("POF"), f("tg"), 16384.0 - 32.0, AL.add)
 
     def piece(r):
-        return P((0, 2, 7, 5, 6)[r // 3], (r % 3) * 160, (r % 3 + 1) * 160) if r < 15 else P(1, 256, 416)
+        return P((0, 7, 5, 6, 2)[r // 3], (r % 3) * 160, (r % 3 + 1) * 160) if r < 15 else P(1, 256, 416)
 
     def spread(r0, r1):
         for r in range(r0, r1):
@@ -381,16 +390,18 @@ def rank_program(g, core, T, topo):
         ts(b_("Ys", 0, 144, 16), f("G9", 0, 9), c_("s03"), AL.mult)
         ts(c_("s23"), c_("s03"), c_("s01"), AL.subtract)
         ts(f("JT"), f("JT"), f("E", 4, 5), AL.mult)
-        cp(b_("SEL", 0, 64), R("sf", 2048, 2112))
-        act(b_("SFb"), R("sf", 0, 512))
-        act(R("bag", DZ + 256, DZ + 512), R("sf", 256, 512))
-        dma(R("sf", SH, 3072, 1, 2, 16), f("nh")); dma(R("sf", SH, 3072, 1, 3, 16), f("nl"))
+        act(b_("SEL", 0, 64), R("sf", 2048, 2112))
+        dma(R("sf", SH, 3072, 1, 2, 16), NH); dma(R("sf", SH, 3072, 1, 3, 16), NL)
         for r in range(2):
-            dma(R("sf", 0, SH, 1, 2 + r, 16), R("bag", DZ, DZ + SH, 1, r, 16))
+            dma(R("sf", 0, 256, 1, 2 + r, 16), R("bag", DZ, DZ + 256, 1, r, 16))
+
+    def stand_ins():
+        act(b_("SFb"), R("sf", 0, 512), scale=c_("s01"))
+        act(R("bag", DZ + 256, DZ + 512), R("sf", 256, 512))
+        for t in range(1, RO):
+            act(b_("SEL", t * 336, t * 336 + 64), R("sf", 2048, 2112), scale=c_("s01"))
         for t in range(RO):
             dma(b_("SL", t * 1024, t * 1024 + 512), b_("SFb"))
-            if t:
-                dma(b_("SEL", t * 336, t * 336 + 64), b_("SEL", 0, 64))
 
     def tables_move():
         ts(f("JW"), f("JW"), f("rcol", 0, 1), AL.add)
@@ -401,17 +412,15 @@ def rank_program(g, core, T, topo):
         act(b_("VD"), b_("ONE", 0, 256), scale=c_("s01"))
         act(b_("ID16"), b_("ID"), scale=0.0625); act(b_("IDm"), b_("ID"), scale=-1.0)
         mset(b_("C75"), -7.5)
-        act(R("d0", 0, 320), b_("ONE", 0, 320), scale=column([(3, -1)], 1.0))
-        act(b_("VN"), b_("ONE", 0, 256), scale=c_("s23"))
-        for k in range(1, 4):
-            dma(R("d0", k * 320, (k + 1) * 320), R("d0", 0, 320))
-
-    def tables_move2():
         ts(c_("y"), c_("s03"), 1.0 / 8192, AL.mult, f("E", 4, 5), AL.add)
-        mset(f("msg"), 0.0)
-        ts(b_("Yj", 0, 144, 16), f("G9", 0, 9), c_("y"), AL.mult)
-        for d in range(N - 1):
-            ts(u("GO", 5 * d + 4, 5 * d + 5), f("rcol", 0, 1), 1600.0 + 512 * d, AL.add)
+        ymat("Yj", c_("y"))
+        ts(R("d0", 0, 512), b_("ONE", 0, 512), f("E", 3, 4), AL.subtract)
+        act(b_("VN"), b_("ONE", 0, 256), scale=c_("s23"))
+        for k in range(1, 5):
+            dma(R("d0", k * 512, (k + 1) * 512), R("d0", 0, 512))
+        dma(b_("d0u"), ZERO)
+        dma(b_("ZR"), ZERO)
+        dma(R("ab", AT["ab"]["d0u"], AT["ab"]["d0u"] + 512, 1, 14, 16), R("ab", AT["ab"]["ONE"], AT["ab"]["ONE"] + 512, 1, 14, 16))
 
     def tables_sort():
         def one():
@@ -425,24 +434,29 @@ def rank_program(g, core, T, topo):
             act(c_("c33"), c_("c"), scale=float(V_), bias=33.0)
             act(f("c513"), f("JW"), bias=513.0)
         weave(one, two, three)
-        iota(f("cD"), [[-2048, 2], [0, 16]])
+        iota(b_("cD"), [[-2048, 2], [0, 16]])
+        for k in range(3 * RO):
+            iota(f("land", 80 * k + 68, 80 * k + 80), [[0, 12]])
 
     def thresholds():
         red(f("T3", 0, 1), f("TS", 0, 3), AL.min)
         red(f("T3", 2, 3), f("TS", 0, 3), AL.max)
         red(c_("t"), f("TS", 0, 3))
-        mset(f("TR"), 0.0)
         ts(f("T3", 1, 2), c_("t"), f("T3", 0, 1), AL.subtract, f("T3", 2, 3), AL.subtract)
-        mset(f("TR", 14, 15), 1e9)
-        for a in (2, 5, 7):
-            cp(f("TR", a, a + 9, 4), f("T3", 0, 3))
 
-    def thresholds2():
-        tt(f("TR2"), f("TR"), f("E"), AL.mult)
-        red(c_("t"), f("TR2"))
-        ts(c_("thc"), c_("t"), float(BIG), AL.add)
-        for t in range(1, RO):
-            ts(c_("sd%d" % t), c_("sd"), float(41 * t), AL.add, c_("k"), AL.mult)
+    def masks():
+        def rows(k):
+            K["m%d" % k] = column([(4 * k + 2, 1), (4 * k + 5, 1), (4 * k + 7, 1)])
+        weave(lambda: rows(0), lambda: rows(1), lambda: rows(2))
+        act(c_("thc"), f("E", 14, 15), scale=1e9, bias=float(BIG))
+
+    def thresholds3():
+        for k in range(3):
+            ts(c_("thc"), K["m%d" % k], f("T3", k, k + 1), AL.mult, c_("thc"), AL.add)
+
+    def spare_ghosts():
+        for d in range(N - 1):
+            ts(u("GO", 5 * d + 4, 5 * d + 5), f("rcol", 0, 1), 1600.0 + 512 * d, AL.add)
 
     def tables_q():
         cp(h_("ID"), b_("ID"))
@@ -451,6 +465,8 @@ def rank_program(g, core, T, topo):
 
     def tables_g1():
         iota(f("IQ"), [[4, 128]])
+        put(b_("TR3"), [[-16, 8], [1000, 16]], -2000, 1.0)
+        put(b_("TR3"), [[-16, 8], [1000, 16]], -4001, 1.0)
         iota(R("pl", 0, SH), [[0, SH]])
         for row in (2, 4):
             put(b_("YP"), [[-16, 9], [0, 4], [1000, 4]], 16 - row, 1.0)
@@ -476,24 +492,31 @@ def rank_program(g, core, T, topo):
         for c in range(4):
             put(f("S32"), [[-16, 9], [1000, 4], [-1, 4]], 16 - 4 * c, 1.0)
 
+    def tables_g3():
+        one, two = [[-16, 8], [1000, 16]], [[-16, 8], [1000, 8], [0, 2]]
+        asel(b_("TR2"), b_("ID"), [[0, 8], [1, 16]], AL.not_equal, -3, 0)
+        for k in range(4):
+            put(b_("TR1b"), one, -1000 * (5 + 2 * k) - 4 * k - 3, 32.0)
+            if k < 2:
+                put(b_("TR2"), one, -3000 - 2 - 2 * k, 1.0)
+                put(b_("TR1"), one, -1000 * (3 + k) - 1, 1.0)
+        put(b_("TR1"), two, -1000, 1.0)
+        for row in (7, 11, 15):
+            put(b_("TR1b"), two, -1000 - row, float(V_))
+
     def tables_s1():
         for nme, w in (("BOm", -1.0), ("BO2", 2.0), ("BOm16", -16.0)):
             act(b_(nme), b_("BO"), scale=w)
 
-    def tables_a():
-        f2 = column([(14, 1), (15, 1)])
-        trmat("TR3", 2, f("E", 0, 1)); trmat("TR3", 4, f("E", 1, 2))
-        hd = column([(2, DZ + 576)])
-        act(R("tt", 0, 512), b_("SFb"), bias=f2)
-        act(b_("d0u"), b_("ONE", 0, 512), scale=f("E", 14, 15))
-        mm(P(7, 0, 512), b_("TR3"), b_("SFb"), True, True)
-        act(R("tt", 512, 1024), P(7, 0, 512), bias=hd)
-        for t in range(1, RO):
-            dma(R("tt", t * 1536, t * 1536 + 1024), R("tt", 0, 1024))
+    def tables_a(t):
+        act(R("tt", t * 1536, t * 1536 + 512), b_("SFb"), bias=K["f2"])
+        act(R("tt", t * 1536 + 512, t * 1536 + 1024), P(7, 0, 512), bias=K["hd"])
 
     def tables_b():
         K["yu"] = column([(15, -544), (14, 1)], c_("s01"))
         K["s24"] = column([(2, 1), (4, 1)])
+        K["f2"] = column([(14, 1), (15, 1)])
+        K["hd"] = column([(2, DZ + 576)])
         ymat("Yt", K["s24"])
         iota(b_("cB"), [[0, 128]], -16384)
         act(c_("sb"), c_("c"), scale=float(V_), bias=-16384.0)
@@ -501,24 +524,17 @@ def rank_program(g, core, T, topo):
         act(f("dP"), f("JW"), bias=float(3072 + 32 - 16384))
 
     def tables_c():
-        mset(h_("Yu"), 0.0)
         cp(h_("S"), f("S32"))
-        ts(h_("Yu", 0, 144, 16), f("G9", 0, 9), K["yu"], AL.mult)
         act(b_("SB"), f("S32"), scale=c_("sb"))
         act(b_("SG"), f("S32"), scale=-16384.0)
+        for k in range(1, RO):
+            act(c_("sd%d" % k), c_("k"), scale=41.0 * k, bias=c_("sd0"))
 
-    def tables_d():
-        act(f("E32"), f("E"), scale=32.0)
-        for k in range(4):
-            trmat("TR1b", 5 + 2 * k, f("E32", 4 * k + 3, 4 * k + 4))
-        w = column([(7, V_), (11, V_), (15, V_)])
-        for p in (2, 3):
-            trmat("TR1b", p, w)
-
-    def tables_e():
-        act(b_("TR2"), b_("ID"))
-        trmat("TR1", 2, f("E", 0, 1)); trmat("TR1", 3, c_("s01")); trmat("TR1", 4, f("E", 1, 2))
-        trmat("TR2", 3, K["s24"])
+    def tables_c2():
+        mset(R("ah", AT["ah"]["Yu"], AT["ah"]["S"]), 0.0)
+        ts(h_("Yu", 0, 144, 16), f("G9", 0, 9), K["yu"], AL.mult)
+        ts(h_("B14"), b_("BO"), f("E", 14, 15), AL.mult)
+        ts(h_("Yv", 0, 144, 16), f("G9", 0, 9), f("E", 15, 16), AL.mult, -16384.0, AL.mult)
 
     draw_sizes()
     weave(lambda: (draw_a(0), draw_b()), tables_draw, tables_z)
@@ -527,7 +543,7 @@ def rank_program(g, core, T, topo):
         SEL, SL = b_("SEL", t * 336, (t + 1) * 336), b_("SL", t * 1024, (t + 1) * 1024)
         TT = R("tt", t * 1536, (t + 1) * 1536)
         DW, N0W, DF, N0F = u("U0", 0, 16), u("U0", 16, 32), b_("UF", 0, 256), b_("UF", 256, 512)
-        msg = f("msg", t * 80, t * 80 + 80)
+        msg = f("msg", t * 80, t * 80 + 68)
         tt(DF, ind(BD, u("DP")), f("JT"), AL.add)
         conv(P(3, 0, 16), DF, "Ys", 256)
         if t == 0:
@@ -536,94 +552,105 @@ def rank_program(g, core, T, topo):
         else:
             leavers()
         ts(DW, P(3, 0, 16), -32.0, AL.add)
-        ts(u("DWc"), P(3, 0, 16), -32.0, AL.add, 1024.0, AL.min)
-        cp(u("NBD", 0, 64), ind(NBT, sub(DW, 0, 4)))
-        cp(u("NBD", 64, 256), ind(NBT, sub(DW, 4, 16)))
+        cp(u("NBD"), ind(NBT, DW))
+        if t:
+            act(N0F, ind(SF, DW), scale=c_("s23"))
         act(b_("XM"), ind(XS, DW), bias=-192.0)
         for a, e in MOVE_S:
             act(R("gg", a * 16, e * 16), ind(XN, u("NBD", a, e)))
 
         def move_sum(a, e):
-            o = P(1, a, e)
+            o = P(1 if a < MOVE_S[2][0] else 2, a, e)
             mm(o, b_("IDm"), b_("XM", a, e), True, False)
             mm(o, b_("ID16"), b_("C75", 0, e - a), False, False)
             for j in range(16):
                 mm(o, b_("ID16"), R("gg", a * 16 + j, e * 16, 16), False, j == 15)
         cp(ind(F, DW), b_("VD"))
-        ts(N0F, ind(SF, DW), c_("s23"), AL.mult)
+        ts(u("DWc"), P(3, 0, 16), -32.0, AL.add, 1024.0, AL.min)
         scan(b_("CS", 512, 1024), sub(F, 512, 1024), b_("CS", 0, 512), 0.0, AL.add, AL.min)
-        move_sum(*MOVE_S[0])
         if t == 0:
-            tables_move2()
+            ts(N0F, ind(SF, DW), c_("s23"), AL.mult)
         ts(b_("RS"), ind(b_("CS"), u("DWc")), K["k64"], AL.subtract, 0.0, AL.max)
         conv(P(4, 0, 32), R("ab", AT["ab"]["UF"] + 256, AT["ab"]["UF"] + 768), "Yr", 512)
+        move_sum(*MOVE_S[0])
         a, e = MOVE_V[0]
         cp(R("gg", a * 16, e * 16), ind(XN, u("NBD", a, e)))
         tt(f("t16"), P(4, 16, 32), f("c65"), AL.min)
         ts(N0W, P(4, 0, 16), -32.0, AL.add)
         ts(u("SW"), f("t16"), -1.0, AL.add)
         cp(ind(SEL, u("SW")), DF)
+        move_sum(*MOVE_V[0])
         move_sum(*MOVE_S[1])
         conv(P(3, 64, 68), sub(SEL, 0, 64), "Yj", 64)
-        for a, e in MOVE_V[1:]:
-            cp(R("gg", a * 16, e * 16), ind(XN, u("NBD", a, e)))
+        a, e = MOVE_V[1]
+        cp(R("gg", a * 16, e * 16), ind(XN, u("NBD", a, e)))
         if t == 0:
+            stand_ins()
             tables_sort()
-        for a, e in SUMS:
-            move_sum(a, e)
-        cp(u("JWu", 0, 4), P(3, 64, 68))
+        a = MOVE_S[2][0]
+        move_sum(a, 256)
         cp(ind(F, N0W), b_("VN"))
+        cp(u("JWu", 0, 4), P(3, 64, 68))
+        ts(b_("DL", 0, a), P(1, 0, a), 189.0, AL.max, 195.0, AL.min)
         ts(f("t16", 0, 4), u("JWu", 0, 4), -1.0, AL.mult, (-32.0 - SH) / 8192, AL.add)
         cp(b_("XL"), ind(b_("XM"), u("JWu", 0, 4)))
         tt(sub(msg, 64, 68), P(3, 64, 68), f("t16", 0, 4), AL.add)
-        ts(b_("DL"), P(1, 0, 256), 189.0, AL.max, 195.0, AL.min)
+        ts(b_("DL", a, 256), P(2, a, 256), 189.0, AL.max, 195.0, AL.min)
         tt(sub(msg, 0, 64), ind(b_("DL"), u("JWu", 0, 4)), b_("XL"), AL.add)
-        ne = send(msg, lambda d, t=t: f("land", (3 * t + d - 1) * 80, (3 * t + d) * 80), "arr%d" % t, "sent")
+        ne = send(msg, lambda d, t=t: f("land", (3 * t + d - 1) * 80, (3 * t + d - 1) * 80 + 68), "arr%d" % t, "sent")
         if t > 0:
             act(f("JVf"), P(6, 0, 512))
             act(ind(PL, u("POF")), f("JVf"), AF.Silu)
         else:
             tables_g1()
             spread(SPR[0], SPR[1])
-            fetch(0, SPR[0])
+            fetch(0, SPR[0] - 1)
+            masks()
+            fetch(SPR[0] - 1, SPR[0])
             tables_z2()
-            fetch(SPR[0], SPR[1])
-        scan(R("ct", SH, SH + 1280), R("d0", 0, 1280), sub(F, SH, SH + 1280), 0.0, AL.mult, AL.add)
-        scan(R("ct", SH + 1280, 3072), R("d0", 0, 1280), sub(F, SH + 1280, 3072), R("ct", SH + 1279, SH + 1280), AL.mult, AL.add)
+        scan(R("ct", SH, 3072), R("d0", 0, V_), sub(F, SH, 3072), 0.0, AL.mult, AL.add)
         act(b_("RK", 0, 256), ind(R("ct", 0, 3072), DW))
         cp(b_("RK", 256, 512), ind(R("ct", 0, 3072), N0W))
-        conv(P(3, 32, 64), b_("RK"), "Yk", 512)
+        conv(P(3, 32, 64), b_("RK"), "Yk", 512, False)
+        mm(P(3, 32, 64), b_("ID"), b_("cD"), False, True)
         if t == 0:
-            weave(tables_s1, tables_b)
+            fetch(SPR[0], SPR[1])
             act(f("IQ"), f("IQ"), bias=f("rcol", 1, 2))
-            tables_a()
-            spread(SPR[1], 16)
-            fetch(SPR[1], 16)
+            weave(tables_s1, tables_b)
+            spread(SPR[1], SPR[2])
+            fetch(SPR[1], SPR[2])
             ext("sent0", ne, R("xw", SH, SH + 512))
         tt(ind(XS, DW), b_("DL"), b_("XM"), AL.add)
         if last:
             dma(T.yx[:], XO)
         if t == 0:
             thresholds()
-        tt(f("t32"), P(3, 32, 64), f("cD"), AL.add)
-        ts(c_("NP"), c_("n"), c_("c33"), AL.add)
-        tt(f("t32b"), f("t32"), f("c513"), AL.min)
-        ts(c_("nNP"), c_("n"), -1.0, AL.mult, c_("c33"), AL.subtract)
+        tt(f("t32b"), P(3, 32, 64), f("c513"), AL.min)
+        act(c_("NP"), c_("n"), bias=c_("c33"))
+        act(c_("fn"), c_("n"), scale=-1.0, bias=float(V_))
+        act(c_("nNP"), c_("NP"), scale=-1.0)
         ts(u("RW"), f("t32b"), -1.0, AL.add)
-        ts(c_("fn"), c_("n"), -1.0, AL.mult, float(V_), AL.add)
         if last:
-            final(SH, 2304)
+            final_s(SH, 2048)
+        if t == 1:
+            mm(P(7, 0, 512), b_("TR3"), b_("SFb"), True, True)
+            tables_a(1)
+            dma(R("tt", 3072, 4096), R("tt", 1536, 2560))
         cp(ind(SL, u("RW")), b_("UF"))
         conv(P(4, 32, 64), sub(SL, 0, 512), "Ys", 512)
         if t == 0:
-            weave(thresholds2, tables_q)
+            spread(SPR[2], 16)
+            weave(thresholds3, spare_ghosts, tables_q)
             tables_g2()
+            tables_g3()
         if not last:
-            iota(R("ff", SH, 3072), [[0, V_]])
+            for k in range(1, 6):
+                dma(R("ff", k * 512, (k + 1) * 512), b_("ZR"))
         ts(u("UW"), P(4, 32, 64), -32.0, AL.add)
         act(b_("XU"), ind(XS, u("UW")))
-        for a, e in ((0, 256), (256, 512)):
-            cp(u("NBU", a, e), ind(NBT, u("UW", a // 16, e // 16)))
+        cp(u("NBU", 0, NBU1), ind(NBT, u("UW", 0, NBU1 // 16)))
+        if t == 0:
+            fetch(SPR[2], 16)
         act(b_("PU"), ind(PL, u("UW")))
         ext("arr%d" % t, ne * (N - 1), f("land", 3 * t * 80, 3 * (t + 1) * 80))
         for d in range(1, N):
@@ -631,63 +658,63 @@ def rank_program(g, core, T, topo):
             ts(u("GO", 5 * (d - 1), 5 * d - 1), f("land", o + 64, o + 68), 8192.0, AL.mult, 512.0 * (d - 1), AL.add)
         cp(ind(R("xw", 3072, 5728), u("GO", 0, 15)), f("land", 3 * t * 80, 3 * (t + 1) * 80))
         mm(P(0, 0, 512), b_("ID"), b_("XU"), True, True)
+        quad(P(5, 0, 128), b_("PU"), "YP", 0, 512)
+        quad(P(5, 128, 256), b_("PU"), "YP", 0, 512, (h_("ID"), h_("nd")))
+        mm(P(6, 0, 128), h_("ID"), h_("nd"), True, False)
+        if t == 0:
+            mm(P(7, 0, 512), b_("TR3"), b_("SFb"), True, True)
         at = 0
         for ci, (ns, nv) in enumerate(CHUNKS):
             if ci == 0:
                 cp(R("gg", 0, nv * 16), ind(XN, u("NBU", 0, nv)))
+                cp(u("NBU", NBU1, 512), ind(NBT, u("UW", NBU1 // 16, 32)))
             if ns:
                 act(R("gg", at * 16, (at + ns) * 16), ind(XN, u("NBU", at, at + ns)))
             at += ns + nv
 
-        def classes(ci, a, n):
-            ts(b_("B", a, a + n), P(1 + ci % 2, 0, n), c_("thc"), AL.is_ge)
+        def classes(a, n):
             quad(P(3, 256 + a // 4, 256 + (a + n) // 4), b_("B"), "YL", a, n)
             quad(P(4, 256 + a // 4, 256 + (a + n) // 4), b_("B"), "YJ", a, n)
         at = 0
         for ci, (ns, nv) in enumerate(CHUNKS):
             n = ns + nv
-            if ci and nv:
-                cp(R("gg", (at + ns) * 16, (at + n) * 16), ind(XN, u("NBU", at + ns, at + n)))
             o = P(1 + ci % 2, 0, n)
-            mo = ci % 2 * 2304
+            mo = ci % 2 * 2048
             mm(o, b_("BOm16"), b_("XU", at, at + n), True, False)
+            mm(o, b_("PEN"), b_("PU", at, at + n), False, False)
             for k in range(16):
                 mm(o, b_("BOm"), R("gg", at * 16 + k, (at + n) * 16, 16), False, False)
             for k in range(16):
                 tt(R("mm", mo + k * n, mo + (k + 1) * n), R("gg", at * 16 + k, (at + n) * 16, 16), P(0, at, at + n), AL.max)
-                mm(o, b_("BO2"), R("mm", mo + k * n, mo + (k + 1) * n), False, False)
-            mm(o, b_("PEN"), b_("PU", at, at + n), False, True)
-            if ci == 1:
-                quad(P(5, 0, 128), b_("PU"), "YP", 0, 512)
-                quad(P(5, 128, 256), b_("PU"), "YP", 0, 512, (h_("ID"), h_("nd")))
-            if ci > 0:
-                classes(ci - 1, at - pn, pn)
+                mm(o, b_("BO2"), R("mm", mo + k * n, mo + (k + 1) * n), False, k == 15)
+                if ci > 0 and k == BAT:
+                    ts(b_("B", at - pn, at), P(1 + (ci - 1) % 2, 0, pn), c_("thc"), AL.is_ge)
+                    if ci == len(CHUNKS) - 2:
+                        classes(0, at)
+                        done = at
             at += n; pn = n
         act(f("dq"), P(5, 0, 128), scale=-1.0, bias=c_("NP"))
         act(f("qq"), P(5, 128, 256), bias=c_("nNP"))
         if t == 0:
-            weave(tables_d, tables_e)
+            tables_a(0)
         act(f("PUf"), b_("PU"))
-        if last:
-            final(2304, 3072)
-        else:
+        if not last:
             act(f("SLf"), sub(SL, 0, 512), scale=c_("s03"))
         if t == 0:
             tables_c()
-        mm(P(6, 0, 128), h_("ID"), h_("nd"), True, False)
-        mm(P(7, 0, 32), h_("ID"), h_("dW"), True, False)
-        classes(len(CHUNKS) - 1, at - pn, pn)
+        ts(b_("B", at - pn, at), P(1 + (len(CHUNKS) - 1) % 2, 0, pn), c_("thc"), AL.is_ge)
+        classes(done, at - done)
         LV, JN = P(3, 256, 384), P(4, 256, 384)
         scan(b_("SLV"), b_("ONE", 0, 128), LV, 0.0, AL.mult, AL.add)
         for k, A in enumerate(("Aeq", "Ale", "Alt")):
             mm(P(5, 488 + k, 489 + k), b_(A), b_("SLV", 127, 128), True, True)
         cm, cMn, cM = P(5, 488, 489), P(5, 489, 490), P(5, 490, 491)
-        tt(f("dl"), LV, f("dq"), AL.mult)
+        tt(h_("dl"), LV, f("dq"), AL.mult)
         mm(P(2, 0, 1), b_("Aeq"), b_("SLV", 127, 128), True, True)
-        tt(f("q"), LV, f("qq"), AL.mult)
+        tt(h_("q"), LV, f("qq"), AL.mult)
         act(b_("JN"), JN)
         act(c_("L"), P(2, 0, 1), scale=-1.0, bias=c_("n"))
-        ts(b_("HF"), f("dl"), cm, AL.is_gt)
+        ts(b_("HF"), h_("dl"), cm, AL.is_gt)
         mm(P(6, 0, 128), b_("MB"), b_("HF"), False, False)
         scan(b_("SJ"), b_("ONE", 0, 128), b_("JN"), 0.0, AL.mult, AL.add)
         scan(b_("SHF"), b_("ONE", 0, 128), b_("HF"), 0.0, AL.mult, AL.add)
@@ -697,11 +724,12 @@ def rank_program(g, core, T, topo):
         mm(P(0, 0, 128), b_("MB"), b_("JN"), False, False)
         mm(P(0, 0, 128), b_("Aeq"), b_("SJ"), False, True)
         mm(P(0, 128, 129), b_("Aeq"), b_("SJ", 127, 128), True, True)
-        ts(f("mk"), f("q"), cMn, AL.add, 0.0, AL.min)
+        ts(h_("mk"), h_("q"), cMn, AL.add, 0.0, AL.min)
         ts(P(1, 128, 256), f("IQ"), cMn, AL.is_ge, c_("fn"), AL.mult)
         ts(P(6, 256, 384), P(6, 0, 128), P(6, 128, 129), AL.add, 511.0 - 16384.0, AL.add)
         ts(f("s1"), f("IQ"), cM, AL.is_ge, c_("L"), AL.mult)
-        tt(h_("fin"), P(6, 256, 384), f("mk"), AL.max)
+        tt(h_("fin"), P(6, 256, 384), h_("mk"), AL.max)
+        mm(P(7, 0, 32), h_("ID"), h_("dW"), True, False)
         fold(P(7, 0, 32), h_, "S", h_("fin"), False, True)
         tt(f("ss"), P(1, 128, 256), f("s1"), AL.add)
         act(f("X"), P(0, 0, 128), AF.Relu, bias=c_("L"))
@@ -709,51 +737,86 @@ def rank_program(g, core, T, topo):
             act(c_("n"), P(0, 128, 129), bias=c_("L"))
         ts(u("SLOT"), P(7, 0, 32), 0.0, AL.add)
         act(ind(TT, u("SLOT")), f("PUf"), AF.Silu)
+        if t == 0:
+            tables_c2()
+
+        def new_places():
+            mm(P(6, 0, 512), b_("TR1b"), b_("B"), True, False)
+            mm(P(6, 0, 512), b_("TR1"), b_("JV"), False, True)
+            conv(P(0, 288, 320), sub(SL, 0, 512), "Ys", 512, False)
+            fold(P(0, 288, 320), b_, "SG", b_("JN"), False, True)
+        if last:
+            final_v(2048, 2560)
+            fold(P(2, 256, 288), f, "S32", f("X"), True, True)
+            ts(u("PN"), P(2, 256, 288), 0.0, AL.add)
+            cp(b_("JV"), ind(SF, u("PN")))
         mm(P(1, 0, 32), h_("ID"), h_("JW"), True, False)
         fold(P(1, 0, 32), f, "S32", f("ss"), False, True)
-        if not last:
+        if last:
+            new_places()
+        else:
             fold(P(2, 32, 64), f, "S32", f("X"), True, False)
             fold(P(2, 32, 64), b_, "SB", b_("JN"), False, True)
             draw_sizes()
-        fold(P(0, 256, 288), f, "S32", f("X"), True, True)
+            fold(P(0, 256, 288), f, "S32", f("X"), True, True)
         ts(u("TP"), P(1, 0, 32), 0.0, AL.add)
-        cp(b_("TSb"), ind(BG, u("TP")))
-        if not last:
+        if last:
+            act(b_("TSb"), ind(BG, u("TP")))
+            act(f("JVf"), P(6, 0, 512), bias=-33.0)
+            scan(h_("CU"), b_("d0u"), sub(TT, 0, 512), 0.0, AL.mult, AL.add)
+            mm(P(3, 384, 416), h_("ID"), h_("nJ"), True, False)
+            conv(P(3, 384, 416), h_("CU"), "Yu", 512, True, False, h_)
+            final_v(2560, 3072)
+            leavers()
+            ts(u("IDX"), P(3, 384, 416), 1023.0, AL.add)
+            act(b_("TG"), ind(sub(TT, 0, 1024), u("IDX")))
+            cp(ind(YP, u("POF")), f("JVf"))
+            conv(P(4, 384, 416), h_("CU"), "Yv", 512, False, True, h_)
+            conv(P(4, 384, 416), b_("TSb"), "Ys", 512, True, False)
+            mm(P(7, 0, 512), b_("TR2"), b_("TG"), True, True)
+            act(f("TGf"), P(7, 0, 512), bias=-33.0)
+            tt(f("tg"), P(4, 384, 416), f("dP"), AL.min)
+            ts(u("PLO"), f("tg"), 16384.0 - 32.0, AL.add)
+            cp(ind(YP, u("PLO")), f("TGf"))
+            dma(T.yp[:], R("ypb", SH, 3072, 1, 3, 16))
+        else:
+            cp(b_("TSb"), ind(BG, u("TP")))
             tt(f("tc"), P(2, 32, 64), f("dB"), AL.min)
             ts(u("BJ"), f("tc"), 16383.0, AL.add)
             act(ind(BS, u("BJ")), f("SLf"), AF.Silu)
-        scan(h_("CU"), b_("d0u"), sub(TT, 0, 512), 0.0, AL.mult, AL.add)
-        mm(P(3, 384, 416), h_("ID"), h_("nJ"), True, False)
-        for r in range(16):
-            mm(P(3, 384, 416), h_("Yu", 16 - r, 144 - r), h_("CU", r, 512, 16), False, r == 15)
-        ts(u("PN"), P(0, 256, 288), 0.0, AL.add)
-        if not last:
-            draw_a(t + 1)
-        ts(u("IDX"), P(3, 384, 416), 1023.0, AL.add)
-        cp(b_("TG"), ind(sub(TT, 0, 1024), u("IDX")))
-        act(b_("JV"), ind(SF, u("PN")))
-        conv(P(4, 384, 416), b_("TSb"), "Ys", 512)
-        if not last:
-            conv(P(5, 32, 64), b_("TG"), "Yt", 512)
-        mm(P(7, 0, 512), b_("TR2"), b_("TG"), True, True)
-        mm(P(6, 0, 512), b_("TR1b"), b_("B"), True, False)
-        mm(P(6, 0, 512), b_("TR1"), b_("JV"), False, True)
-        conv(P(0, 288, 320), sub(SL, 0, 512), "Ys", 512, False)
-        fold(P(0, 288, 320), b_, "SG", b_("JN"), False, True)
-        ts(u("PLO"), P(4, 384, 416), -32.0, AL.add)
-        if not last:
-            draw_b()
-            ts(u("BOW"), P(5, 32, 64), -33.0, AL.add)
-            cp(ind(BS, u("BOW")), b_("TSb"))
+            conv(P(2, 384, 416), b_("TSb"), "Ys", 512)
+            for h, bank in ((0, 3), (1, 1)):
+                a = 256 * h
+                scan(h_("CU", a, a + 256), b_("d0u", 0, 256), sub(TT, a, a + 256), 0.0, AL.mult, AL.add)
+                if h:
+                    mm(P(bank, 400, 401), h_("B14"), h_("CU", 255, 256), True, True)
+                mm(P(bank, 384, 400), h_("ID"), h_("nJ", 16 * h, 16 * h + 16), True, False)
+                conv(P(bank, 384, 400), h_("CU", a, a + 256), "Yu", 256, True, False, h_)
+            ts(u("PN"), P(0, 256, 288), 0.0, AL.add)
+            act(b_("JV"), ind(SF, u("PN")))
+            da, db = aside(lambda: draw_a(t + 1)), aside(draw_b)
+            ops.extend(da[:2])
+            for h, bank in ((0, 3), (1, 1)):
+                a = 256 * h
+                if h:
+                    ts(u("IDX", 16, 32), P(bank, 384, 400), 1023.0, AL.add, P(bank, 400, 401), AL.add)
+                else:
+                    ts(u("IDX", 0, 16), P(bank, 384, 400), 1023.0, AL.add)
+                ops.extend(da[2:4] if h == 0 else da[4:])
+                cp(b_("TG", a, a + 256), ind(sub(TT, 0, 1024), u("IDX", 16 * h, 16 * h + 16)))
+                conv(P(5 - h, 32, 48), b_("TG", a, a + 256), "Yt", 256)
+            mm(P(7, 0, 512), b_("TR2"), b_("TG"), True, True)
+            new_places()
+            ops.append(db[0])
+            ts(u("BOW", 0, 16), P(5, 32, 48), -33.0, AL.add)
+            ops.append(db[1])
+            cp(ind(BS, u("BOW", 0, 16)), b_("TSb", 0, 256))
+            ts(u("BOW", 16, 32), P(4, 32, 48), -33.0, AL.add)
+            ts(u("PLO"), P(2, 384, 416), -32.0, AL.add)
+            ops.append(db[2])
+            cp(ind(BS, u("BOW", 16, 32)), b_("TSb", 256, 512))
             act(f("TGf"), P(7, 0, 512))
             act(ind(PL, u("PLO")), f("TGf"), AF.Silu)
-        else:
-            ts(f("TGf"), P(7, 0, 512), -33.0, AL.add)
-            act(f("JVf"), P(6, 0, 512), bias=-33.0)
-            cp(ind(YP, u("PLO")), f("TGf"))
-            leavers()
-            cp(ind(YP, u("POF")), f("JVf"))
-            dma(T.yp[:], R("ypb", SH, 3072, 1, 3, 16))
 
     def psum(x):
         return x[0][0] == "p" and x[0][1:].isdigit()

from concourse.bass import DstId, RemoteDMATransfer
from concourse.mybir import AluOpType, AxisListType, ActivationFunctionType

AL, AF = AluOpType, ActivationFunctionType
V_, SH, RO = 2560, 512, 3
DZ, BAGW, PLW, BIG = 10240, 11328, 3584, 131072
CHUNKS = ((0, 100), (128, 0), (112, 0), (108, 0), (64, 0))
MOVE_S = ((0, 64), (64, 128), (172, 224))
MOVE_V = ((128, 172), (224, 256))
SPR = (4, 11, 15)
ZG = 11
BAT = 7
NBU1 = 256

CL = {k: n for n, k in enumerate("c cD km p0 k c25 pp iv0 ivc t n sd sd0 sd1 sd2 npp inv bk thc c33 sb NP nNP fn L s01 s03 s23 y".split())}
F32 = dict(blk=128, rcol=16, E=16, BK=32, G9=16, col=48, cl=32, JW=32, JH=16, TS=16, G4=16, G3=16, EQ=16, Aa=16, t4=16, T3=16,
           JT=256, c65=16, c513=32, t16=16, t32b=32, dB=32, dP=32, tc=32, tg=32, AD=128, A0=128,
           S32=144, IQ=128, dq=128, qq=128, s1=128, ss=128, X=128, SLf=512, PUf=512, JVf=512,
           TGf=512, one=128, msg=3 * 80, land=9 * 80)
BF = dict(Z=16 * 144, G2=144, Ys=144, Yj=144, Yr=144, Yk=144, Yt=144, YP=144, YL=144, YJ=144, PEN=128, TR1=128, TR1b=128, TR3=128,
          BO=128, BO2=128, BOm=128, BOm16=128, ID=128, ID16=128, IDm=128, TR2=128, Aeq=128, Ale=128, Alt=128, MB=128, SB=144, SG=144,
          cB=128, cD=32, C75=128, ONE=528, VD=256, VN=256, UF=512, RS=256, XM=256, DL=256, XL=64, RK=512, XU=512, PU=512, B=512,
          JN=128, HF=128, SLV=128, SHF=128, SJ=128, TG=512, TSb=512, JV=512, d0u=512, SFb=512, ZR=512, fl=5 * 160, th=16,
          tl=16, cnt=16, SEL=3 * 336, SL=3 * 1024, CS=1040)
F16 = dict(ID=128, nd=128, dW=32, JW=32, nJ=32, Yu=144, Yv=144, S=144, fin=128, dl=128, q=128, mk=128, B14=128, CU=512)
U16 = dict(plu=160, DP=16, U0=32, DWc=16, NBD=256, SW=16, JWu=16, RW=32, UW=32, NBU=512, GO=16, SLOT=32, TP=32, IDX=32, BOW=32,
           PLO=32, BJ=32, PN=32, POF=32)
I32 = dict(plc=160, pi=16, ts=16, tsh=16, tsl=16, xi=16, bi=16, pr=16, sh=16, b=160, c=160, d=160, e=160, n0=160)


def _arena(d):
    o, at = 0, {}
    for k, n in d.items():
        at[k] = o
        o += (n + 15) // 16 * 16
    return at, o


AT = {}
SCRATCH = {}
for _n, _d, _t in (("af", F32, "float32"), ("ab", BF, "bfloat16"), ("ah", F16, "float16"), ("au", U16, "uint16"), ("ai", I32, "int32")):
    AT[_n], _w = _arena(_d)
    SCRATCH[_n] = ("sbuf", [128, _w], _t)
SCRATCH.update({
    "bag": ("sbuf", [128, BAGW], "float32"), "pl": ("sbuf", [128, PLW], "float32"), "ypb": ("sbuf", [128, PLW], "float32"),
    "nbt": ("sbuf", [128, 3072], "int32"), "xw": ("sbuf", [128, 5728], "bfloat16"), "sf": ("sbuf", [128, 3072], "float32"),
    "ff": ("sbuf", [128, 3072], "bfloat16"), "ct": ("sbuf", [128, 3072], "bfloat16"),
    "d0": ("sbuf", [128, V_], "bfloat16"), "gg": ("sbuf", [128, 8192], "bfloat16"), "mm": ("sbuf", [128, 4096], "bfloat16"),
    "tt": ("sbuf", [128, 3 * 1536], "float32"),
})
for _k in range(8):
    SCRATCH["p%d" % _k] = ("psum", [128, 512], "float32")
NDMA = 48
SEMAPHORES = ["qv", "qs", "qp", "qg", "gin", "sent", "sent0"] + ["arr%d" % k for k in range(3)] + ["dm%d" % k for k in range(NDMA)]


def rank_program(g, core, T, topo):
    rank = T.rank_of(core)
    if rank is None:
        return
    N = len(T.cores)
    ops = []

    def R(buf, a, b, st=1, p0=0, ps=1):
        return (buf, a, b, st, p0, ps)

    def arena(name, tab):
        def get(k, a=0, b=None, st=1):
            o = AT[name][k]
            return (name, o + a, o + (tab[k] if b is None else b), st, 0, 1)
        return get
    f, b_, h_, u, i_ = arena("af", F32), arena("ab", BF), arena("ah", F16), arena("au", U16), arena("ai", I32)

    def P(k, a, b, st=1):
        return ("p%d" % k, a, b, st, 0, 1)

    def ind(win, off):
        return ("ind", win, off)

    def ap(x):
        if not isinstance(x, tuple):
            return x
        if x[0] == "ind":
            return ap(x[1]).indirect(ap(x[2]))
        t = T[x[0]]
        cs = slice(x[1], x[2]) if x[3] == 1 else slice(x[1], x[2], x[3])
        return t[:, cs] if x[5] == 1 else t[x[4]:128:x[5], cs]

    def add(eng, fn, out, ins, dma=False):
        rd, wr = [], []
        for x in ins:
            if isinstance(x, tuple):
                rd += [x[1], x[2]] if x[0] == "ind" else [x]
        if isinstance(out, tuple):
            if out[0] == "ind":
                wr.append(out[1]); rd.append(out[2])
            else:
                wr.append(out)
        ops.append(dict(e=eng, fn=fn, rd=rd, wr=wr, dma=dma, ext=None, scat=isinstance(out, tuple) and out[0] == "ind"))

    def ext(sem, val, region):
        ops.append(dict(e="x", fn=None, rd=[], wr=[region], dma=False, ext=(sem, val), scat=True))

    def cp(o, x):
        add("v", lambda: g.vector.tensor_copy(ap(o), ap(x)), o, [x])

    def tt(o, x, y, op):
        add("v", lambda: g.vector.tensor_tensor(ap(o), ap(x), ap(y), op), o, [x, y])

    def ts(o, x, s1, op0, s2=None, op1=None):
        if op1 is None:
            add("v", lambda: g.vector.tensor_scalar(ap(o), ap(x), ap(s1), None, op0), o, [x, s1])
        else:
            add("v", lambda: g.vector.tensor_scalar(ap(o), ap(x), ap(s1), ap(s2), op0, op1), o, [x, s1, s2])

    def scan(o, d0, d1, init, op0, op1):
        add("v", lambda: g.vector.tensor_tensor_scan(ap(o), ap(d0), ap(d1), ap(init), op0, op1), o, [d0, d1, init])

    def mset(o, c):
        add("v", lambda: g.vector.memset(ap(o), c), o, [])

    def red(o, x, op=AL.add):
        add("v", lambda: g.vector.tensor_reduce(ap(o), ap(x), AxisListType.X, op), o, [x])

    def act(o, x, fn=AF.Identity, bias=None, scale=None):
        kw = {}
        if bias is not None:
            kw["bias"] = bias
        if scale is not None:
            kw["scale"] = scale
        add("s", lambda: g.scalar.activation(ap(o), ap(x), fn, **{k: ap(v) for k, v in kw.items()}), o, [x, bias, scale])

    def mm(o, l, r, st, sp):
        add("p", lambda: g.tensor.matmul(ap(o), ap(l), ap(r), st, sp), o, [l, r])

    def iota(o, pat, base=0, cm=0):
        if o[0] in ("ai", "nbt"):
            add("g", lambda: g.iota(ap(o), pat, base, cm), o, [])
        else:
            add("g", lambda: g.iota(ap(o), pat, base, cm, allow_small_or_imprecise_dtypes=True), o, [])

    def asel(o, x, pat, op, base, cm):
        add("g", lambda: g.affine_select(ap(o), ap(x), pat, op, 0.0, base, cm), o, [x])

    def put(o, pat, base, fill):
        add("g", lambda: g.affine_select(ap(o), ap(o), pat, AL.not_equal, float(fill), base, 1), o, [o])

    def dma(o, x):
        add("y", lambda: g.sync.dma_start(ap(o), ap(x)), o, [x], dma=True)

    def sub(x, a, b, st=1):
        return (x[0], x[1] + a, x[1] + b, st, x[4], x[5])

    def conv(o, src, Y, n, stop=True, start=True, tab=b_):
        for r in range(16):
            mm(o, tab(Y, 16 - r, 144 - r), sub(src, r, n, 16), start and r == 0, stop and r == 15)

    def quad(o, src, Y, a, n, first=None):
        if first is not None:
            mm(o, first[0], first[1], True, False)
        for r in range(4):
            mm(o, b_(Y, 16 - r, 144 - r), sub(src, a + r, a + n, 4), r == 0 and first is None, r == 3)

    def fold(o, tab, Y, src, st, sp):
        for a in range(4):
            mm(o, tab(Y, 16 - 4 * a, 144 - 4 * a), sub(src, a, 128, 4), st and a == 0, sp and a == 3)

    def send(src, dst_of, sem, loc):
        peers = [T.cores[(rank + d) % N] for d in range(1, N)]
        m = topo.mask(core, peers[0])
        for c in peers[1:]:
            m &= topo.mask(core, c)
        ids = [DstId(rid=topo.addr(c)[0], pnc=topo.addr(c)[1]) for c in peers]
        add("g", lambda: g.remote_dma_fused([RemoteDMATransfer(dst_ids=ids, dma_engine_mask=m, remote_sem=T.sem[sem], srcs=[ap(src)],
                                                               dsts=[ap(dst_of(d)) for d in range(1, N)])], local_sem=T.sem[loc]), None, [src])
        ops[-1]["remote"] = True
        return bin(m).count("1")

    def aside(part):
        k = len(ops)
        part()
        l = ops[k:]
        del ops[k:]
        return l

    def weave(*parts):
        lists = [aside(p) for p in parts]
        while any(lists):
            for l in lists:
                if l:
                    ops.append(l.pop(0))

    ncol = [0]

    def column(terms, const=0.0):
        o = f("col", ncol[0], ncol[0] + 1); ncol[0] += 1
        prev = const
        for r, w in terms:
            act(o, f("E", r, r + 1), scale=float(w), bias=prev)
            prev = o
        return o

    def ymat(name, w):
        act(b_(name, 0, 144, 16), f("G9", 0, 9), scale=w)

    def c_(k):
        return f("cl", CL[k], CL[k] + 1)

    XO = R("xw", SH, SH + V_)
    XS, XN = R("xw", 0, 3072), R("xw", SH, SH + 4096)
    NBT, SF, PL = R("nbt", 0, 3072), R("sf", 0, 3072), R("pl", 0, PLW)
    BD, BG, BS = R("bag", 0, DZ + 256), R("bag", 0, DZ + 512), R("bag", 0, BAGW)
    F, YP = R("ff", 0, 3072), R("ypb", 0, PLW)
    HI, LO = f("JVf", 0, 128), f("JVf", 256, 384)
    NH, NL = f("PUf", 0, 160), f("PUf", 160, 320)
    ZERO = R("xw", 0, SH)
    K = {}

    mset(b_("ONE"), 1.0)
    mset(f("one"), 1.0)
    mset(i_("ts"), 0)
    dma(i_("plc"), T.plc[:])
    dma(R("xw", SH, SH + 512), T.x[:, 0:512])
    dma(R("ai", AT["ai"]["ts"], AT["ai"]["ts"] + 3, 1, 0, 16), T.th[:])
    dma(R("ai", AT["ai"]["ts"] + 4, AT["ai"]["ts"] + 8, 1, 0, 16), T.sd[:])
    dma(i_("n0"), T.nb[0:128:16, :])
    act(b_("CS", 0, 528), b_("ONE"), AF.Silu, scale=65.0)
    act(b_("CS", 1024, 1040), b_("ONE", 0, 16), scale=65.0)
    iota(i_("pi", 0, 1), [[0, 1]], 0, 1)
    iota(LO, [[0, 2], [1, 64]])
    iota(HI, [[64, 2], [0, 64]])
    mset(ZERO, 0.0)
    dma(R("nbt", SH, SH + V_), T.nb[:])
    for k in range(1, 6):
        dma(R("ff", k * 512, (k + 1) * 512), ZERO)
    dma(R("xw", SH + 512, SH + V_), T.x[:, 512:V_])
    for k, nme in enumerate(("Yt", "YJ")):
        dma(R("ab", AT["ab"][nme], AT["ab"][nme] + 432 - 32 * k), sub(ZERO, 0, 432 - 32 * k))
    dma(R("ab", AT["ab"]["TR1b"], AT["ab"]["BO"]), sub(ZERO, 0, 256))
    ts(i_("pi", 1, 2), i_("pi", 0, 1), 15, AL.bitwise_and)
    ts(i_("pi", 2, 3), i_("pi", 0, 1), 3, AL.bitwise_and)
    cp(f("rcol", 0, 2), i_("pi", 1, 3))
    ts(f("E"), sub(LO, 0, 16), f("rcol", 0, 1), AL.is_equal)
    ts(f("BK", 0, 24), sub(LO, 0, 24), f("E", 0, 1), AL.mult, 128.0, AL.mult)
    ts(f("blk"), LO, 32.0, AL.add, f("E", 1, 2), AL.mult)
    ts(HI, HI, f("E", 0, 1), AL.mult)
    tt(R("sf", 0, 128), f("blk"), HI, AL.add)

    def sfk(k, n):
        ts(R("sf", k * 128, (k + n) * 128), R("sf", 0, n * 128), f("BK", k, k + 1), AL.add)

    def bags(a, e):
        act(ind(R("bag", 0, DZ), u("plu", (a - 4) * 8, (e - 4) * 8)), R("sf", a * 128, e * 128), AF.Silu)
    sfk(4, 1); sfk(1, 1); sfk(5, 1)
    cp(u("plu"), i_("plc"))
    bags(4, 6)
    mset(R("ab", AT["ab"]["G2"], AT["ab"]["Yt"]), 0.0)
    for a, e in ((6, 12), (12, 24)):
        for k in range(a, e, 2):
            sfk(k, 2)
        bags(a, e)
        if a == 6:
            mset(R("af", AT["af"]["AD"], AT["af"]["S32"] + 144), 0.0)
    sfk(2, 2)
    asel(f("G9", 0, 9), f("one", 0, 9), [[-16, 9]], AL.is_ge, 16, 1)
    asel(f("G9", 0, 9), f("G9", 0, 9), [[16, 9]], AL.is_ge, -1, -1)
    asel(b_("BO"), f("one"), [[-16, 8], [0, 16]], AL.is_ge, 0, 1)
    asel(b_("BO"), b_("BO"), [[16, 8], [0, 16]], AL.is_ge, 15, -1)
    ne = send(R("xw", SH, SH + 512), lambda d: R("xw", 3072 + (d - 1) * 512, 3072 + d * 512), "gin", "sent0")
    ext("gin", ne * (N - 1), R("xw", 3072, 4608))
    put(f("AD"), [[-16, 8], [1000, 8], [0, 2]], 0, 1.0)
    put(f("A0"), [[-16, 8], [1000, 2], [0, 8]], -1000, 52.0)
    put(f("AD"), [[-16, 8], [1000, 8], [0, 2]], -1004, 1.0)
    put(f("A0"), [[-16, 8], [1000, 4], [0, 4]], -1000, 26.0)
    put(f("AD"), [[-16, 8], [1000, 4], [0, 4]], -1008, 0.5)
    put(f("A0"), [[-16, 8], [1000, 4], [0, 4]], 0, 13.0)
    put(f("AD"), [[-16, 8], [1000, 2], [0, 8]], -1012, 0.25)
    iota(f("JT"), [[1, 256]])
    iota(f("JW"), [[16, 32]])
    asel(b_("ID"), f("one"), [[-1, 128]], AL.is_equal, 0, 1)
    iota(R("nbt", 0, SH), [[0, SH]])

    def sizes():
        for c in range(1, 4):
            ts(b_("fl", (c + 1) * 160, (c + 2) * 160), i_("plc"), float(V_ * c), AL.is_ge, 32.0, AL.mult)
        for c in range(1, 4):
            red(f("G4", c - 1, c), b_("fl", (c + 1) * 160, (c + 2) * 160))
        cp(b_("cnt", 0, 3), f("G4", 0, 3))
        mm(P(6, 496, 499), b_("BO"), b_("cnt", 0, 3), True, True)

    def seeds():
        ts(i_("tsh"), i_("ts"), 0x1FF00, AL.bitwise_and)
        ts(i_("tsl"), i_("ts"), 255, AL.bitwise_and)
        cp(b_("th"), i_("tsh")); cp(b_("tl"), i_("tsl"))
        mm(P(6, 480, 496), b_("BO"), b_("th"), True, False); mm(P(6, 480, 496), b_("BO"), b_("tl"), False, True)

    def columns():
        for k, v in enumerate((2.0, 4.0, 8.0)):
            ts(f("G3", k, k + 1), f("rcol", 0, 1), v, AL.is_ge)
        ts(c_("c"), f("rcol", 0, 1), f("rcol", 1, 2), AL.subtract, 0.25, AL.mult)
        ts(c_("cD"), f("G3", 0, 1), f("G3", 1, 2), AL.add, f("G3", 2, 3), AL.add)
        ts(c_("km"), f("G3", 2, 3), 2.0, AL.mult, f("G3", 1, 2), AL.add)
        ts(f("EQ", 0, 4), sub(LO, 0, 4), c_("c"), AL.is_equal)
        ts(f("EQ", 4, 8), sub(LO, 0, 4), c_("cD"), AL.is_equal)
        ts(c_("p0"), c_("km"), f("G3", 0, 1), AL.add, 2.0, AL.mult)
        ts(c_("k"), c_("km"), 1.0, AL.add)
        tt(f("Aa", 0, 3), f("EQ", 1, 4), f("EQ", 0, 3), AL.subtract)
        ts(c_("c25"), c_("cD"), float(V_), AL.mult)
        ts(c_("pp"), c_("p0"), -1.0, AL.mult, f("rcol", 0, 1), AL.add)
        ts(c_("iv0"), c_("p0"), 16.0, AL.mult, float(DZ), AL.add)
        ts(c_("pp"), c_("pp"), 16.0, AL.mult)
        ts(c_("ivc"), c_("iv0"), c_("c25"), AL.subtract)
        ts(f("JH"), sub(LO, 0, 16), c_("pp"), AL.add, 128.0, AL.mult)
    weave(sizes, seeds, columns)

    def first_sizes():
        tt(f("t4", 0, 3), P(6, 496, 499), f("Aa", 0, 3), AL.mult)
        red(c_("t"), f("t4", 0, 3))
        ts(c_("t"), c_("t"), 1.0 / 32, AL.mult)
        ts(c_("n"), f("EQ", 0, 1), float(V_), AL.mult, c_("t"), AL.add)

    def first_seeds():
        cp(f("TS"), P(6, 480, 496))
        tt(f("t4", 4, 8), f("TS", 4, 8), f("EQ", 4, 8), AL.mult)
        red(c_("sd"), f("t4", 4, 8))
        ts(c_("sd0"), c_("sd"), c_("k"), AL.mult)

    def first_fields():
        ts(i_("b"), i_("n0"), 0xFC0, AL.bitwise_and)
        ts(i_("c"), i_("n0"), 63, AL.bitwise_and)
        ts(NH, i_("b"), float(SH), AL.add); ts(NL, i_("c"), 32.0, AL.add)
    weave(first_sizes, first_seeds, first_fields)

    def draw_sizes():
        mm(P(5, 496, 497), f("AD"), c_("n"), True, True)
        mm(P(5, 497, 498), f("A0"), c_("n"), True, True)

    def draw_a(t):
        ts(i_("xi", 0, 1), P(5, 497, 498), c_("sd%d" % t), AL.add)
        ts(c_("npp"), P(5, 496, 497), 32.0, AL.max)
        ts(i_("bi", 0, 1), i_("xi", 0, 1), 127, AL.bitwise_and)
        ts(c_("inv"), P(5, 496, 497), 32.0, AL.is_lt, c_("ivc"), AL.mult)
        cp(c_("bk"), i_("bi", 0, 1))

    def draw_b():
        ts(i_("pr"), f("JH"), c_("bk"), AL.add, c_("npp"), AL.mult)
        ts(i_("sh"), i_("pr"), 12, AL.arith_shift_right)
        ts(u("DP"), i_("sh"), c_("inv"), AL.add, c_("c25"), AL.add)

    def final_s(a, e):
        act(sub(YP, a, e), sub(PL, a, e), bias=12582912.0)
        act(sub(YP, a, e), sub(YP, a, e), bias=-12582912.0 - 33.0)

    def final_v(a, e):
        ts(sub(YP, a, e), sub(PL, a, e), 12582912.0, AL.add, 12582912.0 + 33.0, AL.subtract)

    def leavers():
        tt(f("tg"), P(0, 288, 320), f("dP"), AL.min)
        ts(u("POF"), f("tg"), 16384.0 - 32.0, AL.add)

    def piece(r):
        return P((0, 7, 5, 6, 2)[r // 3], (r % 3) * 160, (r % 3 + 1) * 160) if r < 15 else P(1, 256, 416)

    def spread(r0, r1):
        for r in range(r0, r1):
            for k, row in enumerate((2, 3, 7, 9, 11)):
                mm(piece(r), b_("Z", r * 144 + 16 - row, r * 144 + 144 - row), b_("fl", k * 160, (k + 1) * 160), k == 0, k == 4)

    def fetch(r0, r1):
        for r in range(r0, r1):
            act(R("pl", SH + r, 3072, 16), piece(r), bias=K["c33"])

    def tables_z():
        cp(b_("G2", 0, 144, 16), f("G9", 0, 9)); cp(b_("G2", 1, 144, 16), f("G9", 0, 9))
        ts(i_("d"), i_("plc"), 0x3FC0, AL.bitwise_and)
        ts(i_("e"), i_("plc"), 63, AL.bitwise_and)
        for r in range(ZG):
            asel(b_("Z", r * 144, (r + 1) * 144), b_("G2"), [[-16, 9], [0, 16]], AL.is_equal, 16 - r, 1)
        cp(b_("fl", 0, 160), i_("d"))
        cp(b_("fl", 160, 320), i_("e"))

    def tables_z2():
        for r in range(ZG, 16):
            act(b_("Z", r * 144, (r + 1) * 144), b_("G2"), scale=f("E", r, r + 1))

    def tables_draw():
        ts(c_("s01"), f("rcol", 0, 1), 2.0, AL.is_lt)
        ts(c_("s03"), f("rcol", 0, 1), 4.0, AL.is_lt)
        cp(R("bag", DZ, DZ + 256), R("sf", 0, 256))
        ts(b_("Ys", 0, 144, 16), f("G9", 0, 9), c_("s03"), AL.mult)
        ts(c_("s23"), c_("s03"), c_("s01"), AL.subtract)
        ts(f("JT"), f("JT"), f("E", 4, 5), AL.mult)
        act(b_("SEL", 0, 64), R("sf", 2048, 2112))
        dma(R("sf", SH, 3072, 1, 2, 16), NH); dma(R("sf", SH, 3072, 1, 3, 16), NL)
        for r in range(2):
            dma(R("sf", 0, 256, 1, 2 + r, 16), R("bag", DZ, DZ + 256, 1, r, 16))

    def stand_ins():
        act(b_("SFb"), R("sf", 0, 512), scale=c_("s01"))
        act(R("bag", DZ + 256, DZ + 512), R("sf", 256, 512))
        for t in range(1, RO):
            act(b_("SEL", t * 336, t * 336 + 64), R("sf", 2048, 2112), scale=c_("s01"))
        for t in range(RO):
            dma(b_("SL", t * 1024, t * 1024 + 512), b_("SFb"))

    def tables_move():
        ts(f("JW"), f("JW"), f("rcol", 0, 1), AL.add)
        K["k64"] = column([(1, 64)])
        ts(c_("t"), f("E", 1, 2), 999.0, AL.mult, c_("s03"), AL.add)
        ts(f("c65"), f("JW", 0, 16), 65.0, AL.add)
        ts(b_("Yr", 0, 144, 16), f("G9", 0, 9), c_("t"), AL.mult)
        act(b_("VD"), b_("ONE", 0, 256), scale=c_("s01"))
        act(b_("ID16"), b_("ID"), scale=0.0625); act(b_("IDm"), b_("ID"), scale=-1.0)
        mset(b_("C75"), -7.5)
        ts(c_("y"), c_("s03"), 1.0 / 8192, AL.mult, f("E", 4, 5), AL.add)
        ymat("Yj", c_("y"))
        ts(R("d0", 0, 512), b_("ONE", 0, 512), f("E", 3, 4), AL.subtract)
        act(b_("VN"), b_("ONE", 0, 256), scale=c_("s23"))
        for k in range(1, 5):
            dma(R("d0", k * 512, (k + 1) * 512), R("d0", 0, 512))
        dma(b_("d0u"), ZERO)
        dma(b_("ZR"), ZERO)
        dma(R("ab", AT["ab"]["d0u"], AT["ab"]["d0u"] + 512, 1, 14, 16), R("ab", AT["ab"]["ONE"], AT["ab"]["ONE"] + 512, 1, 14, 16))

    def tables_sort():
        def one():
            K["c33"] = column([(3, 33), (4, 33), (5, 32)])

        def two():
            ymat("Yk", column([(3, 2048), (0, 1), (2, 1)]))

        def three():
            act(R("ct", 0, SH), b_("ONE", 0, 512), scale=column([(3, 2)]))
            act(c_("c33"), c_("c"), scale=float(V_), bias=33.0)
            act(f("c513"), f("JW"), bias=513.0)
        weave(one, two, three)
        iota(b_("cD"), [[-2048, 2], [0, 16]])
        for k in range(3 * RO):
            iota(f("land", 80 * k + 68, 80 * k + 80), [[0, 12]])

    def thresholds():
        red(f("T3", 0, 1), f("TS", 0, 3), AL.min)
        red(f("T3", 2, 3), f("TS", 0, 3), AL.max)
        red(c_("t"), f("TS", 0, 3))
        ts(f("T3", 1, 2), c_("t"), f("T3", 0, 1), AL.subtract, f("T3", 2, 3), AL.subtract)

    def masks():
        def rows(k):
            K["m%d" % k] = column([(4 * k + 2, 1), (4 * k + 5, 1), (4 * k + 7, 1)])
        weave(lambda: rows(0), lambda: rows(1), lambda: rows(2))
        act(c_("thc"), f("E", 14, 15), scale=1e9, bias=float(BIG))

    def thresholds3():
        for k in range(3):
            ts(c_("thc"), K["m%d" % k], f("T3", k, k + 1), AL.mult, c_("thc"), AL.add)

    def spare_ghosts():
        for d in range(N - 1):
            ts(u("GO", 5 * d + 4, 5 * d + 5), f("rcol", 0, 1), 1600.0 + 512 * d, AL.add)

    def tables_q():
        cp(h_("ID"), b_("ID"))
        ts(h_("nd"), f("IQ"), -1.0, AL.mult, -1024.0, AL.add)
        ts(h_("dW"), f("JW"), 1024.0, AL.add); cp(h_("JW"), f("JW")); ts(h_("nJ"), f("JW"), -1.0, AL.mult)

    def tables_g1():
        iota(f("IQ"), [[4, 128]])
        put(b_("TR3"), [[-16, 8], [1000, 16]], -2000, 1.0)
        put(b_("TR3"), [[-16, 8], [1000, 16]], -4001, 1.0)
        iota(R("pl", 0, SH), [[0, SH]])
        for row in (2, 4):
            put(b_("YP"), [[-16, 9], [0, 4], [1000, 4]], 16 - row, 1.0)
        put(b_("PEN"), [[-16, 8], [-2, 4], [0, 4]], -5, BIG / 32)
        put(b_("PEN"), [[-16, 8], [-2, 4], [0, 4]], -7, -BIG / 32)
        asel(b_("PEN"), b_("PEN"), [[0, 32], [1, 4]], AL.not_equal, -3, 0)
        put(b_("PEN"), [[-16, 8], [0, 4], [1000, 4]], -3005, BIG / 32)

    def tables_g2():
        q = [[-16, 9], [-4, 4], [1000, 4]]
        for row, w in ((0, 1.0), (1, -1.0), (2, 1.0)):
            put(b_("YL"), q, 16 - row, w)
        put(b_("YJ"), q, 16 - 7, -1.0)
        asel(b_("YJ"), b_("YJ"), [[0, 9], [1, 4], [0, 4]], AL.not_equal, -3, 0)
        for row, w in ((3, 1.0), (1, -1.0), (2, 1.0)):
            put(b_("YJ"), q, 16 - row, w)
        asel(b_("Ale"), b_("BO"), [[16, 8], [4, 4], [0, 4]], AL.is_ge, 3, -1)
        asel(b_("Alt"), b_("BO"), [[16, 8], [4, 4], [0, 4]], AL.is_ge, -1, -1)
        asel(b_("Aeq"), b_("Ale"), [[-16, 8], [-4, 4], [0, 4]], AL.is_ge, 0, 1)
        asel(b_("MB"), b_("BOm"), [[-1, 128]], AL.is_gt, 0, 1)
        asel(b_("MB"), b_("MB"), [[16, 8], [4, 4], [0, 4]], AL.is_ge, 3, -1)
        put(b_("MB"), [[-1, 128]], 0, 16384.0)
        for c in range(4):
            put(f("S32"), [[-16, 9], [1000, 4], [-1, 4]], 16 - 4 * c, 1.0)

    def tables_g3():
        one, two = [[-16, 8], [1000, 16]], [[-16, 8], [1000, 8], [0, 2]]
        asel(b_("TR2"), b_("ID"), [[0, 8], [1, 16]], AL.not_equal, -3, 0)
        for k in range(4):
            put(b_("TR1b"), one, -1000 * (5 + 2 * k) - 4 * k - 3, 32.0)
            if k < 2:
                put(b_("TR2"), one, -3000 - 2 - 2 * k, 1.0)
                put(b_("TR1"), one, -1000 * (3 + k) - 1, 1.0)
        put(b_("TR1"), two, -1000, 1.0)
        for row in (7, 11, 15):
            put(b_("TR1b"), two, -1000 - row, float(V_))

    def tables_s1():
        for nme, w in (("BOm", -1.0), ("BO2", 2.0), ("BOm16", -16.0)):
            act(b_(nme), b_("BO"), scale=w)

    def tables_a(t):
        act(R("tt", t * 1536, t * 1536 + 512), b_("SFb"), bias=K["f2"])
        act(R("tt", t * 1536 + 512, t * 1536 + 1024), P(7, 0, 512), bias=K["hd"])

    def tables_b():
        K["yu"] = column([(15, -544), (14, 1)], c_("s01"))
        K["s24"] = column([(2, 1), (4, 1)])
        K["f2"] = column([(14, 1), (15, 1)])
        K["hd"] = column([(2, DZ + 576)])
        ymat("Yt", K["s24"])
        iota(b_("cB"), [[0, 128]], -16384)
        act(c_("sb"), c_("c"), scale=float(V_), bias=-16384.0)
        act(f("dB"), f("JW"), bias=float(DZ + 576 - 16383))
        act(f("dP"), f("JW"), bias=float(3072 + 32 - 16384))

    def tables_c():
        cp(h_("S"), f("S32"))
        act(b_("SB"), f("S32"), scale=c_("sb"))
        act(b_("SG"), f("S32"), scale=-16384.0)
        for k in range(1, RO):
            act(c_("sd%d" % k), c_("k"), scale=41.0 * k, bias=c_("sd0"))

    def tables_c2():
        mset(R("ah", AT["ah"]["Yu"], AT["ah"]["S"]), 0.0)
        ts(h_("Yu", 0, 144, 16), f("G9", 0, 9), K["yu"], AL.mult)
        ts(h_("B14"), b_("BO"), f("E", 14, 15), AL.mult)
        ts(h_("Yv", 0, 144, 16), f("G9", 0, 9), f("E", 15, 16), AL.mult, -16384.0, AL.mult)

    draw_sizes()
    weave(lambda: (draw_a(0), draw_b()), tables_draw, tables_z)
    for t in range(RO):
        last = t == RO - 1
        SEL, SL = b_("SEL", t * 336, (t + 1) * 336), b_("SL", t * 1024, (t + 1) * 1024)
        TT = R("tt", t * 1536, (t + 1) * 1536)
        DW, N0W, DF, N0F = u("U0", 0, 16), u("U0", 16, 32), b_("UF", 0, 256), b_("UF", 256, 512)
        msg = f("msg", t * 80, t * 80 + 68)
        tt(DF, ind(BD, u("DP")), f("JT"), AL.add)
        conv(P(3, 0, 16), DF, "Ys", 256)
        if t == 0:
            spread(0, SPR[0])
            tables_move()
        else:
            leavers()
        ts(DW, P(3, 0, 16), -32.0, AL.add)
        cp(u("NBD"), ind(NBT, DW))
        if t:
            act(N0F, ind(SF, DW), scale=c_("s23"))
        act(b_("XM"), ind(XS, DW), bias=-192.0)
        for a, e in MOVE_S:
            act(R("gg", a * 16, e * 16), ind(XN, u("NBD", a, e)))

        def move_sum(a, e):
            o = P(1 if a < MOVE_S[2][0] else 2, a, e)
            mm(o, b_("IDm"), b_("XM", a, e), True, False)
            mm(o, b_("ID16"), b_("C75", 0, e - a), False, False)
            for j in range(16):
                mm(o, b_("ID16"), R("gg", a * 16 + j, e * 16, 16), False, j == 15)
        cp(ind(F, DW), b_("VD"))
        ts(u("DWc"), P(3, 0, 16), -32.0, AL.add, 1024.0, AL.min)
        scan(b_("CS", 512, 1024), sub(F, 512, 1024), b_("CS", 0, 512), 0.0, AL.add, AL.min)
        if t == 0:
            ts(N0F, ind(SF, DW), c_("s23"), AL.mult)
        ts(b_("RS"), ind(b_("CS"), u("DWc")), K["k64"], AL.subtract, 0.0, AL.max)
        conv(P(4, 0, 32), R("ab", AT["ab"]["UF"] + 256, AT["ab"]["UF"] + 768), "Yr", 512)
        move_sum(*MOVE_S[0])
        a, e = MOVE_V[0]
        cp(R("gg", a * 16, e * 16), ind(XN, u("NBD", a, e)))
        tt(f("t16"), P(4, 16, 32), f("c65"), AL.min)
        ts(N0W, P(4, 0, 16), -32.0, AL.add)
        ts(u("SW"), f("t16"), -1.0, AL.add)
        cp(ind(SEL, u("SW")), DF)
        move_sum(*MOVE_V[0])
        move_sum(*MOVE_S[1])
        conv(P(3, 64, 68), sub(SEL, 0, 64), "Yj", 64)
        a, e = MOVE_V[1]
        cp(R("gg", a * 16, e * 16), ind(XN, u("NBD", a, e)))
        if t == 0:
            stand_ins()
            tables_sort()
        a = MOVE_S[2][0]
        move_sum(a, 256)
        cp(ind(F, N0W), b_("VN"))
        cp(u("JWu", 0, 4), P(3, 64, 68))
        ts(b_("DL", 0, a), P(1, 0, a), 189.0, AL.max, 195.0, AL.min)
        ts(f("t16", 0, 4), u("JWu", 0, 4), -1.0, AL.mult, (-32.0 - SH) / 8192, AL.add)
        cp(b_("XL"), ind(b_("XM"), u("JWu", 0, 4)))
        tt(sub(msg, 64, 68), P(3, 64, 68), f("t16", 0, 4), AL.add)
        ts(b_("DL", a, 256), P(2, a, 256), 189.0, AL.max, 195.0, AL.min)
        tt(sub(msg, 0, 64), ind(b_("DL"), u("JWu", 0, 4)), b_("XL"), AL.add)
        ne = send(msg, lambda d, t=t: f("land", (3 * t + d - 1) * 80, (3 * t + d - 1) * 80 + 68), "arr%d" % t, "sent")
        if t > 0:
            act(f("JVf"), P(6, 0, 512))
            act(ind(PL, u("POF")), f("JVf"), AF.Silu)
        else:
            tables_g1()
            spread(SPR[0], SPR[1])
            fetch(0, SPR[0] - 1)
            masks()
            fetch(SPR[0] - 1, SPR[0])
            tables_z2()
        scan(R("ct", SH, 3072), R("d0", 0, V_), sub(F, SH, 3072), 0.0, AL.mult, AL.add)
        act(b_("RK", 0, 256), ind(R("ct", 0, 3072), DW))
        cp(b_("RK", 256, 512), ind(R("ct", 0, 3072), N0W))
        conv(P(3, 32, 64), b_("RK"), "Yk", 512, False)
        mm(P(3, 32, 64), b_("ID"), b_("cD"), False, True)
        if t == 0:
            fetch(SPR[0], SPR[1])
            act(f("IQ"), f("IQ"), bias=f("rcol", 1, 2))
            weave(tables_s1, tables_b)
            spread(SPR[1], SPR[2])
            fetch(SPR[1], SPR[2])
            ext("sent0", ne, R("xw", SH, SH + 512))
        tt(ind(XS, DW), b_("DL"), b_("XM"), AL.add)
        if last:
            dma(T.yx[:], XO)
        if t == 0:
            thresholds()
        tt(f("t32b"), P(3, 32, 64), f("c513"), AL.min)
        act(c_("NP"), c_("n"), bias=c_("c33"))
        act(c_("fn"), c_("n"), scale=-1.0, bias=float(V_))
        act(c_("nNP"), c_("NP"), scale=-1.0)
        ts(u("RW"), f("t32b"), -1.0, AL.add)
        if last:
            final_s(SH, 2048)
        if t == 1:
            mm(P(7, 0, 512), b_("TR3"), b_("SFb"), True, True)
            tables_a(1)
            dma(R("tt", 3072, 4096), R("tt", 1536, 2560))
        cp(ind(SL, u("RW")), b_("UF"))
        conv(P(4, 32, 64), sub(SL, 0, 512), "Ys", 512)
        if t == 0:
            spread(SPR[2], 16)
            weave(thresholds3, spare_ghosts, tables_q)
            tables_g2()
            tables_g3()
        if not last:
            for k in range(1, 6):
                dma(R("ff", k * 512, (k + 1) * 512), b_("ZR"))
        ts(u("UW"), P(4, 32, 64), -32.0, AL.add)
        act(b_("XU"), ind(XS, u("UW")))
        cp(u("NBU", 0, NBU1), ind(NBT, u("UW", 0, NBU1 // 16)))
        if t == 0:
            fetch(SPR[2], 16)
        act(b_("PU"), ind(PL, u("UW")))
        ext("arr%d" % t, ne * (N - 1), f("land", 3 * t * 80, 3 * (t + 1) * 80))
        for d in range(1, N):
            o = (3 * t + d - 1) * 80
            ts(u("GO", 5 * (d - 1), 5 * d - 1), f("land", o + 64, o + 68), 8192.0, AL.mult, 512.0 * (d - 1), AL.add)
        cp(ind(R("xw", 3072, 5728), u("GO", 0, 15)), f("land", 3 * t * 80, 3 * (t + 1) * 80))
        mm(P(0, 0, 512), b_("ID"), b_("XU"), True, True)
        quad(P(5, 0, 128), b_("PU"), "YP", 0, 512)
        quad(P(5, 128, 256), b_("PU"), "YP", 0, 512, (h_("ID"), h_("nd")))
        mm(P(6, 0, 128), h_("ID"), h_("nd"), True, False)
        if t == 0:
            mm(P(7, 0, 512), b_("TR3"), b_("SFb"), True, True)
        at = 0
        for ci, (ns, nv) in enumerate(CHUNKS):
            if ci == 0:
                cp(R("gg", 0, nv * 16), ind(XN, u("NBU", 0, nv)))
                cp(u("NBU", NBU1, 512), ind(NBT, u("UW", NBU1 // 16, 32)))
            if ns:
                act(R("gg", at * 16, (at + ns) * 16), ind(XN, u("NBU", at, at + ns)))
            at += ns + nv

        def classes(a, n):
            quad(P(3, 256 + a // 4, 256 + (a + n) // 4), b_("B"), "YL", a, n)
            quad(P(4, 256 + a // 4, 256 + (a + n) // 4), b_("B"), "YJ", a, n)
        at = 0
        for ci, (ns, nv) in enumerate(CHUNKS):
            n = ns + nv
            o = P(1 + ci % 2, 0, n)
            mo = ci % 2 * 2048
            mm(o, b_("BOm16"), b_("XU", at, at + n), True, False)
            mm(o, b_("PEN"), b_("PU", at, at + n), False, False)
            for k in range(16):
                mm(o, b_("BOm"), R("gg", at * 16 + k, (at + n) * 16, 16), False, False)
            for k in range(16):
                tt(R("mm", mo + k * n, mo + (k + 1) * n), R("gg", at * 16 + k, (at + n) * 16, 16), P(0, at, at + n), AL.max)
                mm(o, b_("BO2"), R("mm", mo + k * n, mo + (k + 1) * n), False, k == 15)
                if ci > 0 and k == BAT:
                    ts(b_("B", at - pn, at), P(1 + (ci - 1) % 2, 0, pn), c_("thc"), AL.is_ge)
                    if ci == len(CHUNKS) - 2:
                        classes(0, at)
                        done = at
            at += n; pn = n
        act(f("dq"), P(5, 0, 128), scale=-1.0, bias=c_("NP"))
        act(f("qq"), P(5, 128, 256), bias=c_("nNP"))
        if t == 0:
            tables_a(0)
        act(f("PUf"), b_("PU"))
        if not last:
            act(f("SLf"), sub(SL, 0, 512), scale=c_("s03"))
        if t == 0:
            tables_c()
        ts(b_("B", at - pn, at), P(1 + (len(CHUNKS) - 1) % 2, 0, pn), c_("thc"), AL.is_ge)
        classes(done, at - done)
        LV, JN = P(3, 256, 384), P(4, 256, 384)
        scan(b_("SLV"), b_("ONE", 0, 128), LV, 0.0, AL.mult, AL.add)
        for k, A in enumerate(("Aeq", "Ale", "Alt")):
            mm(P(5, 488 + k, 489 + k), b_(A), b_("SLV", 127, 128), True, True)
        cm, cMn, cM = P(5, 488, 489), P(5, 489, 490), P(5, 490, 491)
        tt(h_("dl"), LV, f("dq"), AL.mult)
        mm(P(2, 0, 1), b_("Aeq"), b_("SLV", 127, 128), True, True)
        tt(h_("q"), LV, f("qq"), AL.mult)
        act(b_("JN"), JN)
        act(c_("L"), P(2, 0, 1), scale=-1.0, bias=c_("n"))
        ts(b_("HF"), h_("dl"), cm, AL.is_gt)
        mm(P(6, 0, 128), b_("MB"), b_("HF"), False, False)
        scan(b_("SJ"), b_("ONE", 0, 128), b_("JN"), 0.0, AL.mult, AL.add)
        scan(b_("SHF"), b_("ONE", 0, 128), b_("HF"), 0.0, AL.mult, AL.add)
        mm(P(6, 0, 128), b_("Aeq"), b_("SHF"), False, True)
        mm(P(6, 128, 129), b_("Alt"), b_("SHF", 127, 128), True, True)
        mm(P(0, 0, 128), b_("ID"), b_("cB"), True, False)
        mm(P(0, 0, 128), b_("MB"), b_("JN"), False, False)
        mm(P(0, 0, 128), b_("Aeq"), b_("SJ"), False, True)
        mm(P(0, 128, 129), b_("Aeq"), b_("SJ", 127, 128), True, True)
        ts(h_("mk"), h_("q"), cMn, AL.add, 0.0, AL.min)
        ts(P(1, 128, 256), f("IQ"), cMn, AL.is_ge, c_("fn"), AL.mult)
        ts(P(6, 256, 384), P(6, 0, 128), P(6, 128, 129), AL.add, 511.0 - 16384.0, AL.add)
        ts(f("s1"), f("IQ"), cM, AL.is_ge, c_("L"), AL.mult)
        tt(h_("fin"), P(6, 256, 384), h_("mk"), AL.max)
        mm(P(7, 0, 32), h_("ID"), h_("dW"), True, False)
        fold(P(7, 0, 32), h_, "S", h_("fin"), False, True)
        tt(f("ss"), P(1, 128, 256), f("s1"), AL.add)
        act(f("X"), P(0, 0, 128), AF.Relu, bias=c_("L"))
        if not last:
            act(c_("n"), P(0, 128, 129), bias=c_("L"))
        ts(u("SLOT"), P(7, 0, 32), 0.0, AL.add)
        act(ind(TT, u("SLOT")), f("PUf"), AF.Silu)
        if t == 0:
            tables_c2()

        def new_places():
            mm(P(6, 0, 512), b_("TR1b"), b_("B"), True, False)
            mm(P(6, 0, 512), b_("TR1"), b_("JV"), False, True)
            conv(P(0, 288, 320), sub(SL, 0, 512), "Ys", 512, False)
            fold(P(0, 288, 320), b_, "SG", b_("JN"), False, True)
        if last:
            final_v(2048, 2560)
            fold(P(2, 256, 288), f, "S32", f("X"), True, True)
            ts(u("PN"), P(2, 256, 288), 0.0, AL.add)
            cp(b_("JV"), ind(SF, u("PN")))
        mm(P(1, 0, 32), h_("ID"), h_("JW"), True, False)
        fold(P(1, 0, 32), f, "S32", f("ss"), False, True)
        if last:
            new_places()
        else:
            fold(P(2, 32, 64), f, "S32", f("X"), True, False)
            fold(P(2, 32, 64), b_, "SB", b_("JN"), False, True)
            draw_sizes()
            fold(P(0, 256, 288), f, "S32", f("X"), True, True)
        ts(u("TP"), P(1, 0, 32), 0.0, AL.add)
        if last:
            act(b_("TSb"), ind(BG, u("TP")))
            act(f("JVf"), P(6, 0, 512), bias=-33.0)
            scan(h_("CU"), b_("d0u"), sub(TT, 0, 512), 0.0, AL.mult, AL.add)
            mm(P(3, 384, 416), h_("ID"), h_("nJ"), True, False)
            conv(P(3, 384, 416), h_("CU"), "Yu", 512, True, False, h_)
            final_v(2560, 3072)
            leavers()
            ts(u("IDX"), P(3, 384, 416), 1023.0, AL.add)
            act(b_("TG"), ind(sub(TT, 0, 1024), u("IDX")))
            cp(ind(YP, u("POF")), f("JVf"))
            conv(P(4, 384, 416), h_("CU"), "Yv", 512, False, True, h_)
            conv(P(4, 384, 416), b_("TSb"), "Ys", 512, True, False)
            mm(P(7, 0, 512), b_("TR2"), b_("TG"), True, True)
            act(f("TGf"), P(7, 0, 512), bias=-33.0)
            tt(f("tg"), P(4, 384, 416), f("dP"), AL.min)
            ts(u("PLO"), f("tg"), 16384.0 - 32.0, AL.add)
            cp(ind(YP, u("PLO")), f("TGf"))
            dma(T.yp[:], R("ypb", SH, 3072, 1, 3, 16))
        else:
            cp(b_("TSb"), ind(BG, u("TP")))
            tt(f("tc"), P(2, 32, 64), f("dB"), AL.min)
            ts(u("BJ"), f("tc"), 16383.0, AL.add)
            act(ind(BS, u("BJ")), f("SLf"), AF.Silu)
            conv(P(2, 384, 416), b_("TSb"), "Ys", 512)
            for h, bank in ((0, 3), (1, 1)):
                a = 256 * h
                scan(h_("CU", a, a + 256), b_("d0u", 0, 256), sub(TT, a, a + 256), 0.0, AL.mult, AL.add)
                if h:
                    mm(P(bank, 400, 401), h_("B14"), h_("CU", 255, 256), True, True)
                mm(P(bank, 384, 400), h_("ID"), h_("nJ", 16 * h, 16 * h + 16), True, False)
                conv(P(bank, 384, 400), h_("CU", a, a + 256), "Yu", 256, True, False, h_)
            ts(u("PN"), P(0, 256, 288), 0.0, AL.add)
            act(b_("JV"), ind(SF, u("PN")))
            da, db = aside(lambda: draw_a(t + 1)), aside(draw_b)
            ops.extend(da[:2])
            for h, bank in ((0, 3), (1, 1)):
                a = 256 * h
                if h:
                    ts(u("IDX", 16, 32), P(bank, 384, 400), 1023.0, AL.add, P(bank, 400, 401), AL.add)
                else:
                    ts(u("IDX", 0, 16), P(bank, 384, 400), 1023.0, AL.add)
                ops.extend(da[2:4] if h == 0 else da[4:])
                cp(b_("TG", a, a + 256), ind(sub(TT, 0, 1024), u("IDX", 16 * h, 16 * h + 16)))
                conv(P(5 - h, 32, 48), b_("TG", a, a + 256), "Yt", 256)
            mm(P(7, 0, 512), b_("TR2"), b_("TG"), True, True)
            new_places()
            ops.append(db[0])
            ts(u("BOW", 0, 16), P(5, 32, 48), -33.0, AL.add)
            ops.append(db[1])
            cp(ind(BS, u("BOW", 0, 16)), b_("TSb", 0, 256))
            ts(u("BOW", 16, 32), P(4, 32, 48), -33.0, AL.add)
            ts(u("PLO"), P(2, 384, 416), -32.0, AL.add)
            ops.append(db[2])
            cp(ind(BS, u("BOW", 16, 32)), b_("TSb", 256, 512))
            act(f("TGf"), P(7, 0, 512))
            act(ind(PL, u("PLO")), f("TGf"), AF.Silu)

    def psum(x):
        return x[0][0] == "p" and x[0][1:].isdigit()

    def cols(x, y):
        if x[3] == y[3] and x[3] > 1 and (x[1] - y[1]) % x[3]:
            return False
        return x[1] < y[2] and y[1] < x[2]

    def meet(x, y):
        if psum(x):
            return True
        if x[5] == y[5] and x[5] > 1 and x[4] != y[4]:
            return False
        return cols(x, y)

    def covers(x, y):
        return x[3] == 1 and x[5] == 1 and x[1] <= y[1] and y[2] <= x[2]

    live = {}
    deps = []
    for n, o in enumerate(ops):
        dp = set()
        for x, w in [(x, False) for x in o["rd"]] + [(x, True) for x in o["wr"]]:
            for y, m, wy in live.get(x[0], []):
                if m == n or not meet(x, y):
                    continue
                q = ops[m]
                if q["e"] == o["e"] and not q["dma"]:
                    if o["e"] != "p" and cols(x, y) and (wy or w):
                        dp.add(m)
                elif (wy or w or psum(x)) and o["e"] != "x":
                    dp.add(m)
        deps.append(dp)
        for x in o["wr"]:
            if not o["scat"]:
                live[x[0]] = [z for z in live.get(x[0], []) if not (covers(x, z[0]) and z[1] in dp)]
            live.setdefault(x[0], []).append((x, n, True))
        if not o.get("remote"):
            for x in o["rd"]:
                lst = live.setdefault(x[0], [])
                if not o["dma"]:
                    lst[:] = [z for z in lst if not (z[0] == x and not z[2] and ops[z[1]]["e"] == o["e"])]
                lst.append((x, n, False))
    seen = {e: {} for e in "vspgy"}
    need = set()
    for n, o in enumerate(ops):
        if o["e"] == "x":
            continue
        best, s, kept = {}, seen[o["e"]], set()
        for m in deps[n]:
            q = ops[m]
            key = m if (q["dma"] or q["ext"]) else q["e"]
            best[key] = max(best.get(key, -1), m)
        for key, m in best.items():
            if s.get(key, -1) < m:
                s[key] = m
                kept.add(m)
        deps[n] = kept
        need |= kept
    queue = {"v": g.vector, "s": g.scalar, "p": g.tensor, "g": g, "y": g.sync}
    cnt = {e: 0 for e in "vspg"}
    tok = {}
    nd = 0
    for n, o in enumerate(ops):
        if o["ext"]:
            tok[n] = o["ext"]
            continue
        for m in sorted(deps[n]):
            queue[o["e"]].wait_ge(T.sem[tok[m][0]], tok[m][1])
        ins = o["fn"]()
        if o["dma"]:
            tok[n] = ("dm%d" % nd, 16); nd += 1
            ins.then_inc(T.sem[tok[n][0]], 16)
        elif n in need:
            cnt[o["e"]] += 1
            tok[n] = ("q" + o["e"], cnt[o["e"]])
            ins.then_inc(T.sem["q" + o["e"]], 1)
    for n, o in enumerate(ops):
        if o["dma"] and n not in need:
            g.sync.wait_ge(T.sem[tok[n][0]], 16)
    g.wait_ge(T.sem.sent, RO * ne)
